import numpy as np
import ml_dtypes


def mxq(x, axis, fmt="e4m3"):
    dtype, down = {"e4m3": (ml_dtypes.float8_e4m3fn, 7), "e5m2": (ml_dtypes.float8_e5m2, 14)}[fmt]
    v = np.moveaxis(np.asarray(x, np.float32).astype(ml_dtypes.bfloat16).astype(np.float64), axis, -1)
    blocks = v.reshape(v.shape[:-1] + (-1, 32))
    amax = np.abs(blocks).max(-1, keepdims=True)
    byte = np.maximum(np.where(amax > 0, np.frexp(amax)[1] - 1 + 127, 0) - down, 1)
    scale = np.exp2(byte - 127.0)
    codes = (blocks / scale).astype(np.float32).astype(dtype).astype(np.float64)
    return np.moveaxis((codes * scale).reshape(v.shape), -1, axis)


WIDE = False


def mx_kscale(k):
    if not WIDE:
        return np.ones(k)
    levels = np.array([10, -10, 5, -5, 0])
    if k % 512:
        return np.exp2(np.random.permutation(np.resize(levels, k // 32))).repeat(32)
    a = np.empty((k // 512, 16))
    for p in range(k // 512):
        a[p, :8] = np.random.permutation(np.resize(levels, 8))
        for g in range(8):
            far = levels[np.abs(levels - a[p, g]) >= 10]
            a[p, g + 8] = far[np.random.randint(len(far))]
    return np.exp2(a.ravel()).repeat(32)


def f64(x):
    return np.asarray(x).astype(np.float64)


def striped(idx):
    return np.tile(idx.reshape(-1, 16).T, (8, 1)).astype(np.uint16)


def unstriped(offs):
    return offs[:16].T.reshape(-1).astype(np.int64)


E2M1 = np.array([0.0, 0.5, 1.0, 1.5, 2.0, 3.0, 4.0, 6.0, -0.0, -0.5, -1.0, -1.5, -2.0, -3.0, -4.0, -6.0])


def pack_weight(w, fmt):
    k, n = w.shape
    w = f64(np.asarray(w, np.float32).astype(ml_dtypes.bfloat16)).reshape(k // 32, 32, n)
    amax = np.abs(w).max(1)
    if fmt == "e4m3":
        byte = np.frexp(amax)[1] - 1 + 127 - 7
    else:
        mant, ex = np.frexp(amax / 6.0)
        byte = np.where(mant > 0.5, ex, ex - 1) + 127
    byte = np.clip(np.where(amax > 0, byte, 1), 1, 254)
    scaled = (w * np.exp2(127.0 - byte)[:, None, :]).reshape(k, n).astype(np.float32)
    by_word = np.ascontiguousarray(scaled.reshape(k // 512, 128, 4, n).transpose(0, 1, 3, 2))
    if fmt == "e4m3":
        words = by_word.astype(ml_dtypes.float8_e4m3fn).view(np.uint8)
    else:
        c = by_word.astype(ml_dtypes.float4_e2m1fn).view(np.uint8) & 0xF
        words = (c[..., 0::2] | (c[..., 1::2] << 4)).reshape(k // 512, 128, 2 * n)
    return np.ascontiguousarray(words), np.ascontiguousarray(byte.astype(np.uint8).reshape(k // 512, 16, n))


def unpack_weight(words, scales, fmt):
    g, _, n = scales.shape
    words = np.ascontiguousarray(words).reshape(g, 128, n, -1)
    if fmt == "e4m3":
        vals = words.view(ml_dtypes.float8_e4m3fn).astype(np.float64)
    else:
        nib = np.empty((g, 128, n, 4), np.uint8)
        nib[..., 0::2] = words & 0xF
        nib[..., 1::2] = words >> 4
        vals = E2M1[nib]
    vals = vals * np.repeat(np.exp2(scales.astype(np.float64) - 127.0), 8, axis=1)[..., None]
    return vals.transpose(0, 1, 3, 2).reshape(g * 512, n)


K, T, E, C, N = 256, 512, 6, 256, 1536
TOP = 3


def by_expert(wq, xq):
    return np.concatenate([wq[e].T @ xq[:, e * C:(e + 1) * C] for e in range(E)], axis=1)


def setup_inputs():
    n = np.random.standard_normal
    s = mx_kscale(N)[:, None]
    deal = np.repeat(np.arange(E), C).reshape(TOP, T)[:, np.random.permutation(T)]
    deal = np.take_along_axis(deal, np.argsort(np.random.rand(TOP, T), axis=0), axis=0)
    for _ in range(8):
        s_, t_ = np.random.permutation(T).reshape(2, -1); r = np.random.randint(TOP, size=T // 2); x, y = deal[r, s_].copy(), deal[r, t_].copy()
        ok = ~((deal[:, s_] == y).any(0) | (deal[:, t_] == x).any(0)); deal[r[ok], s_[ok]] = y[ok]; deal[r[ok], t_[ok]] = x[ok]
    order = np.lexsort((np.random.rand(TOP * T), deal.reshape(-1)))
    slot_token = order % T; pos = np.empty(TOP * T, np.int64); pos[order] = np.arange(TOP * T); pos = pos.reshape(TOP, T)
    g = np.random.uniform(0.5, 1.5, (TOP, T)); g = g / g.sum(0)
    w_slot = np.empty(E * C)
    for r in range(TOP): w_slot[pos[r]] = g[r]
    w = [pack_weight(m, "e2m1") for m in n((E + 1, N, K)) / np.sqrt(N) / s[None]]
    return {
        "dyT": (n((N, T)) * s).astype(np.float32),
        "w_words": np.stack([m[0] for m in w]),
        "w_scales": np.stack([m[1] for m in w]),
        "gate": np.tile(w_slot, (N, 1)).astype(np.float32),
        "offs": striped(slot_token),
        "pos1": striped(pos[0]),
        "pos2": striped(pos[1]),
        "pos3": striped(pos[2]),
    }


def reference(dyT, w_words, w_scales, gate, offs, pos1, pos2, pos3):
    idx = unstriped(offs)
    w = np.stack([unpack_weight(w_words[e], w_scales[e], "e2m1") for e in range(E + 1)])
    gq = mxq(f64(gate) * f64(dyT)[:, idx], 0, "e4m3")
    wq = w
    ds = wq[E].T @ mxq(f64(dyT), 0, "e4m3")
    dx = by_expert(wq, gq)
    return ds + dx[:, unstriped(pos1)] + dx[:, unstriped(pos2)] + dx[:, unstriped(pos3)]

@@ -1,0 +1,161 @@
+from contextlib import ExitStack
+
+import concourse.mybir as mybir
+
+K, T, E, C, N = 256, 512, 6, 256, 1536
+S = E * C
+P = 128
+PACK = 4
+PASSES = N // (P * PACK)
+MM = 128
+FLOPS = 2 * K * N * (S + T)
+BYTES = N * T * 4 + (E + 1) * PASSES * (P * 512 + 16 * K) + P * S * 4 + P * (S + 3 * T) // 16 * 2 + K * T * 4
+
+F32 = mybir.dt.float32
+BF16 = mybir.dt.bfloat16
+I32 = mybir.dt.int32
+U32 = mybir.dt.uint32
+U16 = mybir.dt.uint16
+U8 = mybir.dt.uint8
+FP8X4 = mybir.dt.float8_e4m3fn_x4
+FP4X4 = mybir.dt.float4_e2m1fn_x4
+MULT = mybir.AluOpType.mult
+ADD = mybir.AluOpType.add
+
+HEAD_CUTS = (256, 512, 768)
+LAST_CUTS = (512, 384, 256, 256, 128)
+ROW_ORDER = (1, 2, 3, 0)
+
+
+def spans(widths, first=0):
+    res = []
+    for w in widths:
+        res.append((first, first + w))
+        first += w
+    return res
+
+
+def pow2_widths(n):
+    return [w for w in (512, 256, 128) if n & w]
+
+
+def tile_moe_bds_lin_none_kernel(tc, dyT, w_words, w_scales, gate, offs, pos1, pos2, pos3, out):
+    nc = tc.nc
+    with ExitStack() as ctx:
+        lists = ctx.enter_context(tc.tile_pool(name="lists", bufs=1))
+        keep = ctx.enter_context(tc.tile_pool(name="keep", bufs=1))
+        gath = ctx.enter_context(tc.tile_pool(name="gath", bufs=2))
+        stage = ctx.enter_context(tc.tile_pool(name="stage", bufs=4))
+        psum = ctx.enter_context(tc.psum_pool(name="psum", bufs=6))
+        psum_s = ctx.enter_context(tc.psum_pool(name="psum_s", bufs=1))
+
+        slot_token = lists.tile([P, S // 16], U16, name="slot_token")
+        token_slot = [lists.tile([P, T // 16], U16, name="token_slot%d" % r) for r in range(3)]
+
+        dy_rows = dyT.rearrange("(a p j) t -> a p j t", p=P, j=PACK)
+        w_codes = keep.tile([P, (E + 1) * PASSES, 2 * K], U8, name="w_codes", align_bytes=64)
+        w_exp = keep.tile([P, (E + 1) * PASSES, K], U8, name="w_exp", align_bytes=64)
+        nc.gpsimd.memset(w_exp[:].rearrange("p g k -> p (g k)").bitcast(I32), 0)
+
+        gates = keep.tile([P, S], F32, name="gates")
+        dy_all = [keep.tile([P, PACK * T], F32, name="dy_all%d" % a) for a in range(PASSES)]
+        window = {}
+        for a in range(PASSES):
+            width = (S if a < PASSES - 1 else max(LAST_CUTS)) + 16
+            window[a, 0] = dy_all[a]
+            for j in range(1, PACK):
+                window[a, j] = keep.tile([P, width], F32, name="window%d_%d" % (a, j))
+
+        nc.sync.dma_start(slot_token[:], offs)
+        for a in range(PASSES):
+            for j in range(1, PACK):
+                nc.sync.dma_start(out=window[a, j][:, 0:T], in_=dy_rows[a, :, j, :])
+                if (a, j) == (0, 1):
+                    for c0, c1 in spans(HEAD_CUTS):
+                        nc.sync.dma_start(out=gates[:, c0:c1], in_=gate[0:P, c0:c1])
+            nc.sync.dma_start(out=dy_all[a][:], in_=dy_rows[a].rearrange("p j t -> p (j t)"))
+        w_src = w_words.rearrange("e a p b -> p (e a) b")
+        for e in range(E + 1):
+            g = slice(e * PASSES, (e + 1) * PASSES)
+            nc.sync.dma_start(out=w_codes[:, g, :].bitcast(I32), in_=w_src[:, g, :].bitcast(I32))
+        s_src = w_scales.rearrange("e a f k -> f (e a) k")
+        for q in range(4):
+            nc.sync.dma_start(out=w_exp[32 * q : 32 * q + 4, :, :].bitcast(I32), in_=s_src[4 * q : 4 * q + 4].bitcast(I32))
+        for r, src in enumerate((pos1, pos2, pos3)):
+            nc.sync.dma_start(token_slot[r][:], src)
+
+        g_codes = [keep.tile([P, S], U32, name="g_codes%d" % a, align_bytes=64) for a in range(PASSES)]
+        g_exp = [keep.tile([P, S], U8, name="g_exp%d" % a, align_bytes=64) for a in range(PASSES)]
+        d_codes = [keep.tile([P, T], U32, name="d_codes%d" % a, align_bytes=64) for a in range(PASSES)]
+        d_exp = [keep.tile([P, T], U8, name="d_exp%d" % a, align_bytes=64) for a in range(PASSES)]
+        d_bf = [keep.tile([P, T * PACK], BF16, name="d_bf%d" % a, align_bytes=64) for a in range(PASSES)]
+        dx = [keep.tile([P, S], F32, name="dx%d" % h) for h in range(K // P)]
+
+        def gather(a, j, dst, c0, c1):
+            nc.vector.tensor_tensor(dst, window[a, j][:].indirect(slot_token[:, c0 // 16 : c1 // 16]), gates[:, c0:c1], MULT)
+
+        def interleave(dst, src):
+            nc.scalar.copy(out=dst.rearrange("p (c j) -> p c j", j=PACK), in_=src.rearrange("p j c -> p c j"))
+
+        def round_and_quantize(a, src, c0, c1):
+            g_bf = stage.tile([P, PACK * T], BF16, name="g_bf", align_bytes=64)
+            view = g_bf[:, 0 : PACK * (c1 - c0)]
+            interleave(view, src)
+            nc.vector.quantize_mx(out=g_codes[a][:, c0:c1].bitcast(FP8X4), scales=g_exp[a][:, c0:c1], in_=view)
+
+        def product(acc, e, h, codes, exps, c0, c1):
+            for a in range(PASSES):
+                g = e * PASSES + a
+                nc.tensor.matmul_mx(
+                    out=acc,
+                    lhsT=w_codes[:, g, 2 * P * h : 2 * P * (h + 1)].bitcast(FP4X4),
+                    lhsT_scale=w_exp[:, g, P * h : P * (h + 1)],
+                    rhs=codes[a][:, c0:c1].bitcast(FP8X4),
+                    rhs_scale=exps[a][:, c0:c1],
+                    start=(a == 0),
+                    stop=(a == PASSES - 1),
+                )
+
+        for a in range(PASSES - 1):
+            g_f32 = gath.tile([P, PACK * S], F32, name="g_f32")
+            planes = g_f32[:].rearrange("p (j c) -> p j c", j=PACK)
+            for j in ROW_ORDER:
+                cuts = HEAD_CUTS if (a, j) == (0, ROW_ORDER[0]) else (S,)
+                for c0, c1 in spans(cuts):
+                    gather(a, j, planes[:, j, c0:c1], c0, c1)
+            interleave(d_bf[a][:], dy_all[a][:].rearrange("p (j t) -> p j t", j=PACK))
+            for c0, c1 in spans((T,) * (S // T)):
+                round_and_quantize(a, planes[:, :, c0:c1], c0, c1)
+
+        a = PASSES - 1
+        interleave(d_bf[a][:], dy_all[a][:].rearrange("p (j t) -> p j t", j=PACK))
+        g_f32 = gath.tile([P, PACK * S], F32, name="g_f32")
+        for c0, c1 in spans(LAST_CUTS):
+            planes = g_f32[:, PACK * c0 : PACK * c1].rearrange("p (j c) -> p j c", j=PACK)
+            for j in ROW_ORDER:
+                gather(a, j, planes[:, j, :], c0, c1)
+            for q0, q1 in spans(pow2_widths(c1 - c0), c0):
+                round_and_quantize(a, planes[:, :, q0 - c0 : q1 - c0], q0, q1)
+            for m0 in range(c0, c1, MM):
+                for h in range(K // P):
+                    if m0 + MM < S:
+                        acc = psum.tile([P, MM], F32, name="acc")
+                    else:
+                        acc = psum_s.tile([P, T], F32, name="end%d" % h)
+                    product(acc[:, 0:MM], m0 // C, h, g_codes, g_exp, m0, m0 + MM)
+                    nc.scalar.copy(out=dx[h][:, m0 : m0 + MM], in_=acc[:, 0:MM])
+
+        for a in range(PASSES):
+            nc.vector.quantize_mx(out=d_codes[a][:].bitcast(FP8X4), scales=d_exp[a][:], in_=d_bf[a][:])
+        for h in range(K // P):
+            ds = psum_s.tile([P, T], F32, name="end%d" % h)
+            product(ds[:], E, h, d_codes, d_exp, 0, T)
+            picked = [keep.tile([P, T], F32, name="picked%d_%d" % (h, r)) for r in range(3)]
+            for r in range(3):
+                nc.vector.tensor_copy(picked[r][:], dx[h][:].indirect(token_slot[r][:]))
+            left = keep.tile([P, T], F32, name="left%d" % h)
+            nc.vector.tensor_tensor(left[:], picked[0][:], ds[:], ADD)
+            nc.vector.tensor_tensor(picked[1][:], picked[1][:], left[:], ADD)
+            for t0, t1 in spans((T,) if h == 0 else (T // 2, T // 2)):
+                nc.vector.tensor_tensor(left[:, t0:t1], picked[2][:, t0:t1], picked[1][:, t0:t1], ADD)
+                nc.sync.dma_start(out=out[P * h : P * (h + 1), t0:t1], in_=left[:, t0:t1])

@@ -22,8 +22,10 @@ FP4X4 = mybir.dt.float4_e2m1fn_x4
 MULT = mybir.AluOpType.mult
 ADD = mybir.AluOpType.add
 
-HEAD_CUTS = (256, 512, 768)
-LAST_CUTS = (512, 384, 256, 256, 128)
+FIRST = 1024
+HEAD_CUTS = (256, 768)
+GATE_CUTS = HEAD_CUTS + (S - FIRST,)
+LAST_CUTS = (256, 128, 128)
 ROW_ORDER = (1, 2, 3, 0)
 
 
@@ -33,10 +35,6 @@ def spans(widths, first=0):
         res.append((first, first + w))
         first += w
     return res
-
-
-def pow2_widths(n):
-    return [w for w in (512, 256, 128) if n & w]
 
 
 def tile_moe_bds_lin_none_kernel(tc, dyT, w_words, w_scales, gate, offs, pos1, pos2, pos3, out):
@@ -61,17 +59,16 @@ def tile_moe_bds_lin_none_kernel(tc, dyT, w_words, w_scales, gate, offs, pos1, p
         dy_all = [keep.tile([P, PACK * T], F32, name="dy_all%d" % a) for a in range(PASSES)]
         window = {}
         for a in range(PASSES):
-            width = (S if a < PASSES - 1 else max(LAST_CUTS)) + 16
             window[a, 0] = dy_all[a]
             for j in range(1, PACK):
-                window[a, j] = keep.tile([P, width], F32, name="window%d_%d" % (a, j))
+                window[a, j] = keep.tile([P, FIRST + 16], F32, name="window%d_%d" % (a, j))
 
         nc.sync.dma_start(slot_token[:], offs)
         for a in range(PASSES):
             for j in range(1, PACK):
                 nc.sync.dma_start(out=window[a, j][:, 0:T], in_=dy_rows[a, :, j, :])
                 if (a, j) == (0, 1):
-                    for c0, c1 in spans(HEAD_CUTS):
+                    for c0, c1 in spans(GATE_CUTS):
                         nc.sync.dma_start(out=gates[:, c0:c1], in_=gate[0:P, c0:c1])
             nc.sync.dma_start(out=dy_all[a][:], in_=dy_rows[a].rearrange("p j t -> p (j t)"))
         w_src = w_words.rearrange("e a p b -> p (e a) b")
@@ -86,22 +83,18 @@ def tile_moe_bds_lin_none_kernel(tc, dyT, w_words, w_scales, gate, offs, pos1, p
 
         g_codes = [keep.tile([P, S], U32, name="g_codes%d" % a, align_bytes=64) for a in range(PASSES)]
         g_exp = [keep.tile([P, S], U8, name="g_exp%d" % a, align_bytes=64) for a in range(PASSES)]
-        d_codes = [keep.tile([P, T], U32, name="d_codes%d" % a, align_bytes=64) for a in range(PASSES)]
-        d_exp = [keep.tile([P, T], U8, name="d_exp%d" % a, align_bytes=64) for a in range(PASSES)]
-        d_bf = [keep.tile([P, T * PACK], BF16, name="d_bf%d" % a, align_bytes=64) for a in range(PASSES)]
+        d_exp = keep.tile([P, PASSES * T], U8, name="d_exp", align_bytes=64)
+        d_bf = keep.tile([P, PASSES * T * PACK], BF16, name="d_bf", align_bytes=64)
         dx = [keep.tile([P, S], F32, name="dx%d" % h) for h in range(K // P)]
 
         def gather(a, j, dst, c0, c1):
             nc.vector.tensor_tensor(dst, window[a, j][:].indirect(slot_token[:, c0 // 16 : c1 // 16]), gates[:, c0:c1], MULT)
 
         def interleave(dst, src):
-            nc.scalar.copy(out=dst.rearrange("p (c j) -> p c j", j=PACK), in_=src.rearrange("p j c -> p c j"))
-
-        def round_and_quantize(a, src, c0, c1):
-            g_bf = stage.tile([P, PACK * T], BF16, name="g_bf", align_bytes=64)
-            view = g_bf[:, 0 : PACK * (c1 - c0)]
-            interleave(view, src)
-            nc.vector.quantize_mx(out=g_codes[a][:, c0:c1].bitcast(FP8X4), scales=g_exp[a][:, c0:c1], in_=view)
+            nc.scalar.copy(
+                out=dst.rearrange("p (c i j) -> p c j i", i=4, j=PACK),
+                in_=src.rearrange("p j (c i) -> p c j i", i=4),
+            )
 
         def product(acc, e, h, codes, exps, c0, c1):
             for a in range(PASSES):
@@ -116,46 +109,53 @@ def tile_moe_bds_lin_none_kernel(tc, dyT, w_words, w_scales, gate, offs, pos1, p
                     stop=(a == PASSES - 1),
                 )
 
-        for a in range(PASSES - 1):
-            g_f32 = gath.tile([P, PACK * S], F32, name="g_f32")
+        units = [(a, 0, FIRST) for a in range(PASSES)] + [(a, FIRST, S) for a in range(PASSES - 1)]
+        units += [(PASSES - 1, c0, c1) for c0, c1 in spans(LAST_CUTS, FIRST)]
+        for u, (a, c0, c1) in enumerate(units):
+            g_f32 = gath.tile([P, PACK * (c1 - c0)], F32, name="g_f32")
             planes = g_f32[:].rearrange("p (j c) -> p j c", j=PACK)
             for j in ROW_ORDER:
-                cuts = HEAD_CUTS if (a, j) == (0, ROW_ORDER[0]) else (S,)
-                for c0, c1 in spans(cuts):
-                    gather(a, j, planes[:, j, c0:c1], c0, c1)
-            interleave(d_bf[a][:], dy_all[a][:].rearrange("p (j t) -> p j t", j=PACK))
-            for c0, c1 in spans((T,) * (S // T)):
-                round_and_quantize(a, planes[:, :, c0:c1], c0, c1)
+                cuts = HEAD_CUTS if (u, j) == (0, ROW_ORDER[0]) else (c1 - c0,)
+                for s0, s1 in spans(cuts, c0):
+                    gather(a, j, planes[:, j, s0 - c0 : s1 - c0], s0, s1)
+            if c0 == 0:
+                interleave(d_bf[:, a * T * PACK : (a + 1) * T * PACK], dy_all[a][:].rearrange("p (j t) -> p j t", j=PACK))
+            for q0 in range(c0, c1, T):
+                q1 = min(q0 + T, c1)
+                if u < len(units) - 2:
+                    g_bf = stage.tile([P, PACK * (q1 - q0)], BF16, name="g_bf", align_bytes=64)
+                else:
+                    g_bf = keep.tile([P, PACK * (q1 - q0)], BF16, name="late%d" % (len(units) - u), align_bytes=64)
+                interleave(g_bf[:], planes[:, :, q0 - c0 : q1 - c0])
+                nc.vector.quantize_mx(out=g_codes[a][:, q0:q1].bitcast(FP8X4), scales=g_exp[a][:, q0:q1], in_=g_bf[:])
+            if a == PASSES - 1:
+                width = T if c0 == 0 else MM
+                for b0 in range(c0, c1, width):
+                    for h in range(K // P):
+                        if b0 + width < S:
+                            acc = psum.tile([P, width], F32, name="acc")
+                        else:
+                            acc = psum_s.tile([P, width], F32, name="end%d" % h)
+                        for m0 in range(b0, b0 + width, MM):
+                            product(acc[:, m0 - b0 : m0 - b0 + MM], m0 // C, h, g_codes, g_exp, m0, m0 + MM)
+                        nc.scalar.copy(out=dx[h][:, b0 : b0 + width], in_=acc[:])
 
-        a = PASSES - 1
-        interleave(d_bf[a][:], dy_all[a][:].rearrange("p (j t) -> p j t", j=PACK))
-        g_f32 = gath.tile([P, PACK * S], F32, name="g_f32")
-        for c0, c1 in spans(LAST_CUTS):
-            planes = g_f32[:, PACK * c0 : PACK * c1].rearrange("p (j c) -> p j c", j=PACK)
-            for j in ROW_ORDER:
-                gather(a, j, planes[:, j, :], c0, c1)
-            for q0, q1 in spans(pow2_widths(c1 - c0), c0):
-                round_and_quantize(a, planes[:, :, q0 - c0 : q1 - c0], q0, q1)
-            for m0 in range(c0, c1, MM):
-                for h in range(K // P):
-                    if m0 + MM < S:
-                        acc = psum.tile([P, MM], F32, name="acc")
-                    else:
-                        acc = psum_s.tile([P, T], F32, name="end%d" % h)
-                    product(acc[:, 0:MM], m0 // C, h, g_codes, g_exp, m0, m0 + MM)
-                    nc.scalar.copy(out=dx[h][:, m0 : m0 + MM], in_=acc[:, 0:MM])
-
-        for a in range(PASSES):
-            nc.vector.quantize_mx(out=d_codes[a][:].bitcast(FP8X4), scales=d_exp[a][:], in_=d_bf[a][:])
+        d_first = keep.tile([P, T], U32, name="late2", align_bytes=64)
+        d_rest = keep.tile([P, 2 * T], U32, name="late1", align_bytes=64)
+        nc.vector.quantize_mx(out=d_first[:].bitcast(FP8X4), scales=d_exp[:, 0:T], in_=d_bf[:, 0 : T * PACK])
+        nc.vector.quantize_mx(out=d_rest[:].bitcast(FP8X4), scales=d_exp[:, T:], in_=d_bf[:, T * PACK :])
+        d_codes = [d_first[:], d_rest[:, 0:T], d_rest[:, T:]]
+        d_exps = [d_exp[:, a * T : (a + 1) * T] for a in range(PASSES)]
         for h in range(K // P):
             ds = psum_s.tile([P, T], F32, name="end%d" % h)
-            product(ds[:], E, h, d_codes, d_exp, 0, T)
+            product(ds[:], E, h, d_codes, d_exps, 0, T)
             picked = [keep.tile([P, T], F32, name="picked%d_%d" % (h, r)) for r in range(3)]
             for r in range(3):
                 nc.vector.tensor_copy(picked[r][:], dx[h][:].indirect(token_slot[r][:]))
-            left = keep.tile([P, T], F32, name="left%d" % h)
-            nc.vector.tensor_tensor(left[:], picked[0][:], ds[:], ADD)
-            nc.vector.tensor_tensor(picked[1][:], picked[1][:], left[:], ADD)
-            for t0, t1 in spans((T,) if h == 0 else (T // 2, T // 2)):
-                nc.vector.tensor_tensor(left[:, t0:t1], picked[2][:, t0:t1], picked[1][:, t0:t1], ADD)
-                nc.sync.dma_start(out=out[P * h : P * (h + 1), t0:t1], in_=left[:, t0:t1])
+            halves = spans((T,) if h == 0 else (T // 2, T // 2))
+            nc.vector.tensor_tensor(picked[0][:], picked[0][:], ds[:], ADD)
+            for t0, t1 in halves:
+                nc.vector.tensor_tensor(picked[1][:, t0:t1], picked[1][:, t0:t1], picked[2][:, t0:t1], ADD)
+            for t0, t1 in halves:
+                nc.vector.tensor_tensor(picked[2][:, t0:t1], picked[0][:, t0:t1], picked[1][:, t0:t1], ADD)
+                nc.sync.dma_start(out=out[P * h : P * (h + 1), t0:t1], in_=picked[2][:, t0:t1])

@@ -109,6 +109,15 @@ def tile_moe_bds_lin_none_kernel(tc, dyT, w_words, w_scales, gate, offs, pos1, p
                     stop=(a == PASSES - 1),
                 )
 
+        def slot_sums(h, b0, width):
+            if b0 + width < S:
+                acc = psum.tile([P, width], F32, name="acc")
+            else:
+                acc = psum_s.tile([P, width], F32, name="end%d" % h)
+            for m0 in range(b0, b0 + width, MM):
+                product(acc[:, m0 - b0 : m0 - b0 + MM], m0 // C, h, g_codes, g_exp, m0, m0 + MM)
+            nc.scalar.copy(out=dx[h][:, b0 : b0 + width], in_=acc[:])
+
         units = [(a, 0, FIRST) for a in range(PASSES)] + [(a, FIRST, S) for a in range(PASSES - 1)]
         units += [(PASSES - 1, c0, c1) for c0, c1 in spans(LAST_CUTS, FIRST)]
         for u, (a, c0, c1) in enumerate(units):
@@ -131,14 +140,10 @@ def tile_moe_bds_lin_none_kernel(tc, dyT, w_words, w_scales, gate, offs, pos1, p
             if a == PASSES - 1:
                 width = T if c0 == 0 else MM
                 for b0 in range(c0, c1, width):
-                    for h in range(K // P):
-                        if b0 + width < S:
-                            acc = psum.tile([P, width], F32, name="acc")
-                        else:
-                            acc = psum_s.tile([P, width], F32, name="end%d" % h)
-                        for m0 in range(b0, b0 + width, MM):
-                            product(acc[:, m0 - b0 : m0 - b0 + MM], m0 // C, h, g_codes, g_exp, m0, m0 + MM)
-                        nc.scalar.copy(out=dx[h][:, b0 : b0 + width], in_=acc[:])
+                    for h in range(K // P if u < len(units) - 2 else 1):
+                        slot_sums(h, b0, width)
+        for b0 in range(S - 2 * MM, S, MM):
+            slot_sums(1, b0, MM)
 
         d_first = keep.tile([P, T], U32, name="late2", align_bytes=64)
         d_rest = keep.tile([P, 2 * T], U32, name="late1", align_bytes=64)
@@ -152,7 +157,15 @@ def tile_moe_bds_lin_none_kernel(tc, dyT, w_words, w_scales, gate, offs, pos1, p
             picked = [keep.tile([P, T], F32, name="picked%d_%d" % (h, r)) for r in range(3)]
             for r in range(3):
                 nc.vector.tensor_copy(picked[r][:], dx[h][:].indirect(token_slot[r][:]))
-            halves = spans((T,) if h == 0 else (T // 2, T // 2))
+            if h == 0:
+                ds_sb = keep.tile([P, T], F32, name="ds_sb")
+                nc.scalar.copy(out=ds_sb[:], in_=ds[:])
+                nc.gpsimd.tensor_tensor(picked[0][:], picked[0][:], picked[1][:], ADD)
+                nc.gpsimd.tensor_tensor(ds_sb[:], ds_sb[:], picked[0][:], ADD)
+                nc.gpsimd.tensor_tensor(picked[2][:], picked[2][:], ds_sb[:], ADD)
+                nc.sync.dma_start(out=out[0:P, :], in_=picked[2][:])
+                continue
+            halves = spans((T // 2, T // 2))
             nc.vector.tensor_tensor(picked[0][:], picked[0][:], ds[:], ADD)
             for t0, t1 in halves:
                 nc.vector.tensor_tensor(picked[1][:, t0:t1], picked[1][:, t0:t1], picked[2][:, t0:t1], ADD)

@@ -23,7 +23,7 @@ MULT = mybir.AluOpType.mult
 ADD = mybir.AluOpType.add
 
 FIRST = 1024
-HEAD_CUTS = (256, 768)
+HEAD_CUTS = (128, 256, 640)
 GATE_CUTS = HEAD_CUTS + (S - FIRST,)
 LAST_CUTS = (256, 128, 128)
 ROW_ORDER = (1, 2, 3, 0)
@@ -43,7 +43,7 @@ def tile_moe_bds_lin_none_kernel(tc, dyT, w_words, w_scales, gate, offs, pos1, p
         lists = ctx.enter_context(tc.tile_pool(name="lists", bufs=1))
         keep = ctx.enter_context(tc.tile_pool(name="keep", bufs=1))
         gath = ctx.enter_context(tc.tile_pool(name="gath", bufs=2))
-        stage = ctx.enter_context(tc.tile_pool(name="stage", bufs=4))
+        stage = ctx.enter_context(tc.tile_pool(name="stage", bufs=3))
         psum = ctx.enter_context(tc.psum_pool(name="psum", bufs=6))
         psum_s = ctx.enter_context(tc.psum_pool(name="psum_s", bufs=1))
 
@@ -96,8 +96,8 @@ def tile_moe_bds_lin_none_kernel(tc, dyT, w_words, w_scales, gate, offs, pos1, p
                 in_=src.rearrange("p j (c i) -> p c j i", i=4),
             )
 
-        def product(acc, e, h, codes, exps, c0, c1):
-            for a in range(PASSES):
+        def product(acc, e, h, codes, exps, c0, c1, order=(0, 1, 2)):
+            for a in order:
                 g = e * PASSES + a
                 nc.tensor.matmul_mx(
                     out=acc,
@@ -105,15 +105,12 @@ def tile_moe_bds_lin_none_kernel(tc, dyT, w_words, w_scales, gate, offs, pos1, p
                     lhsT_scale=w_exp[:, g, P * h : P * (h + 1)],
                     rhs=codes[a][:, c0:c1].bitcast(FP8X4),
                     rhs_scale=exps[a][:, c0:c1],
-                    start=(a == 0),
-                    stop=(a == PASSES - 1),
+                    start=(a == order[0]),
+                    stop=(a == order[-1]),
                 )
 
         def slot_sums(h, b0, width):
-            if b0 + width < S:
-                acc = psum.tile([P, width], F32, name="acc")
-            else:
-                acc = psum_s.tile([P, width], F32, name="end%d" % h)
+            acc = psum.tile([P, width], F32, name="acc")
             for m0 in range(b0, b0 + width, MM):
                 product(acc[:, m0 - b0 : m0 - b0 + MM], m0 // C, h, g_codes, g_exp, m0, m0 + MM)
             nc.scalar.copy(out=dx[h][:, b0 : b0 + width], in_=acc[:])
@@ -121,7 +118,7 @@ def tile_moe_bds_lin_none_kernel(tc, dyT, w_words, w_scales, gate, offs, pos1, p
         units = [(a, 0, FIRST) for a in range(PASSES)] + [(a, FIRST, S) for a in range(PASSES - 1)]
         units += [(PASSES - 1, c0, c1) for c0, c1 in spans(LAST_CUTS, FIRST)]
         for u, (a, c0, c1) in enumerate(units):
-            g_f32 = gath.tile([P, PACK * (c1 - c0)], F32, name="g_f32")
+            g_f32 = gath.tile([P, PACK * (c1 - c0)], F32, name="g_f32", align_bytes=64)
             planes = g_f32[:].rearrange("p (j c) -> p j c", j=PACK)
             for j in ROW_ORDER:
                 cuts = HEAD_CUTS if (u, j) == (0, ROW_ORDER[0]) else (c1 - c0,)
@@ -129,46 +126,45 @@ def tile_moe_bds_lin_none_kernel(tc, dyT, w_words, w_scales, gate, offs, pos1, p
                     gather(a, j, planes[:, j, s0 - c0 : s1 - c0], s0, s1)
             if c0 == 0:
                 interleave(d_bf[:, a * T * PACK : (a + 1) * T * PACK], dy_all[a][:].rearrange("p (j t) -> p j t", j=PACK))
-            for q0 in range(c0, c1, T):
-                q1 = min(q0 + T, c1)
-                if u < len(units) - 2:
-                    g_bf = stage.tile([P, PACK * (q1 - q0)], BF16, name="g_bf", align_bytes=64)
-                else:
-                    g_bf = keep.tile([P, PACK * (q1 - q0)], BF16, name="late%d" % (len(units) - u), align_bytes=64)
+            step = c1 - c0 if a < PASSES - 1 else T
+            for q0 in range(c0, c1, step):
+                q1 = min(q0 + step, c1)
+                g_bf = stage.tile([P, PACK * (q1 - q0)], BF16, name="g_bf", align_bytes=64)
                 interleave(g_bf[:], planes[:, :, q0 - c0 : q1 - c0])
                 nc.vector.quantize_mx(out=g_codes[a][:, q0:q1].bitcast(FP8X4), scales=g_exp[a][:, q0:q1], in_=g_bf[:])
             if a == PASSES - 1:
-                width = T if c0 == 0 else MM
+                width = min(T, c1 - c0)
                 for b0 in range(c0, c1, width):
                     for h in range(K // P if u < len(units) - 2 else 1):
                         slot_sums(h, b0, width)
         for b0 in range(S - 2 * MM, S, MM):
             slot_sums(1, b0, MM)
 
-        d_first = keep.tile([P, T], U32, name="late2", align_bytes=64)
-        d_rest = keep.tile([P, 2 * T], U32, name="late1", align_bytes=64)
+        d_first = gath.tile([P, T], U32, name="g_f32", align_bytes=64)
+        d_rest = gath.tile([P, 2 * T], U32, name="g_f32", align_bytes=64)
         nc.vector.quantize_mx(out=d_first[:].bitcast(FP8X4), scales=d_exp[:, 0:T], in_=d_bf[:, 0 : T * PACK])
         nc.vector.quantize_mx(out=d_rest[:].bitcast(FP8X4), scales=d_exp[:, T:], in_=d_bf[:, T * PACK :])
         d_codes = [d_first[:], d_rest[:, 0:T], d_rest[:, T:]]
         d_exps = [d_exp[:, a * T : (a + 1) * T] for a in range(PASSES)]
         for h in range(K // P):
-            ds = psum_s.tile([P, T], F32, name="end%d" % h)
-            product(ds[:], E, h, d_codes, d_exps, 0, T)
+            ds = psum_s.tile([P, T], F32, name="ds%d" % h)
+            product(ds[:], E, h, d_codes, d_exps, 0, T, (1, 2, 0))
             picked = [keep.tile([P, T], F32, name="picked%d_%d" % (h, r)) for r in range(3)]
             for r in range(3):
-                nc.vector.tensor_copy(picked[r][:], dx[h][:].indirect(token_slot[r][:]))
+                for t0, t1 in spans((T // 2, T // 2) if (h, r) == (1, 2) else (T,)):
+                    nc.vector.tensor_copy(picked[r][:, t0:t1], dx[h][:].indirect(token_slot[r][:, t0 // 16 : t1 // 16]))
             if h == 0:
                 ds_sb = keep.tile([P, T], F32, name="ds_sb")
                 nc.scalar.copy(out=ds_sb[:], in_=ds[:])
-                nc.gpsimd.tensor_tensor(picked[0][:], picked[0][:], picked[1][:], ADD)
                 nc.gpsimd.tensor_tensor(ds_sb[:], ds_sb[:], picked[0][:], ADD)
+                nc.gpsimd.tensor_tensor(ds_sb[:], ds_sb[:], picked[1][:], ADD)
                 nc.gpsimd.tensor_tensor(picked[2][:], picked[2][:], ds_sb[:], ADD)
                 nc.sync.dma_start(out=out[0:P, :], in_=picked[2][:])
                 continue
             halves = spans((T // 2, T // 2))
-            nc.vector.tensor_tensor(picked[0][:], picked[0][:], ds[:], ADD)
+            nc.gpsimd.tensor_tensor(ds_sb[:], picked[0][:], picked[1][:], ADD)
             for t0, t1 in halves:
-                nc.vector.tensor_tensor(picked[1][:, t0:t1], picked[1][:, t0:t1], picked[2][:, t0:t1], ADD)
+                nc.vector.tensor_tensor(picked[2][:, t0:t1], picked[2][:, t0:t1], ds[:, t0:t1], ADD)
             for t0, t1 in halves:
-                nc.vector.tensor_tensor(picked[2][:, t0:t1], picked[0][:, t0:t1], picked[1][:, t0:t1], ADD)
+                nc.vector.tensor_tensor(picked[2][:, t0:t1], ds_sb[:, t0:t1], picked[2][:, t0:t1], ADD)
                 nc.sync.dma_start(out=out[P * h : P * (h + 1), t0:t1], in_=picked[2][:, t0:t1])

@@ -24,7 +24,6 @@ ADD = mybir.AluOpType.add
 
 FIRST = 1024
 HEAD_CUTS = (128, 256, 640)
-GATE_CUTS = HEAD_CUTS + (S - FIRST,)
 LAST_CUTS = (256, 128, 128)
 ROW_ORDER = (1, 2, 3, 0)
 
@@ -68,9 +67,10 @@ def tile_moe_bds_lin_none_kernel(tc, dyT, w_words, w_scales, gate, offs, pos1, p
             for j in range(1, PACK):
                 nc.sync.dma_start(out=window[a, j][:, 0:T], in_=dy_rows[a, :, j, :])
                 if (a, j) == (0, 1):
-                    for c0, c1 in spans(GATE_CUTS):
+                    for c0, c1 in spans(HEAD_CUTS):
                         nc.sync.dma_start(out=gates[:, c0:c1], in_=gate[0:P, c0:c1])
             nc.sync.dma_start(out=dy_all[a][:], in_=dy_rows[a].rearrange("p j t -> p (j t)"))
+        nc.sync.dma_start(out=gates[:, FIRST:S], in_=gate[0:P, FIRST:S])
         w_src = w_words.rearrange("e a p b -> p (e a) b")
         for e in range(E + 1):
             g = slice(e * PASSES, (e + 1) * PASSES)

@@ -22,6 +22,7 @@ FP4X4 = mybir.dt.float4_e2m1fn_x4
 MULT = mybir.AluOpType.mult
 ADD = mybir.AluOpType.add
 
+HALF = T // 2
 FIRST = 1024
 HEAD_CUTS = (128, 256, 640)
 LAST_CUTS = (256, 128, 128)
@@ -43,8 +44,7 @@ def tile_moe_bds_lin_none_kernel(tc, dyT, w_words, w_scales, gate, offs, pos1, p
         keep = ctx.enter_context(tc.tile_pool(name="keep", bufs=1))
         gath = ctx.enter_context(tc.tile_pool(name="gath", bufs=2))
         stage = ctx.enter_context(tc.tile_pool(name="stage", bufs=3))
-        psum = ctx.enter_context(tc.psum_pool(name="psum", bufs=6))
-        psum_s = ctx.enter_context(tc.psum_pool(name="psum_s", bufs=1))
+        psum = ctx.enter_context(tc.psum_pool(name="psum", bufs=8))
 
         slot_token = lists.tile([P, S // 16], U16, name="slot_token")
         token_slot = [lists.tile([P, T // 16], U16, name="token_slot%d" % r) for r in range(3)]
@@ -83,8 +83,8 @@ def tile_moe_bds_lin_none_kernel(tc, dyT, w_words, w_scales, gate, offs, pos1, p
 
         g_codes = [keep.tile([P, S], U32, name="g_codes%d" % a, align_bytes=64) for a in range(PASSES)]
         g_exp = [keep.tile([P, S], U8, name="g_exp%d" % a, align_bytes=64) for a in range(PASSES)]
-        d_exp = keep.tile([P, PASSES * T], U8, name="d_exp", align_bytes=64)
-        d_bf = keep.tile([P, PASSES * T * PACK], BF16, name="d_bf", align_bytes=64)
+        d_exp = [keep.tile([P, PASSES * HALF], U8, name="d_exp%d" % b, align_bytes=64) for b in range(2)]
+        d_bf = [keep.tile([P, PASSES * HALF * PACK], BF16, name="d_bf%d" % b, align_bytes=64) for b in range(2)]
         dx = [keep.tile([P, S], F32, name="dx%d" % h) for h in range(K // P)]
 
         def gather(a, j, dst, c0, c1):
@@ -125,7 +125,9 @@ def tile_moe_bds_lin_none_kernel(tc, dyT, w_words, w_scales, gate, offs, pos1, p
                 for s0, s1 in spans(cuts, c0):
                     gather(a, j, planes[:, j, s0 - c0 : s1 - c0], s0, s1)
             if c0 == 0:
-                interleave(d_bf[:, a * T * PACK : (a + 1) * T * PACK], dy_all[a][:].rearrange("p (j t) -> p j t", j=PACK))
+                rows = dy_all[a][:].rearrange("p (j t) -> p j t", j=PACK)
+                for b in range(2):
+                    interleave(d_bf[b][:, a * HALF * PACK : (a + 1) * HALF * PACK], rows[:, :, b * HALF : (b + 1) * HALF])
             step = c1 - c0 if a < PASSES - 1 else T
             for q0 in range(c0, c1, step):
                 q1 = min(q0 + step, c1)
@@ -137,34 +139,40 @@ def tile_moe_bds_lin_none_kernel(tc, dyT, w_words, w_scales, gate, offs, pos1, p
                 for b0 in range(c0, c1, width):
                     for h in range(K // P if u < len(units) - 2 else 1):
                         slot_sums(h, b0, width)
-        for b0 in range(S - 2 * MM, S, MM):
-            slot_sums(1, b0, MM)
 
-        d_first = gath.tile([P, T], U32, name="g_f32", align_bytes=64)
-        d_rest = gath.tile([P, 2 * T], U32, name="g_f32", align_bytes=64)
-        nc.vector.quantize_mx(out=d_first[:].bitcast(FP8X4), scales=d_exp[:, 0:T], in_=d_bf[:, 0 : T * PACK])
-        nc.vector.quantize_mx(out=d_rest[:].bitcast(FP8X4), scales=d_exp[:, T:], in_=d_bf[:, T * PACK :])
-        d_codes = [d_first[:], d_rest[:, 0:T], d_rest[:, T:]]
-        d_exps = [d_exp[:, a * T : (a + 1) * T] for a in range(PASSES)]
+        ds_sb = [keep.tile([P, T], F32, name="ds_sb%d" % h) for h in range(K // P)]
+
+        def shared_sums(h, b, codes):
+            acc = psum.tile([P, HALF], F32, name="acc")
+            by_pass = [codes[:, a * HALF : (a + 1) * HALF] for a in range(PASSES)]
+            exps = [d_exp[b][:, a * HALF : (a + 1) * HALF] for a in range(PASSES)]
+            for m0 in range(0, HALF, MM):
+                product(acc[:, m0 : m0 + MM], E, h, by_pass, exps, m0, m0 + MM)
+            nc.scalar.copy(out=ds_sb[h][:, b * HALF : (b + 1) * HALF], in_=acc[:])
+
+        for b in range(2):
+            d_codes = gath.tile([P, PASSES * HALF], U32, name="g_f32", align_bytes=64)
+            for w0, w1 in spans((2 * HALF, HALF)):
+                nc.vector.quantize_mx(out=d_codes[:, w0:w1].bitcast(FP8X4), scales=d_exp[b][:, w0:w1], in_=d_bf[b][:, w0 * PACK : w1 * PACK])
+            shared_sums(0, b, d_codes)
+            if b == 0:
+                for b0 in range(S - 2 * MM, S, MM):
+                    slot_sums(1, b0, MM)
+            shared_sums(1, b, d_codes)
+
+        totals = [[keep.tile([P, T], F32, name="total%d_%d" % (h, r)) for r in range(3)] for h in range(K // P)]
+
+        def combine(h, r, t0, t1):
+            before = ds_sb[h] if r == 0 else totals[h][r - 1]
+            nc.vector.tensor_tensor(totals[h][r][:, t0:t1], dx[h][:].indirect(token_slot[r][:, t0 // 16 : t1 // 16]), before[:, t0:t1], ADD)
+            if r == 2:
+                nc.sync.dma_start(out=out[P * h : P * (h + 1), t0:t1], in_=totals[h][r][:, t0:t1])
+
+        for t0, t1 in spans((HALF, HALF)):
+            for h in range(K // P):
+                combine(h, 0, t0, t1)
         for h in range(K // P):
-            ds = psum_s.tile([P, T], F32, name="ds%d" % h)
-            product(ds[:], E, h, d_codes, d_exps, 0, T, (1, 2, 0))
-            picked = [keep.tile([P, T], F32, name="picked%d_%d" % (h, r)) for r in range(3)]
-            for r in range(3):
-                for t0, t1 in spans((T // 2, T // 2) if (h, r) == (1, 2) else (T,)):
-                    nc.vector.tensor_copy(picked[r][:, t0:t1], dx[h][:].indirect(token_slot[r][:, t0 // 16 : t1 // 16]))
-            if h == 0:
-                ds_sb = keep.tile([P, T], F32, name="ds_sb")
-                nc.scalar.copy(out=ds_sb[:], in_=ds[:])
-                nc.gpsimd.tensor_tensor(ds_sb[:], ds_sb[:], picked[0][:], ADD)
-                nc.gpsimd.tensor_tensor(ds_sb[:], ds_sb[:], picked[1][:], ADD)
-                nc.gpsimd.tensor_tensor(picked[2][:], picked[2][:], ds_sb[:], ADD)
-                nc.sync.dma_start(out=out[0:P, :], in_=picked[2][:])
-                continue
-            halves = spans((T // 2, T // 2))
-            nc.gpsimd.tensor_tensor(ds_sb[:], picked[0][:], picked[1][:], ADD)
-            for t0, t1 in halves:
-                nc.vector.tensor_tensor(picked[2][:, t0:t1], picked[2][:, t0:t1], ds[:, t0:t1], ADD)
-            for t0, t1 in halves:
-                nc.vector.tensor_tensor(picked[2][:, t0:t1], ds_sb[:, t0:t1], picked[2][:, t0:t1], ADD)
-                nc.sync.dma_start(out=out[P * h : P * (h + 1), t0:t1], in_=picked[2][:, t0:t1])
+            combine(h, 1, 0, T)
+        combine(0, 2, 0, T)
+        for t0, t1 in spans((HALF, HALF)):
+            combine(1, 2, t0, t1)

@@ -25,7 +25,6 @@ ADD = mybir.AluOpType.add
 HALF = T // 2
 FIRST = 1024
 HEAD_CUTS = (128, 256, 640)
-LAST_CUTS = (256, 128, 128)
 ROW_ORDER = (1, 2, 3, 0)
 
 
@@ -44,7 +43,8 @@ def tile_moe_bds_lin_none_kernel(tc, dyT, w_words, w_scales, gate, offs, pos1, p
         keep = ctx.enter_context(tc.tile_pool(name="keep", bufs=1))
         gath = ctx.enter_context(tc.tile_pool(name="gath", bufs=2))
         stage = ctx.enter_context(tc.tile_pool(name="stage", bufs=3))
-        psum = ctx.enter_context(tc.psum_pool(name="psum", bufs=8))
+        psum = ctx.enter_context(tc.psum_pool(name="psum", bufs=4))
+        psum_end = ctx.enter_context(tc.psum_pool(name="psum_end", bufs=1))
 
         slot_token = lists.tile([P, S // 16], U16, name="slot_token")
         token_slot = [lists.tile([P, T // 16], U16, name="token_slot%d" % r) for r in range(3)]
@@ -62,11 +62,11 @@ def tile_moe_bds_lin_none_kernel(tc, dyT, w_words, w_scales, gate, offs, pos1, p
             for j in range(1, PACK):
                 window[a, j] = keep.tile([P, FIRST + 16], F32, name="window%d_%d" % (a, j))
 
-        nc.sync.dma_start(slot_token[:], offs)
         for a in range(PASSES):
             for j in range(1, PACK):
                 nc.sync.dma_start(out=window[a, j][:, 0:T], in_=dy_rows[a, :, j, :])
                 if (a, j) == (0, 1):
+                    nc.sync.dma_start(slot_token[:], offs)
                     for c0, c1 in spans(HEAD_CUTS):
                         nc.sync.dma_start(out=gates[:, c0:c1], in_=gate[0:P, c0:c1])
             nc.sync.dma_start(out=dy_all[a][:], in_=dy_rows[a].rearrange("p j t -> p (j t)"))
@@ -81,10 +81,19 @@ def tile_moe_bds_lin_none_kernel(tc, dyT, w_words, w_scales, gate, offs, pos1, p
         for r, src in enumerate((pos1, pos2, pos3)):
             nc.sync.dma_start(token_slot[r][:], src)
 
-        g_codes = [keep.tile([P, S], U32, name="g_codes%d" % a, align_bytes=64) for a in range(PASSES)]
+        code_spans = [spans((FIRST, S - FIRST)), spans((FIRST, S - FIRST)), spans((T, T, S - FIRST))]
+        code_tiles = {}
+        for a, c0, c1 in sorted(((a, c0, c1) for a in range(PASSES) for c0, c1 in code_spans[a]), key=lambda u: u[1]):
+            tag = "g_codes%d_%d" % (a, c0)
+            code_tiles[a, c0] = keep.tile([P, c1 - c0], U32, name="g_codes%d_%d" % (a, c0), tag=tag, align_bytes=64)
+
+        def g_codes(a, q0, q1):
+            c0 = max(c for c, stop in code_spans[a] if c <= q0)
+            return code_tiles[a, c0][:, q0 - c0 : q1 - c0]
+
         g_exp = [keep.tile([P, S], U8, name="g_exp%d" % a, align_bytes=64) for a in range(PASSES)]
-        d_exp = [keep.tile([P, PASSES * HALF], U8, name="d_exp%d" % b, align_bytes=64) for b in range(2)]
-        d_bf = [keep.tile([P, PASSES * HALF * PACK], BF16, name="d_bf%d" % b, align_bytes=64) for b in range(2)]
+        d_exp = keep.tile([P, PASSES * T], U8, name="d_exp", align_bytes=64)
+        d_bf = keep.tile([P, PASSES * T * PACK], BF16, name="d_bf", align_bytes=64)
         dx = [keep.tile([P, S], F32, name="dx%d" % h) for h in range(K // P)]
 
         def gather(a, j, dst, c0, c1):
@@ -96,69 +105,111 @@ def tile_moe_bds_lin_none_kernel(tc, dyT, w_words, w_scales, gate, offs, pos1, p
                 in_=src.rearrange("p j (c i) -> p c j i", i=4),
             )
 
-        def product(acc, e, h, codes, exps, c0, c1, order=(0, 1, 2)):
-            for a in order:
+        def product(acc, e, h, codes, exps, passes, opening=0):
+            for a in passes:
                 g = e * PASSES + a
                 nc.tensor.matmul_mx(
                     out=acc,
                     lhsT=w_codes[:, g, 2 * P * h : 2 * P * (h + 1)].bitcast(FP4X4),
                     lhsT_scale=w_exp[:, g, P * h : P * (h + 1)],
-                    rhs=codes[a][:, c0:c1].bitcast(FP8X4),
-                    rhs_scale=exps[a][:, c0:c1],
-                    start=(a == order[0]),
-                    stop=(a == order[-1]),
+                    rhs=codes[a].bitcast(FP8X4),
+                    rhs_scale=exps[a],
+                    start=(a == opening),
+                    stop=(a == PASSES - 1),
                 )
+
+        def slot_product(acc, h, m0, passes):
+            product(acc, m0 // C, h, [g_codes(a, m0, m0 + MM) for a in range(PASSES)], [t[:, m0 : m0 + MM] for t in g_exp], passes, 0 if m0 < FIRST else 1)
 
         def slot_sums(h, b0, width):
             acc = psum.tile([P, width], F32, name="acc")
             for m0 in range(b0, b0 + width, MM):
-                product(acc[:, m0 - b0 : m0 - b0 + MM], m0 // C, h, g_codes, g_exp, m0, m0 + MM)
+                slot_product(acc[:, m0 - b0 : m0 - b0 + MM], h, m0, (0, 1, 2) if m0 < FIRST else (1, 0, 2))
             nc.scalar.copy(out=dx[h][:, b0 : b0 + width], in_=acc[:])
 
-        units = [(a, 0, FIRST) for a in range(PASSES)] + [(a, FIRST, S) for a in range(PASSES - 1)]
-        units += [(PASSES - 1, c0, c1) for c0, c1 in spans(LAST_CUTS, FIRST)]
-        for u, (a, c0, c1) in enumerate(units):
+        def gather_unit(a, c0, c1, head_cuts=None):
             g_f32 = gath.tile([P, PACK * (c1 - c0)], F32, name="g_f32", align_bytes=64)
             planes = g_f32[:].rearrange("p (j c) -> p j c", j=PACK)
             for j in ROW_ORDER:
-                cuts = HEAD_CUTS if (u, j) == (0, ROW_ORDER[0]) else (c1 - c0,)
-                for s0, s1 in spans(cuts, c0):
+                for s0, s1 in spans(head_cuts if head_cuts and j == ROW_ORDER[0] else (c1 - c0,), c0):
                     gather(a, j, planes[:, j, s0 - c0 : s1 - c0], s0, s1)
-            if c0 == 0:
-                rows = dy_all[a][:].rearrange("p (j t) -> p j t", j=PACK)
-                for b in range(2):
-                    interleave(d_bf[b][:, a * HALF * PACK : (a + 1) * HALF * PACK], rows[:, :, b * HALF : (b + 1) * HALF])
-            step = c1 - c0 if a < PASSES - 1 else T
-            for q0 in range(c0, c1, step):
-                q1 = min(q0 + step, c1)
-                g_bf = stage.tile([P, PACK * (q1 - q0)], BF16, name="g_bf", align_bytes=64)
-                interleave(g_bf[:], planes[:, :, q0 - c0 : q1 - c0])
-                nc.vector.quantize_mx(out=g_codes[a][:, q0:q1].bitcast(FP8X4), scales=g_exp[a][:, q0:q1], in_=g_bf[:])
-            if a == PASSES - 1:
-                width = min(T, c1 - c0)
-                for b0 in range(c0, c1, width):
-                    for h in range(K // P if u < len(units) - 2 else 1):
-                        slot_sums(h, b0, width)
+            return planes
+
+        def round_slots(planes, held=None):
+            if held:
+                g_bf = keep.tile([P, PACK * planes.shape[2]], BF16, name="bf_on_" + held, tag=held, align_bytes=64)
+            else:
+                g_bf = stage.tile([P, PACK * planes.shape[2]], BF16, name="g_bf", align_bytes=64)
+            interleave(g_bf[:], planes)
+            return g_bf
+
+        def quantize_slots(a, q0, q1, g_bf):
+            nc.vector.quantize_mx(out=g_codes(a, q0, q1).bitcast(FP8X4), scales=g_exp[a][:, q0:q1], in_=g_bf[:])
+
+        def quantize_tokens(codes, base, w0, w1):
+            nc.vector.quantize_mx(
+                out=codes[:, w0 - base : w1 - base].bitcast(FP8X4), scales=d_exp[:, w0:w1], in_=d_bf[:, w0 * PACK : w1 * PACK]
+            )
+
+        last = PASSES - 1
+        for a in range(PASSES):
+            planes = gather_unit(a, 0, FIRST, HEAD_CUTS if a == 0 else None)
+            nc.scalar.copy(
+                out=d_bf[:].rearrange("p (q a c i j) -> p q a c j i", a=PASSES, c=MM // 4, i=4, j=PACK)[:, :, a],
+                in_=dy_all[a][:].rearrange("p (j q c i) -> p q c j i", j=PACK, c=MM // 4, i=4),
+            )
+            for q0, q1 in spans((FIRST,) if a < last else (HALF, HALF, T)):
+                quantize_slots(a, q0, q1, round_slots(planes[:, :, q0:q1]))
+        for b0 in range(0, FIRST, T):
+            for h in range(K // P):
+                slot_sums(h, b0, T)
+        for a in range(last):
+            quantize_slots(a, FIRST, S, round_slots(gather_unit(a, FIRST, S), held="g_codes1_0" if a == 1 else None))
+
+        prev, end = S - 2 * MM, S - MM
+        open_sums = {}
+        for h in range(K // P):
+            for m0 in (prev, end):
+                open_sums[h, m0] = psum_end.tile([P, MM], F32, name="open%d_%d" % (h, m0))
+                slot_product(open_sums[h, m0][:], h, m0, (1, 0))
+
+        def close_sums(h, m0):
+            slot_product(open_sums[h, m0][:], h, m0, (last,))
+            nc.scalar.copy(out=dx[h][:, m0 : m0 + MM], in_=open_sums[h, m0][:])
+
+        quantize_slots(last, FIRST, prev, round_slots(gather_unit(last, FIRST, prev), held="g_codes2_%d" % T))
+        slot_sums(0, FIRST, prev - FIRST)
+        prev_bf = round_slots(gather_unit(last, prev, end))
+        end_bf = round_slots(gather_unit(last, end, S))
 
         ds_sb = [keep.tile([P, T], F32, name="ds_sb%d" % h) for h in range(K // P)]
+        half_words = PASSES * HALF
+        d_codes = [gath.tile([P, half_words], U32, name="g_f32", align_bytes=64) for b in range(2)]
 
-        def shared_sums(h, b, codes):
-            acc = psum.tile([P, HALF], F32, name="acc")
-            by_pass = [codes[:, a * HALF : (a + 1) * HALF] for a in range(PASSES)]
-            exps = [d_exp[b][:, a * HALF : (a + 1) * HALF] for a in range(PASSES)]
-            for m0 in range(0, HALF, MM):
-                product(acc[:, m0 : m0 + MM], E, h, by_pass, exps, m0, m0 + MM)
-            nc.scalar.copy(out=ds_sb[h][:, b * HALF : (b + 1) * HALF], in_=acc[:])
+        def shared_sums(h, quarters):
+            acc = psum.tile([P, MM * len(quarters)], F32, name="acc")
+            for i, q in enumerate(quarters):
+                first = [(q * PASSES + a) * MM for a in range(PASSES)]
+                codes = [d_codes[w // half_words][:, w % half_words : w % half_words + MM] for w in first]
+                product(acc[:, i * MM : (i + 1) * MM], E, h, codes, [d_exp[:, w : w + MM] for w in first], range(PASSES))
+            nc.scalar.copy(out=ds_sb[h][:, quarters[0] * MM : (quarters[-1] + 1) * MM], in_=acc[:])
 
-        for b in range(2):
-            d_codes = gath.tile([P, PASSES * HALF], U32, name="g_f32", align_bytes=64)
-            for w0, w1 in spans((2 * HALF, HALF)):
-                nc.vector.quantize_mx(out=d_codes[:, w0:w1].bitcast(FP8X4), scales=d_exp[b][:, w0:w1], in_=d_bf[b][:, w0 * PACK : w1 * PACK])
-            shared_sums(0, b, d_codes)
-            if b == 0:
-                for b0 in range(S - 2 * MM, S, MM):
-                    slot_sums(1, b0, MM)
-            shared_sums(1, b, d_codes)
+        quantize_slots(last, prev, end, prev_bf)
+        close_sums(0, prev)
+        quantize_tokens(d_codes[0], 0, 0, T)
+        shared_sums(0, (0,))
+        quantize_slots(last, end, S, end_bf)
+        close_sums(0, end)
+        quantize_tokens(d_codes[0], 0, T, half_words)
+        shared_sums(0, (1,))
+        slot_sums(1, FIRST, prev - FIRST)
+        close_sums(1, prev)
+        close_sums(1, end)
+        shared_sums(1, (0, 1))
+        for w0, w1 in spans((T, HALF), half_words):
+            quantize_tokens(d_codes[1], half_words, w0, w1)
+        for h in range(K // P):
+            shared_sums(h, (2, 3))
 
         totals = [[keep.tile([P, T], F32, name="total%d_%d" % (h, r)) for r in range(3)] for h in range(K // P)]
 
@@ -168,11 +219,13 @@ def tile_moe_bds_lin_none_kernel(tc, dyT, w_words, w_scales, gate, offs, pos1, p
             if r == 2:
                 nc.sync.dma_start(out=out[P * h : P * (h + 1), t0:t1], in_=totals[h][r][:, t0:t1])
 
-        for t0, t1 in spans((HALF, HALF)):
-            for h in range(K // P):
-                combine(h, 0, t0, t1)
+        combine(0, 0, 0, MM)
+        combine(0, 0, MM, HALF)
+        combine(1, 0, 0, HALF)
+        for h in range(K // P):
+            combine(h, 0, HALF, T)
         for h in range(K // P):
             combine(h, 1, 0, T)
         combine(0, 2, 0, T)
-        for t0, t1 in spans((HALF, HALF)):
+        for t0, t1 in spans((HALF, MM, MM)):
             combine(1, 2, t0, t1)

@@ -52,7 +52,7 @@ def tile_moe_bds_lin_none_kernel(tc, dyT, w_words, w_scales, gate, offs, pos1, p
         dy_rows = dyT.rearrange("(a p j) t -> a p j t", p=P, j=PACK)
         w_codes = keep.tile([P, (E + 1) * PASSES, 2 * K], U8, name="w_codes", align_bytes=64)
         w_exp = keep.tile([P, (E + 1) * PASSES, K], U8, name="w_exp", align_bytes=64)
-        nc.gpsimd.memset(w_exp[:].rearrange("p g k -> p (g k)").bitcast(I32), 0)
+        nc.vector.memset(w_exp[:].rearrange("p g k -> p (g k)").bitcast(I32), 0)
 
         gates = keep.tile([P, S], F32, name="gates")
         dy_all = [keep.tile([P, PACK * T], F32, name="dy_all%d" % a) for a in range(PASSES)]
@@ -164,7 +164,7 @@ def tile_moe_bds_lin_none_kernel(tc, dyT, w_words, w_scales, gate, offs, pos1, p
             for h in range(K // P):
                 slot_sums(h, b0, T)
         for a in range(last):
-            quantize_slots(a, FIRST, S, round_slots(gather_unit(a, FIRST, S), held="g_codes1_0" if a == 1 else None))
+            quantize_slots(a, FIRST, S, round_slots(gather_unit(a, FIRST, S), held="g_codes0_0" if a == 1 else None))
 
         prev, end = S - 2 * MM, S - MM
         open_sums = {}
@@ -177,9 +177,10 @@ def tile_moe_bds_lin_none_kernel(tc, dyT, w_words, w_scales, gate, offs, pos1, p
             slot_product(open_sums[h, m0][:], h, m0, (last,))
             nc.scalar.copy(out=dx[h][:, m0 : m0 + MM], in_=open_sums[h, m0][:])
 
-        quantize_slots(last, FIRST, prev, round_slots(gather_unit(last, FIRST, prev), held="g_codes2_%d" % T))
+        planes = gather_unit(last, FIRST, end)
+        quantize_slots(last, FIRST, prev, round_slots(planes[:, :, : prev - FIRST], held="g_codes1_0"))
         slot_sums(0, FIRST, prev - FIRST)
-        prev_bf = round_slots(gather_unit(last, prev, end))
+        prev_bf = round_slots(planes[:, :, prev - FIRST :], held="g_codes2_%d" % T)
         end_bf = round_slots(gather_unit(last, end, S))
 
         ds_sb = [keep.tile([P, T], F32, name="ds_sb%d" % h) for h in range(K // P)]
@@ -219,13 +220,14 @@ def tile_moe_bds_lin_none_kernel(tc, dyT, w_words, w_scales, gate, offs, pos1, p
             if r == 2:
                 nc.sync.dma_start(out=out[P * h : P * (h + 1), t0:t1], in_=totals[h][r][:, t0:t1])
 
-        combine(0, 0, 0, MM)
-        combine(0, 0, MM, HALF)
+        for r in range(2):
+            for t0, t1 in spans((MM, MM)):
+                combine(0, r, t0, t1)
         combine(1, 0, 0, HALF)
         for h in range(K // P):
             combine(h, 0, HALF, T)
-        for h in range(K // P):
-            combine(h, 1, 0, T)
+        combine(0, 1, HALF, T)
+        combine(1, 1, 0, T)
         combine(0, 2, 0, T)
         for t0, t1 in spans((HALF, MM, MM)):
             combine(1, 2, t0, t1)

@@ -23,9 +23,12 @@ MULT = mybir.AluOpType.mult
 ADD = mybir.AluOpType.add
 
 HALF = T // 2
+BANK = 512
 FIRST = 1024
 HEAD_CUTS = (128, 256, 640)
 ROW_ORDER = (1, 2, 3, 0)
+FIRST_LAST_CUTS = (256, 256, 512)
+TAIL_CUTS = (256, 128, 128)
 
 
 def spans(widths, first=0):
@@ -65,7 +68,7 @@ def tile_moe_bds_lin_none_kernel(tc, dyT, w_words, w_scales, gate, offs, pos1, p
         for a in range(PASSES):
             for j in range(1, PACK):
                 nc.sync.dma_start(out=window[a, j][:, 0:T], in_=dy_rows[a, :, j, :])
-                if (a, j) == (0, 1):
+                if (a, j) == (0, ROW_ORDER[0]):
                     nc.sync.dma_start(slot_token[:], offs)
                     for c0, c1 in spans(HEAD_CUTS):
                         nc.sync.dma_start(out=gates[:, c0:c1], in_=gate[0:P, c0:c1])
@@ -81,29 +84,23 @@ def tile_moe_bds_lin_none_kernel(tc, dyT, w_words, w_scales, gate, offs, pos1, p
         for r, src in enumerate((pos1, pos2, pos3)):
             nc.sync.dma_start(token_slot[r][:], src)
 
-        code_spans = [spans((FIRST, S - FIRST)), spans((FIRST, S - FIRST)), spans((T, T, S - FIRST))]
+        code_spans = [spans((FIRST, S - FIRST)), spans((FIRST, S - FIRST)), spans((BANK, BANK, S - FIRST))]
         code_tiles = {}
-        for a, c0, c1 in sorted(((a, c0, c1) for a in range(PASSES) for c0, c1 in code_spans[a]), key=lambda u: u[1]):
-            tag = "g_codes%d_%d" % (a, c0)
-            code_tiles[a, c0] = keep.tile([P, c1 - c0], U32, name="g_codes%d_%d" % (a, c0), tag=tag, align_bytes=64)
 
-        def g_codes(a, q0, q1):
-            c0 = max(c for c, stop in code_spans[a] if c <= q0)
-            return code_tiles[a, c0][:, q0 - c0 : q1 - c0]
+        def code_tag(a, c0):
+            return "g_codes%d_%d" % (a, c0)
+
+        for a, c0, c1 in sorted(((a, c0, c1) for a in range(PASSES) for c0, c1 in code_spans[a]), key=lambda u: u[1]):
+            code_tiles[a, c0] = keep.tile([P, c1 - c0], U32, name=code_tag(a, c0), tag=code_tag(a, c0), align_bytes=64)
+
+        def g_codes(a, c0, c1):
+            base = max(start for start, stop in code_spans[a] if start <= c0)
+            return code_tiles[a, base][:, c0 - base : c1 - base]
 
         g_exp = [keep.tile([P, S], U8, name="g_exp%d" % a, align_bytes=64) for a in range(PASSES)]
         d_exp = keep.tile([P, PASSES * T], U8, name="d_exp", align_bytes=64)
         d_bf = keep.tile([P, PASSES * T * PACK], BF16, name="d_bf", align_bytes=64)
         dx = [keep.tile([P, S], F32, name="dx%d" % h) for h in range(K // P)]
-
-        def gather(a, j, dst, c0, c1):
-            nc.vector.tensor_tensor(dst, window[a, j][:].indirect(slot_token[:, c0 // 16 : c1 // 16]), gates[:, c0:c1], MULT)
-
-        def interleave(dst, src):
-            nc.scalar.copy(
-                out=dst.rearrange("p (c i j) -> p c j i", i=4, j=PACK),
-                in_=src.rearrange("p j (c i) -> p c j i", i=4),
-            )
 
         def product(acc, e, h, codes, exps, passes, opening=0):
             for a in passes:
@@ -118,97 +115,109 @@ def tile_moe_bds_lin_none_kernel(tc, dyT, w_words, w_scales, gate, offs, pos1, p
                     stop=(a == PASSES - 1),
                 )
 
+        def pass_order(m0):
+            return (0, 1, 2) if m0 < FIRST else (1, 0, 2)
+
         def slot_product(acc, h, m0, passes):
-            product(acc, m0 // C, h, [g_codes(a, m0, m0 + MM) for a in range(PASSES)], [t[:, m0 : m0 + MM] for t in g_exp], passes, 0 if m0 < FIRST else 1)
+            codes = [g_codes(a, m0, m0 + MM) for a in range(PASSES)]
+            product(acc, m0 // C, h, codes, [t[:, m0 : m0 + MM] for t in g_exp], passes, pass_order(m0)[0])
 
         def slot_sums(h, b0, width):
             acc = psum.tile([P, width], F32, name="acc")
             for m0 in range(b0, b0 + width, MM):
-                slot_product(acc[:, m0 - b0 : m0 - b0 + MM], h, m0, (0, 1, 2) if m0 < FIRST else (1, 0, 2))
+                slot_product(acc[:, m0 - b0 : m0 - b0 + MM], h, m0, pass_order(m0))
             nc.scalar.copy(out=dx[h][:, b0 : b0 + width], in_=acc[:])
 
-        def gather_unit(a, c0, c1, head_cuts=None):
+        def gather_rows(a, c0, c1, head_cuts=None):
             g_f32 = gath.tile([P, PACK * (c1 - c0)], F32, name="g_f32", align_bytes=64)
-            planes = g_f32[:].rearrange("p (j c) -> p j c", j=PACK)
+            rows = g_f32[:].rearrange("p (j c) -> p j c", j=PACK)
             for j in ROW_ORDER:
                 for s0, s1 in spans(head_cuts if head_cuts and j == ROW_ORDER[0] else (c1 - c0,), c0):
-                    gather(a, j, planes[:, j, s0 - c0 : s1 - c0], s0, s1)
-            return planes
+                    picked = window[a, j][:].indirect(slot_token[:, s0 // 16 : s1 // 16])
+                    nc.vector.tensor_tensor(rows[:, j, s0 - c0 : s1 - c0], picked, gates[:, s0:s1], MULT)
+            return rows
 
-        def round_slots(planes, held=None):
-            if held:
-                g_bf = keep.tile([P, PACK * planes.shape[2]], BF16, name="bf_on_" + held, tag=held, align_bytes=64)
+        def round_slots(rows, reuse=None):
+            if reuse:
+                g_bf = keep.tile([P, PACK * rows.shape[2]], BF16, name="bf_on_" + reuse, tag=reuse, align_bytes=64)
             else:
-                g_bf = stage.tile([P, PACK * planes.shape[2]], BF16, name="g_bf", align_bytes=64)
-            interleave(g_bf[:], planes)
+                g_bf = stage.tile([P, PACK * rows.shape[2]], BF16, name="g_bf", align_bytes=64)
+            nc.scalar.copy(
+                out=g_bf[:].rearrange("p (c i j) -> p c j i", i=4, j=PACK),
+                in_=rows.rearrange("p j (c i) -> p c j i", i=4),
+            )
             return g_bf
 
-        def quantize_slots(a, q0, q1, g_bf):
-            nc.vector.quantize_mx(out=g_codes(a, q0, q1).bitcast(FP8X4), scales=g_exp[a][:, q0:q1], in_=g_bf[:])
-
-        def quantize_tokens(codes, base, w0, w1):
-            nc.vector.quantize_mx(
-                out=codes[:, w0 - base : w1 - base].bitcast(FP8X4), scales=d_exp[:, w0:w1], in_=d_bf[:, w0 * PACK : w1 * PACK]
-            )
+        def quantize_slots(a, c0, c1, g_bf):
+            nc.vector.quantize_mx(out=g_codes(a, c0, c1).bitcast(FP8X4), scales=g_exp[a][:, c0:c1], in_=g_bf[:])
 
         last = PASSES - 1
         for a in range(PASSES):
-            planes = gather_unit(a, 0, FIRST, HEAD_CUTS if a == 0 else None)
+            rows = gather_rows(a, 0, FIRST, HEAD_CUTS if a == 0 else None)
             nc.scalar.copy(
                 out=d_bf[:].rearrange("p (q a c i j) -> p q a c j i", a=PASSES, c=MM // 4, i=4, j=PACK)[:, :, a],
                 in_=dy_all[a][:].rearrange("p (j q c i) -> p q c j i", j=PACK, c=MM // 4, i=4),
             )
-            for q0, q1 in spans((FIRST,) if a < last else (HALF, HALF, T)):
-                quantize_slots(a, q0, q1, round_slots(planes[:, :, q0:q1]))
-        for b0 in range(0, FIRST, T):
+            for c0, c1 in spans((FIRST,) if a < last else FIRST_LAST_CUTS):
+                quantize_slots(a, c0, c1, round_slots(rows[:, :, c0:c1]))
+        for b0 in range(0, FIRST, BANK):
             for h in range(K // P):
-                slot_sums(h, b0, T)
-        for a in range(last):
-            quantize_slots(a, FIRST, S, round_slots(gather_unit(a, FIRST, S), held="g_codes0_0" if a == 1 else None))
+                slot_sums(h, b0, BANK)
+
+        quantize_slots(0, FIRST, S, round_slots(gather_rows(0, FIRST, S)))
+        quantize_slots(1, FIRST, S, round_slots(gather_rows(1, FIRST, S), reuse=code_tag(0, 0)))
 
         prev, end = S - 2 * MM, S - MM
         open_sums = {}
         for h in range(K // P):
             for m0 in (prev, end):
                 open_sums[h, m0] = psum_end.tile([P, MM], F32, name="open%d_%d" % (h, m0))
-                slot_product(open_sums[h, m0][:], h, m0, (1, 0))
+                slot_product(open_sums[h, m0][:], h, m0, pass_order(m0)[:last])
 
         def close_sums(h, m0):
             slot_product(open_sums[h, m0][:], h, m0, (last,))
             nc.scalar.copy(out=dx[h][:, m0 : m0 + MM], in_=open_sums[h, m0][:])
 
-        planes = gather_unit(last, FIRST, end)
-        quantize_slots(last, FIRST, prev, round_slots(planes[:, :, : prev - FIRST], held="g_codes1_0"))
+        rows = gather_rows(last, FIRST, end)
+        quantize_slots(last, FIRST, prev, round_slots(rows[:, :, : prev - FIRST], reuse=code_tag(1, 0)))
         slot_sums(0, FIRST, prev - FIRST)
-        prev_bf = round_slots(planes[:, :, prev - FIRST :], held="g_codes2_%d" % T)
-        end_bf = round_slots(gather_unit(last, end, S))
+        prev_bf = round_slots(rows[:, :, prev - FIRST :], reuse=code_tag(last, BANK))
+        end_bf = round_slots(gather_rows(last, end, S))
 
         ds_sb = [keep.tile([P, T], F32, name="ds_sb%d" % h) for h in range(K // P)]
-        half_words = PASSES * HALF
-        d_codes = [gath.tile([P, half_words], U32, name="g_f32", align_bytes=64) for b in range(2)]
+        ahead = 5 * MM
+        d_codes = [gath.tile([P, words], U32, name="g_f32", align_bytes=64) for words in (ahead, PASSES * T - ahead)]
+
+        def token_words(w0, w1):
+            return d_codes[0][:, w0:w1] if w0 < ahead else d_codes[1][:, w0 - ahead : w1 - ahead]
+
+        def quantize_tokens(w0, w1):
+            nc.vector.quantize_mx(out=token_words(w0, w1).bitcast(FP8X4), scales=d_exp[:, w0:w1], in_=d_bf[:, w0 * PACK : w1 * PACK])
 
         def shared_sums(h, quarters):
             acc = psum.tile([P, MM * len(quarters)], F32, name="acc")
             for i, q in enumerate(quarters):
-                first = [(q * PASSES + a) * MM for a in range(PASSES)]
-                codes = [d_codes[w // half_words][:, w % half_words : w % half_words + MM] for w in first]
-                product(acc[:, i * MM : (i + 1) * MM], E, h, codes, [d_exp[:, w : w + MM] for w in first], range(PASSES))
+                starts = [(q * PASSES + a) * MM for a in range(PASSES)]
+                codes = [token_words(w, w + MM) for w in starts]
+                product(acc[:, i * MM : (i + 1) * MM], E, h, codes, [d_exp[:, w : w + MM] for w in starts], range(PASSES))
             nc.scalar.copy(out=ds_sb[h][:, quarters[0] * MM : (quarters[-1] + 1) * MM], in_=acc[:])
 
+        wide, narrow = 4 * MM, 2 * MM
         quantize_slots(last, prev, end, prev_bf)
         close_sums(0, prev)
-        quantize_tokens(d_codes[0], 0, 0, T)
+        quantize_tokens(0, wide)
         shared_sums(0, (0,))
+        quantize_tokens(wide, ahead)
         quantize_slots(last, end, S, end_bf)
         close_sums(0, end)
-        quantize_tokens(d_codes[0], 0, T, half_words)
+        quantize_tokens(ahead, wide + narrow)
         shared_sums(0, (1,))
         slot_sums(1, FIRST, prev - FIRST)
         close_sums(1, prev)
         close_sums(1, end)
         shared_sums(1, (0, 1))
-        for w0, w1 in spans((T, HALF), half_words):
-            quantize_tokens(d_codes[1], half_words, w0, w1)
+        for w0, w1 in spans((wide, narrow), wide + narrow):
+            quantize_tokens(w0, w1)
         for h in range(K // P):
             shared_sums(h, (2, 3))
 
@@ -216,7 +225,8 @@ def tile_moe_bds_lin_none_kernel(tc, dyT, w_words, w_scales, gate, offs, pos1, p
 
         def combine(h, r, t0, t1):
             before = ds_sb[h] if r == 0 else totals[h][r - 1]
-            nc.vector.tensor_tensor(totals[h][r][:, t0:t1], dx[h][:].indirect(token_slot[r][:, t0 // 16 : t1 // 16]), before[:, t0:t1], ADD)
+            picked = dx[h][:].indirect(token_slot[r][:, t0 // 16 : t1 // 16])
+            nc.vector.tensor_tensor(totals[h][r][:, t0:t1], picked, before[:, t0:t1], ADD)
             if r == 2:
                 nc.sync.dma_start(out=out[P * h : P * (h + 1), t0:t1], in_=totals[h][r][:, t0:t1])
 
@@ -229,5 +239,5 @@ def tile_moe_bds_lin_none_kernel(tc, dyT, w_words, w_scales, gate, offs, pos1, p
         combine(0, 1, HALF, T)
         combine(1, 1, 0, T)
         combine(0, 2, 0, T)
-        for t0, t1 in spans((HALF, MM, MM)):
+        for t0, t1 in spans(TAIL_CUTS):
             combine(1, 2, t0, t1)

@@ -25,7 +25,7 @@ ADD = mybir.AluOpType.add
 HALF = T // 2
 BANK = 512
 FIRST = 1024
-HEAD_CUTS = (128, 256, 640)
+HEAD_CUTS = (128, 192, 288, 416)
 ROW_ORDER = (1, 2, 3, 0)
 FIRST_LAST_CUTS = (256, 256, 512)
 TAIL_CUTS = (256, 128, 128)

@@ -24,10 +24,9 @@ ADD = mybir.AluOpType.add
 
 HALF = T // 2
 BANK = 512
-FIRST = 1024
-HEAD_CUTS = (128, 192, 288, 416)
+HEAD_CUTS = (128, 256, 448, 704)
 ROW_ORDER = (1, 2, 3, 0)
-FIRST_LAST_CUTS = (256, 256, 512)
+A1, A2, B_END = 512, 896, 1280
 TAIL_CUTS = (256, 128, 128)
 
 
@@ -44,9 +43,8 @@ def tile_moe_bds_lin_none_kernel(tc, dyT, w_words, w_scales, gate, offs, pos1, p
     with ExitStack() as ctx:
         lists = ctx.enter_context(tc.tile_pool(name="lists", bufs=1))
         keep = ctx.enter_context(tc.tile_pool(name="keep", bufs=1))
-        gath = ctx.enter_context(tc.tile_pool(name="gath", bufs=2))
-        stage = ctx.enter_context(tc.tile_pool(name="stage", bufs=3))
-        psum = ctx.enter_context(tc.psum_pool(name="psum", bufs=4))
+        over = ctx.enter_context(tc.tile_pool(name="over", bufs=1))
+        psum = ctx.enter_context(tc.psum_pool(name="psum", bufs=3))
         psum_end = ctx.enter_context(tc.psum_pool(name="psum_end", bufs=1))
 
         slot_token = lists.tile([P, S // 16], U16, name="slot_token")
@@ -57,13 +55,14 @@ def tile_moe_bds_lin_none_kernel(tc, dyT, w_words, w_scales, gate, offs, pos1, p
         w_exp = keep.tile([P, (E + 1) * PASSES, K], U8, name="w_exp", align_bytes=64)
         nc.vector.memset(w_exp[:].rearrange("p g k -> p (g k)").bitcast(I32), 0)
 
+        last = PASSES - 1
         gates = keep.tile([P, S], F32, name="gates")
         dy_all = [keep.tile([P, PACK * T], F32, name="dy_all%d" % a) for a in range(PASSES)]
         window = {}
         for a in range(PASSES):
             window[a, 0] = dy_all[a]
             for j in range(1, PACK):
-                window[a, j] = keep.tile([P, FIRST + 16], F32, name="window%d_%d" % (a, j))
+                window[a, j] = keep.tile([P, (S if a < last else A2) + 16], F32, name="window%d_%d" % (a, j))
 
         for a in range(PASSES):
             for j in range(1, PACK):
@@ -73,7 +72,6 @@ def tile_moe_bds_lin_none_kernel(tc, dyT, w_words, w_scales, gate, offs, pos1, p
                     for c0, c1 in spans(HEAD_CUTS):
                         nc.sync.dma_start(out=gates[:, c0:c1], in_=gate[0:P, c0:c1])
             nc.sync.dma_start(out=dy_all[a][:], in_=dy_rows[a].rearrange("p j t -> p (j t)"))
-        nc.sync.dma_start(out=gates[:, FIRST:S], in_=gate[0:P, FIRST:S])
         w_src = w_words.rearrange("e a p b -> p (e a) b")
         for e in range(E + 1):
             g = slice(e * PASSES, (e + 1) * PASSES)
@@ -84,144 +82,191 @@ def tile_moe_bds_lin_none_kernel(tc, dyT, w_words, w_scales, gate, offs, pos1, p
         for r, src in enumerate((pos1, pos2, pos3)):
             nc.sync.dma_start(token_slot[r][:], src)
 
-        code_spans = [spans((FIRST, S - FIRST)), spans((FIRST, S - FIRST)), spans((BANK, BANK, S - FIRST))]
-        code_tiles = {}
-
-        def code_tag(a, c0):
-            return "g_codes%d_%d" % (a, c0)
-
-        for a, c0, c1 in sorted(((a, c0, c1) for a in range(PASSES) for c0, c1 in code_spans[a]), key=lambda u: u[1]):
-            code_tiles[a, c0] = keep.tile([P, c1 - c0], U32, name=code_tag(a, c0), tag=code_tag(a, c0), align_bytes=64)
-
-        def g_codes(a, c0, c1):
-            base = max(start for start, stop in code_spans[a] if start <= c0)
-            return code_tiles[a, base][:, c0 - base : c1 - base]
-
-        g_exp = [keep.tile([P, S], U8, name="g_exp%d" % a, align_bytes=64) for a in range(PASSES)]
+        TAIL = S - B_END
+        HELD = B_END - MM
+        NH = S - HELD
+        ga = over.tile([P, PACK * S], F32, name="ga", align_bytes=64, offset=0)
+        gb = keep.tile([P, PACK * S], F32, name="gb", tag="gb", align_bytes=64)
+        bf_main = keep.tile([P, last * HELD * PACK], BF16, name="bf_main", align_bytes=64)
+        bf_tail = keep.tile([P, last * NH * PACK], BF16, name="bf_tail", align_bytes=64)
+        codes_main = keep.tile([P, last * HELD], U32, name="codes_main", align_bytes=64)
+        exp_main = keep.tile([P, last * HELD], U8, name="exp_main", align_bytes=64)
+        exp_tail = keep.tile([P, last * NH], U8, name="exp_tail", align_bytes=64)
+        codes_a = keep.tile([P, A1], U32, name="codes_a", tag="codes_a", align_bytes=64)
+        codes_last = keep.tile([P, S], U32, name="codes_last", align_bytes=64)
+        exp_last = keep.tile([P, S], U8, name="exp_last", align_bytes=64)
         d_exp = keep.tile([P, PASSES * T], U8, name="d_exp", align_bytes=64)
         d_bf = keep.tile([P, PASSES * T * PACK], BF16, name="d_bf", align_bytes=64)
         dx = [keep.tile([P, S], F32, name="dx%d" % h) for h in range(K // P)]
+        late = {}
 
-        def product(acc, e, h, codes, exps, passes, opening=0):
+        def slot_operand(a, m0):
+            if a == last:
+                return (codes_a if m0 < A1 else codes_last)[:, m0 : m0 + MM], exp_last[:, m0 : m0 + MM]
+            if m0 < HELD:
+                w = a * HELD + m0
+                return codes_main[:, w : w + MM], exp_main[:, w : w + MM]
+            w = ((m0 - HELD) // MM * last + a) * MM
+            return late["codes_tail"][:, w : w + MM], exp_tail[:, w : w + MM]
+
+        def product(acc, e, h, operand, passes):
             for a in passes:
                 g = e * PASSES + a
+                codes, exps = operand(a)
                 nc.tensor.matmul_mx(
                     out=acc,
                     lhsT=w_codes[:, g, 2 * P * h : 2 * P * (h + 1)].bitcast(FP4X4),
                     lhsT_scale=w_exp[:, g, P * h : P * (h + 1)],
-                    rhs=codes[a].bitcast(FP8X4),
-                    rhs_scale=exps[a],
-                    start=(a == opening),
-                    stop=(a == PASSES - 1),
+                    rhs=codes.bitcast(FP8X4),
+                    rhs_scale=exps,
+                    start=(a == 0),
+                    stop=(a == last),
                 )
 
-        def pass_order(m0):
-            return (0, 1, 2) if m0 < FIRST else (1, 0, 2)
-
         def slot_product(acc, h, m0, passes):
-            codes = [g_codes(a, m0, m0 + MM) for a in range(PASSES)]
-            product(acc, m0 // C, h, codes, [t[:, m0 : m0 + MM] for t in g_exp], passes, pass_order(m0)[0])
+            product(acc, m0 // C, h, lambda a: slot_operand(a, m0), passes)
 
-        def slot_sums(h, b0, width):
-            acc = psum.tile([P, width], F32, name="acc")
-            for m0 in range(b0, b0 + width, MM):
-                slot_product(acc[:, m0 - b0 : m0 - b0 + MM], h, m0, pass_order(m0))
-            nc.scalar.copy(out=dx[h][:, b0 : b0 + width], in_=acc[:])
+        def slot_sums(h, b0, b1, acc=None):
+            if acc is None:
+                acc = psum.tile([P, b1 - b0], F32, name="acc")
+            for m0 in range(b0, b1, MM):
+                slot_product(acc[:, m0 - b0 : m0 - b0 + MM], h, m0, range(PASSES))
+            return acc
 
-        def gather_rows(a, c0, c1, head_cuts=None):
-            g_f32 = gath.tile([P, PACK * (c1 - c0)], F32, name="g_f32", align_bytes=64)
-            rows = g_f32[:].rearrange("p (j c) -> p j c", j=PACK)
-            for j in ROW_ORDER:
-                for s0, s1 in spans(head_cuts if head_cuts and j == ROW_ORDER[0] else (c1 - c0,), c0):
-                    picked = window[a, j][:].indirect(slot_token[:, s0 // 16 : s1 // 16])
-                    nc.vector.tensor_tensor(rows[:, j, s0 - c0 : s1 - c0], picked, gates[:, s0:s1], MULT)
-            return rows
+        def leave(acc, h, b0, b1):
+            nc.scalar.copy(out=dx[h][:, b0:b1], in_=acc[:])
 
-        def round_slots(rows, reuse=None):
-            if reuse:
-                g_bf = keep.tile([P, PACK * rows.shape[2]], BF16, name="bf_on_" + reuse, tag=reuse, align_bytes=64)
-            else:
-                g_bf = stage.tile([P, PACK * rows.shape[2]], BF16, name="g_bf", align_bytes=64)
+        def gather(rows, a, j, c0, c1, first):
+            picked = window[a, j][:].indirect(slot_token[:, c0 // 16 : c1 // 16])
+            nc.vector.tensor_tensor(rows[:, j, c0 - first : c1 - first], picked, gates[:, c0:c1], MULT)
+
+        def round_slots(g_bf, rows):
             nc.scalar.copy(
-                out=g_bf[:].rearrange("p (c i j) -> p c j i", i=4, j=PACK),
+                out=g_bf.rearrange("p (c i j) -> p c j i", i=4, j=PACK),
                 in_=rows.rearrange("p j (c i) -> p c j i", i=4),
             )
-            return g_bf
 
-        def quantize_slots(a, c0, c1, g_bf):
-            nc.vector.quantize_mx(out=g_codes(a, c0, c1).bitcast(FP8X4), scales=g_exp[a][:, c0:c1], in_=g_bf[:])
+        def quantize(codes, exps, g_bf, w0, w1, first=0):
+            nc.vector.quantize_mx(out=codes[:, w0:w1].bitcast(FP8X4), scales=exps[:, w0:w1], in_=g_bf[:, (w0 - first) * PACK : (w1 - first) * PACK])
 
-        last = PASSES - 1
-        for a in range(PASSES):
-            rows = gather_rows(a, 0, FIRST, HEAD_CUTS if a == 0 else None)
+        def round_tokens(a):
             nc.scalar.copy(
                 out=d_bf[:].rearrange("p (q a c i j) -> p q a c j i", a=PASSES, c=MM // 4, i=4, j=PACK)[:, :, a],
                 in_=dy_all[a][:].rearrange("p (j q c i) -> p q c j i", j=PACK, c=MM // 4, i=4),
             )
-            for c0, c1 in spans((FIRST,) if a < last else FIRST_LAST_CUTS):
-                quantize_slots(a, c0, c1, round_slots(rows[:, :, c0:c1]))
-        for b0 in range(0, FIRST, BANK):
-            for h in range(K // P):
-                slot_sums(h, b0, BANK)
 
-        quantize_slots(0, FIRST, S, round_slots(gather_rows(0, FIRST, S)))
-        quantize_slots(1, FIRST, S, round_slots(gather_rows(1, FIRST, S), reuse=code_tag(0, 0)))
+        half_words = PASSES * HALF
 
-        prev, end = S - 2 * MM, S - MM
-        open_sums = {}
+        def quantize_tokens(u, w0, w1):
+            first = u * half_words
+            nc.vector.quantize_mx(out=late["d_codes", u][:, w0:w1].bitcast(FP8X4), scales=d_exp[:, first + w0 : first + w1], in_=d_bf[:, (first + w0) * PACK : (first + w1) * PACK])
+
+        def shared_products(acc, h, u):
+            for i in range(HALF // MM):
+                def operand(a):
+                    w = (i * PASSES + a) * MM
+                    return late["d_codes", u][:, w : w + MM], d_exp[:, u * half_words + w : u * half_words + w + MM]
+                product(acc[:, i * MM : (i + 1) * MM], E, h, operand, range(PASSES))
+
+        for a, tile in enumerate((ga, gb)):
+            rows = tile[:].rearrange("p (j c) -> p j c", j=PACK)
+            for j in ROW_ORDER:
+                for c0, c1 in spans(HEAD_CUTS if (a, j) == (0, ROW_ORDER[0]) else (S,)):
+                    gather(rows, a, j, c0, c1, 0)
+            if a == 0:
+                round_tokens(0)
+            round_slots(bf_main[:, a * HELD * PACK : (a + 1) * HELD * PACK], rows[:, :, :HELD])
+            nc.scalar.copy(
+                out=bf_tail[:].rearrange("p (m a c i j) -> p m a c j i", a=last, c=MM // 4, i=4, j=PACK)[:, :, a],
+                in_=rows[:, :, HELD:].rearrange("p j (m c i) -> p m c j i", c=MM // 4, i=4),
+            )
+            if a == 0:
+                round_tokens(1)
+                round_tokens(2)
+                quantize(codes_main, exp_main, bf_main, 0, 1024)
+
+        rows_a = ga[:, : PACK * A2].rearrange("p (j c) -> p j c", j=PACK)
+        for j in ROW_ORDER:
+            gather(rows_a, last, j, 0, A2, 0)
+        rows_b = ga[:, 384 : 384 + PACK * 1088].rearrange("p (j c) -> p j c", j=PACK)[:, :, : B_END - A2]
+        gather(rows_b, last, 3, A2, B_END, A2)
+        total_tile = keep.tile([P, 8 * T], F32, name="totals", tag="gb", align_bytes=64)
+        ds_sb = [total_tile[:, (6 + h) * T : (7 + h) * T] for h in range(K // P)]
+        late["d_codes", 0] = keep.tile([P, half_words], U32, name="d_codes0", align_bytes=64)
+        for w0, w1 in spans((256, 512)):
+            quantize_tokens(0, w0, w1)
+        early = psum.tile([P, 2 * HALF], F32, name="acc")
         for h in range(K // P):
-            for m0 in (prev, end):
-                open_sums[h, m0] = psum_end.tile([P, MM], F32, name="open%d_%d" % (h, m0))
-                slot_product(open_sums[h, m0][:], h, m0, pass_order(m0)[:last])
+            shared_products(early[:, h * HALF : (h + 1) * HALF], h, 0)
+        for w0, w1 in spans((1024, 256), 1024):
+            quantize(codes_main, exp_main, bf_main, w0, w1)
+        pair0 = psum_end.tile([P, 2 * MM], F32, name="pair0", tag="pair0")
+        slot_product(pair0[:, :MM], 0, A2, range(last))
 
-        def close_sums(h, m0):
-            slot_product(open_sums[h, m0][:], h, m0, (last,))
-            nc.scalar.copy(out=dx[h][:, m0 : m0 + MM], in_=open_sums[h, m0][:])
-
-        rows = gather_rows(last, FIRST, end)
-        quantize_slots(last, FIRST, prev, round_slots(rows[:, :, : prev - FIRST], reuse=code_tag(1, 0)))
-        slot_sums(0, FIRST, prev - FIRST)
-        prev_bf = round_slots(rows[:, :, prev - FIRST :], reuse=code_tag(last, BANK))
-        end_bf = round_slots(gather_rows(last, end, S))
-
-        ds_sb = [keep.tile([P, T], F32, name="ds_sb%d" % h) for h in range(K // P)]
-        ahead = 5 * MM
-        d_codes = [gath.tile([P, words], U32, name="g_f32", align_bytes=64) for words in (ahead, PASSES * T - ahead)]
-
-        def token_words(w0, w1):
-            return d_codes[0][:, w0:w1] if w0 < ahead else d_codes[1][:, w0 - ahead : w1 - ahead]
-
-        def quantize_tokens(w0, w1):
-            nc.vector.quantize_mx(out=token_words(w0, w1).bitcast(FP8X4), scales=d_exp[:, w0:w1], in_=d_bf[:, w0 * PACK : w1 * PACK])
-
-        def shared_sums(h, quarters):
-            acc = psum.tile([P, MM * len(quarters)], F32, name="acc")
-            for i, q in enumerate(quarters):
-                starts = [(q * PASSES + a) * MM for a in range(PASSES)]
-                codes = [token_words(w, w + MM) for w in starts]
-                product(acc[:, i * MM : (i + 1) * MM], E, h, codes, [d_exp[:, w : w + MM] for w in starts], range(PASSES))
-            nc.scalar.copy(out=ds_sb[h][:, quarters[0] * MM : (quarters[-1] + 1) * MM], in_=acc[:])
-
-        wide, narrow = 4 * MM, 2 * MM
-        quantize_slots(last, prev, end, prev_bf)
-        close_sums(0, prev)
-        quantize_tokens(0, wide)
-        shared_sums(0, (0,))
-        quantize_tokens(wide, ahead)
-        quantize_slots(last, end, S, end_bf)
-        close_sums(0, end)
-        quantize_tokens(ahead, wide + narrow)
-        shared_sums(0, (1,))
-        slot_sums(1, FIRST, prev - FIRST)
-        close_sums(1, prev)
-        close_sums(1, end)
-        shared_sums(1, (0, 1))
-        for w0, w1 in spans((wide, narrow), wide + narrow):
-            quantize_tokens(w0, w1)
+        bf_a = keep.tile([P, A2 * PACK], BF16, name="bf_a", tag="chain", align_bytes=64)
+        for i, (c0, c1) in enumerate(spans((512, 256, 128))):
+            round_slots(bf_a[:, c0 * PACK : c1 * PACK], rows_a[:, :, c0:c1])
+            quantize(codes_a if i == 0 else codes_last, exp_last, bf_a, c0, c1)
+            if i == 1:
+                gather(rows_b, last, 0, A2, B_END, A2)
+        nc.scalar.copy(
+            out=total_tile[:, 6 * T :].rearrange("p (h t) -> p h t", h=2)[:, :, :HALF],
+            in_=early[:].rearrange("p (h t) -> p h t", h=2),
+        )
         for h in range(K // P):
-            shared_sums(h, (2, 3))
+            leave(slot_sums(h, 0, A1), h, 0, A1)
+        for j in (1, 2):
+            gather(rows_b, last, j, A2, B_END, A2)
+        a2_first = psum_end.tile([P, A2 - A1], F32, name="a2_first", tag="a2")
+        slot_sums(0, A1, A2, a2_first)
 
-        totals = [[keep.tile([P, T], F32, name="total%d_%d" % (h, r)) for r in range(3)] for h in range(K // P)]
+        gc = keep.tile([P, PACK * TAIL], F32, name="gc", tag="chain", align_bytes=64)
+        rows_c = gc[:].rearrange("p (j c) -> p j c", j=PACK)
+        for j in ROW_ORDER:
+            gather(rows_c, last, j, B_END, S, B_END)
+        bf_b = keep.tile([P, (B_END - A2) * PACK], BF16, name="bf_b", tag="codes_a", align_bytes=64)
+        for c0, c1 in spans((256, 128)):
+            round_slots(bf_b[:, c0 * PACK : c1 * PACK], rows_b[:, :, c0:c1])
+            quantize(codes_last, exp_last, bf_b, A2 + c0, A2 + c1, A2)
+            if c0 == 0:
+                leave(a2_first, 0, A1, A2)
+                a2_second = psum_end.tile([P, BANK], F32, name="a2_second", tag="a2")
+                slot_sums(1, A1, A2, a2_second)
+        bf_c = over.tile([P, TAIL * PACK], BF16, name="bf_c", align_bytes=64, offset=4096)
+        for c0, c1 in spans((MM, MM)):
+            round_slots(bf_c[:, c0 * PACK : c1 * PACK], rows_c[:, :, c0:c1])
+
+        slot_product(pair0[:, :MM], 0, A2, (last,))
+        slot_product(pair0[:, MM:], 0, A2 + MM, range(PASSES))
+        leave(pair0, 0, A2, HELD)
+        late["codes_tail"] = over.tile([P, last * NH], U32, name="codes_tail", align_bytes=64, offset=0)
+        quantize(late["codes_tail"], exp_tail, bf_tail, 0, 512)
+        pair1 = psum_end.tile([P, 2 * MM], F32, name="pair1", tag="pair1")
+        end_sums = psum_end.tile([P, MM], F32, name="end_sums", tag="end_sums")
+        slot_product(pair1[:, :MM], 0, HELD, range(PASSES))
+        quantize(codes_last, exp_last, bf_c, B_END, S - MM, B_END)
+        slot_product(pair1[:, MM:], 0, B_END, range(PASSES))
+        quantize(late["codes_tail"], exp_tail, bf_tail, 512, 768)
+        slot_product(end_sums[:], 0, S - MM, range(last))
+        leave(pair1, 0, HELD, S - MM)
+        quantize(codes_last, exp_last, bf_c, S - MM, S, B_END)
+        slot_product(end_sums[:], 0, S - MM, (last,))
+        leave(end_sums, 0, S - MM, S)
+        late["d_codes", 1] = keep.tile([P, half_words], U32, name="d_codes1", tag="chain", align_bytes=64)
+        for w0, w1 in spans((256, 512)):
+            quantize_tokens(1, w0, w1)
+        held = psum_end.tile([P, BANK], F32, name="held", tag="pair0")
+        slot_product(a2_second[:, A2 - A1 :], 1, S - MM, range(PASSES))
+        slot_sums(1, A2, S - MM, held)
+        nc.scalar.copy(out=dx[1][:, A1:A2], in_=a2_second[:, : A2 - A1])
+        nc.scalar.copy(out=dx[1][:, S - MM :], in_=a2_second[:, A2 - A1 :])
+        leave(held, 1, A2, S - MM)
+        for h in range(K // P):
+            acc = psum.tile([P, HALF], F32, name="acc")
+            shared_products(acc[:], h, 1)
+            nc.scalar.copy(out=ds_sb[h][:, HALF:], in_=acc[:])
+
+        totals = [[total_tile[:, (3 * h + r) * T : (3 * h + r + 1) * T] for r in range(3)] for h in range(K // P)]
 
         def combine(h, r, t0, t1):
             before = ds_sb[h] if r == 0 else totals[h][r - 1]

@@ -62,7 +62,7 @@ def tile_moe_bds_lin_none_kernel(tc, dyT, w_words, w_scales, gate, offs, pos1, p
         for a in range(PASSES):
             window[a, 0] = dy_all[a]
             for j in range(1, PACK):
-                window[a, j] = keep.tile([P, (S if a < last else A2) + 16], F32, name="window%d_%d" % (a, j))
+                window[a, j] = keep.tile([P, (S if a < last else A2) + 16], F32, name="window%d_%d" % (a, j), tag="window%d_%d" % (a, j), align_bytes=64)
 
         for a in range(PASSES):
             for j in range(1, PACK):
@@ -83,8 +83,9 @@ def tile_moe_bds_lin_none_kernel(tc, dyT, w_words, w_scales, gate, offs, pos1, p
             nc.sync.dma_start(token_slot[r][:], src)
 
         TAIL = S - B_END
-        HELD = B_END - MM
+        HELD = A2
         NH = S - HELD
+        MID = 4 * MM
         ga = over.tile([P, PACK * S], F32, name="ga", align_bytes=64, offset=0)
         gb = keep.tile([P, PACK * S], F32, name="gb", tag="gb", align_bytes=64)
         bf_main = keep.tile([P, last * HELD * PACK], BF16, name="bf_main", align_bytes=64)
@@ -92,7 +93,7 @@ def tile_moe_bds_lin_none_kernel(tc, dyT, w_words, w_scales, gate, offs, pos1, p
         codes_main = keep.tile([P, last * HELD], U32, name="codes_main", align_bytes=64)
         exp_main = keep.tile([P, last * HELD], U8, name="exp_main", align_bytes=64)
         exp_tail = keep.tile([P, last * NH], U8, name="exp_tail", align_bytes=64)
-        codes_a = keep.tile([P, A1], U32, name="codes_a", tag="codes_a", align_bytes=64)
+        codes_a = keep.tile([P, A2], U32, name="codes_a", tag="codes_a", align_bytes=64)
         codes_last = keep.tile([P, S], U32, name="codes_last", align_bytes=64)
         exp_last = keep.tile([P, S], U8, name="exp_last", align_bytes=64)
         d_exp = keep.tile([P, PASSES * T], U8, name="d_exp", align_bytes=64)
@@ -102,12 +103,14 @@ def tile_moe_bds_lin_none_kernel(tc, dyT, w_words, w_scales, gate, offs, pos1, p
 
         def slot_operand(a, m0):
             if a == last:
-                return (codes_a if m0 < A1 else codes_last)[:, m0 : m0 + MM], exp_last[:, m0 : m0 + MM]
+                return (codes_a if m0 < A2 else codes_last)[:, m0 : m0 + MM], exp_last[:, m0 : m0 + MM]
             if m0 < HELD:
                 w = a * HELD + m0
                 return codes_main[:, w : w + MM], exp_main[:, w : w + MM]
             w = ((m0 - HELD) // MM * last + a) * MM
-            return late["codes_tail"][:, w : w + MM], exp_tail[:, w : w + MM]
+            if w < MID:
+                return late["codes_mid"][:, w : w + MM], exp_tail[:, w : w + MM]
+            return late["codes_tail"][:, w - MID : w - MID + MM], exp_tail[:, w : w + MM]
 
         def product(acc, e, h, operand, passes):
             for a in passes:
@@ -183,13 +186,11 @@ def tile_moe_bds_lin_none_kernel(tc, dyT, w_words, w_scales, gate, offs, pos1, p
             if a == 0:
                 round_tokens(1)
                 round_tokens(2)
-                quantize(codes_main, exp_main, bf_main, 0, 1024)
 
         rows_a = ga[:, : PACK * A2].rearrange("p (j c) -> p j c", j=PACK)
         for j in ROW_ORDER:
             gather(rows_a, last, j, 0, A2, 0)
-        rows_b = ga[:, 384 : 384 + PACK * 1088].rearrange("p (j c) -> p j c", j=PACK)[:, :, : B_END - A2]
-        gather(rows_b, last, 3, A2, B_END, A2)
+        rows_b = ga[:, 256 : 256 + PACK * 1024].rearrange("p (j c) -> p j c", j=PACK)[:, :, : B_END - A2]
         total_tile = keep.tile([P, 8 * T], F32, name="totals", tag="gb", align_bytes=64)
         ds_sb = [total_tile[:, (6 + h) * T : (7 + h) * T] for h in range(K // P)]
         late["d_codes", 0] = keep.tile([P, half_words], U32, name="d_codes0", align_bytes=64)
@@ -198,69 +199,76 @@ def tile_moe_bds_lin_none_kernel(tc, dyT, w_words, w_scales, gate, offs, pos1, p
         early = psum.tile([P, 2 * HALF], F32, name="acc")
         for h in range(K // P):
             shared_products(early[:, h * HALF : (h + 1) * HALF], h, 0)
-        for w0, w1 in spans((1024, 256), 1024):
+        for w0, w1 in spans((1024, 512, 256)):
             quantize(codes_main, exp_main, bf_main, w0, w1)
-        pair0 = psum_end.tile([P, 2 * MM], F32, name="pair0", tag="pair0")
-        slot_product(pair0[:, :MM], 0, A2, range(last))
 
         bf_a = keep.tile([P, A2 * PACK], BF16, name="bf_a", tag="chain", align_bytes=64)
-        for i, (c0, c1) in enumerate(spans((512, 256, 128))):
+        for i, (c0, c1) in enumerate(spans((512, 128, 256))):
             round_slots(bf_a[:, c0 * PACK : c1 * PACK], rows_a[:, :, c0:c1])
-            quantize(codes_a if i == 0 else codes_last, exp_last, bf_a, c0, c1)
+            quantize(codes_a, exp_last, bf_a, c0, c1)
             if i == 1:
                 gather(rows_b, last, 0, A2, B_END, A2)
         nc.scalar.copy(
             out=total_tile[:, 6 * T :].rearrange("p (h t) -> p h t", h=2)[:, :, :HALF],
             in_=early[:].rearrange("p (h t) -> p h t", h=2),
         )
-        for h in range(K // P):
-            leave(slot_sums(h, 0, A1), h, 0, A1)
-        for j in (1, 2):
+        for j in (1, 2, 3):
             gather(rows_b, last, j, A2, B_END, A2)
-        a2_first = psum_end.tile([P, A2 - A1], F32, name="a2_first", tag="a2")
-        slot_sums(0, A1, A2, a2_first)
+        for b0, b1 in ((0, A1), (A1, A2)):
+            for h in range(K // P):
+                leave(slot_sums(h, b0, b1), h, b0, b1)
+
+        def quantize_held(codes, w0, w1, first):
+            nc.vector.quantize_mx(out=codes[:, w0 - first : w1 - first].bitcast(FP8X4), scales=exp_tail[:, w0:w1], in_=bf_tail[:, w0 * PACK : w1 * PACK])
 
         gc = keep.tile([P, PACK * TAIL], F32, name="gc", tag="chain", align_bytes=64)
         rows_c = gc[:].rearrange("p (j c) -> p j c", j=PACK)
         for j in ROW_ORDER:
             gather(rows_c, last, j, B_END, S, B_END)
-        bf_b = keep.tile([P, (B_END - A2) * PACK], BF16, name="bf_b", tag="codes_a", align_bytes=64)
-        for c0, c1 in spans((256, 128)):
-            round_slots(bf_b[:, c0 * PACK : c1 * PACK], rows_b[:, :, c0:c1])
-            quantize(codes_last, exp_last, bf_b, A2 + c0, A2 + c1, A2)
-            if c0 == 0:
-                leave(a2_first, 0, A1, A2)
-                a2_second = psum_end.tile([P, BANK], F32, name="a2_second", tag="a2")
-                slot_sums(1, A1, A2, a2_second)
-        bf_c = over.tile([P, TAIL * PACK], BF16, name="bf_c", align_bytes=64, offset=4096)
-        for c0, c1 in spans((MM, MM)):
-            round_slots(bf_c[:, c0 * PACK : c1 * PACK], rows_c[:, :, c0:c1])
+            if j == ROW_ORDER[1]:
+                late["codes_mid"] = keep.tile([P, MID], U32, name="codes_mid", tag="window%d_%d" % (last, ROW_ORDER[0]), align_bytes=64)
+                quantize_held(late["codes_mid"], 0, MID, 0)
+        b1, b2, b3, c1, c2 = range(A2, S, MM)
+        x0 = psum_end.tile([P, MM], F32, name="x0", tag="x0")
+        y0 = psum_end.tile([P, 3 * MM], F32, name="y0")
+        z0 = psum_end.tile([P, MM], F32, name="z0")
+        x1 = psum_end.tile([P, MM], F32, name="x1")
+        y1 = psum_end.tile([P, MM], F32, name="y1")
+        slot_product(x0[:], 0, b1, range(last))
+        slot_product(y0[:, :MM], 0, b2, range(last))
+        slot_product(x1[:], 1, b1, range(last))
+        slot_product(y1[:], 1, b2, range(last))
 
-        slot_product(pair0[:, :MM], 0, A2, (last,))
-        slot_product(pair0[:, MM:], 0, A2 + MM, range(PASSES))
-        leave(pair0, 0, A2, HELD)
-        late["codes_tail"] = over.tile([P, last * NH], U32, name="codes_tail", align_bytes=64, offset=0)
-        quantize(late["codes_tail"], exp_tail, bf_tail, 0, 512)
-        pair1 = psum_end.tile([P, 2 * MM], F32, name="pair1", tag="pair1")
-        end_sums = psum_end.tile([P, MM], F32, name="end_sums", tag="end_sums")
-        slot_product(pair1[:, :MM], 0, HELD, range(PASSES))
-        quantize(codes_last, exp_last, bf_c, B_END, S - MM, B_END)
-        slot_product(pair1[:, MM:], 0, B_END, range(PASSES))
-        quantize(late["codes_tail"], exp_tail, bf_tail, 512, 768)
-        slot_product(end_sums[:], 0, S - MM, range(last))
-        leave(pair1, 0, HELD, S - MM)
-        quantize(codes_last, exp_last, bf_c, S - MM, S, B_END)
-        slot_product(end_sums[:], 0, S - MM, (last,))
-        leave(end_sums, 0, S - MM, S)
+        bf_b = keep.tile([P, (B_END - A2) * PACK], BF16, name="bf_b", tag="codes_a", align_bytes=64)
+        round_slots(bf_b[:], rows_b)
+        bf_c = over.tile([P, TAIL * PACK], BF16, name="bf_c", align_bytes=64, offset=4096)
+        for u0, u1 in spans((MM, MM)):
+            round_slots(bf_c[:, u0 * PACK : u1 * PACK], rows_c[:, :, u0:u1])
+        quantize(codes_last, exp_last, bf_b, b1, b3, A2)
+        slot_product(x0[:], 0, b1, (last,))
+        leave(x0, 0, b1, b2)
+        slot_product(y0[:, :MM], 0, b2, (last,))
+        quantize(codes_last, exp_last, bf_b, b3, c1, A2)
+        late["codes_tail"] = over.tile([P, last * NH - MID], U32, name="codes_tail", align_bytes=64, offset=0)
+        quantize_held(late["codes_tail"], MID, MID + 512, MID)
+        slot_product(y0[:, MM : 2 * MM], 0, b3, range(PASSES))
+        quantize(codes_last, exp_last, bf_c, c1, c2, B_END)
+        slot_product(y0[:, 2 * MM :], 0, c1, range(PASSES))
+        leave(y0, 0, b2, c2)
+        quantize_held(late["codes_tail"], MID + 512, MID + 768, MID)
+        slot_product(z0[:], 0, c2, range(last))
+        quantize(codes_last, exp_last, bf_c, c2, S, B_END)
+        slot_product(z0[:], 0, c2, (last,))
+        leave(z0, 0, c2, S)
         late["d_codes", 1] = keep.tile([P, half_words], U32, name="d_codes1", tag="chain", align_bytes=64)
         for w0, w1 in spans((256, 512)):
             quantize_tokens(1, w0, w1)
-        held = psum_end.tile([P, BANK], F32, name="held", tag="pair0")
-        slot_product(a2_second[:, A2 - A1 :], 1, S - MM, range(PASSES))
-        slot_sums(1, A2, S - MM, held)
-        nc.scalar.copy(out=dx[1][:, A1:A2], in_=a2_second[:, : A2 - A1])
-        nc.scalar.copy(out=dx[1][:, S - MM :], in_=a2_second[:, A2 - A1 :])
-        leave(held, 1, A2, S - MM)
+        slot_product(x1[:], 1, b1, (last,))
+        leave(x1, 1, b1, b2)
+        slot_product(y1[:], 1, b2, (last,))
+        leave(y1, 1, b2, b3)
+        held = psum_end.tile([P, 3 * MM], F32, name="held", tag="x0")
+        leave(slot_sums(1, b3, S, held), 1, b3, S)
         for h in range(K // P):
             acc = psum.tile([P, HALF], F32, name="acc")
             shared_products(acc[:], h, 1)
@@ -275,13 +283,13 @@ def tile_moe_bds_lin_none_kernel(tc, dyT, w_words, w_scales, gate, offs, pos1, p
             if r == 2:
                 nc.sync.dma_start(out=out[P * h : P * (h + 1), t0:t1], in_=totals[h][r][:, t0:t1])
 
-        for r in range(2):
-            for t0, t1 in spans((MM, MM)):
-                combine(0, r, t0, t1)
+        for t0, t1 in spans((MM, MM)):
+            combine(0, 0, t0, t1)
+        combine(0, 1, 0, MM)
         combine(1, 0, 0, HALF)
         for h in range(K // P):
             combine(h, 0, HALF, T)
-        combine(0, 1, HALF, T)
+        combine(0, 1, MM, T)
         combine(1, 1, 0, T)
         combine(0, 2, 0, T)
         for t0, t1 in spans(TAIL_CUTS):

@@ -24,7 +24,7 @@ ADD = mybir.AluOpType.add
 
 HALF = T // 2
 BANK = 512
-HEAD_CUTS = (128, 256, 448, 704)
+HEAD_CUTS = (128, 192, 288, 416, 512)
 ROW_ORDER = (1, 2, 3, 0)
 A1, A2, B_END = 512, 896, 1280
 TAIL_CUTS = (256, 128, 128)

@@ -23,10 +23,12 @@ MULT = mybir.AluOpType.mult
 ADD = mybir.AluOpType.add
 
 HALF = T // 2
-BANK = 512
+LAST = PASSES - 1
 HEAD_CUTS = (128, 192, 288, 416, 512)
 ROW_ORDER = (1, 2, 3, 0)
-A1, A2, B_END = 512, 896, 1280
+FRONT, MIDDLE = 896, 1280
+FRONT_CUTS = (512, 128, 256)
+BANK = FRONT_CUTS[0]
 TAIL_CUTS = (256, 128, 128)
 
 
@@ -55,14 +57,13 @@ def tile_moe_bds_lin_none_kernel(tc, dyT, w_words, w_scales, gate, offs, pos1, p
         w_exp = keep.tile([P, (E + 1) * PASSES, K], U8, name="w_exp", align_bytes=64)
         nc.vector.memset(w_exp[:].rearrange("p g k -> p (g k)").bitcast(I32), 0)
 
-        last = PASSES - 1
         gates = keep.tile([P, S], F32, name="gates")
         dy_all = [keep.tile([P, PACK * T], F32, name="dy_all%d" % a) for a in range(PASSES)]
         window = {}
         for a in range(PASSES):
             window[a, 0] = dy_all[a]
             for j in range(1, PACK):
-                window[a, j] = keep.tile([P, (S if a < last else A2) + 16], F32, name="window%d_%d" % (a, j), tag="window%d_%d" % (a, j), align_bytes=64)
+                window[a, j] = keep.tile([P, (S if a < LAST else FRONT) + 16], F32, name="window%d_%d" % (a, j), tag="window%d_%d" % (a, j), align_bytes=64)
 
         for a in range(PASSES):
             for j in range(1, PACK):
@@ -82,18 +83,16 @@ def tile_moe_bds_lin_none_kernel(tc, dyT, w_words, w_scales, gate, offs, pos1, p
         for r, src in enumerate((pos1, pos2, pos3)):
             nc.sync.dma_start(token_slot[r][:], src)
 
-        TAIL = S - B_END
-        HELD = A2
-        NH = S - HELD
-        MID = 4 * MM
-        ga = over.tile([P, PACK * S], F32, name="ga", align_bytes=64, offset=0)
-        gb = keep.tile([P, PACK * S], F32, name="gb", tag="gb", align_bytes=64)
-        bf_main = keep.tile([P, last * HELD * PACK], BF16, name="bf_main", align_bytes=64)
-        bf_tail = keep.tile([P, last * NH * PACK], BF16, name="bf_tail", align_bytes=64)
-        codes_main = keep.tile([P, last * HELD], U32, name="codes_main", align_bytes=64)
-        exp_main = keep.tile([P, last * HELD], U8, name="exp_main", align_bytes=64)
-        exp_tail = keep.tile([P, last * NH], U8, name="exp_tail", align_bytes=64)
-        codes_a = keep.tile([P, A2], U32, name="codes_a", tag="codes_a", align_bytes=64)
+        rest = S - FRONT
+        opened = 2 * LAST * MM
+        gather_a = over.tile([P, PACK * S], F32, name="gather_a", align_bytes=64, offset=0)
+        gather_b = keep.tile([P, PACK * S], F32, name="gather_b", tag="gather_b", align_bytes=64)
+        bf_front = keep.tile([P, LAST * FRONT * PACK], BF16, name="bf_front", tag="bf_front", align_bytes=64)
+        bf_rest = keep.tile([P, LAST * rest * PACK], BF16, name="bf_rest", align_bytes=64)
+        codes_front = keep.tile([P, LAST * FRONT], U32, name="codes_front", align_bytes=64)
+        exp_front = keep.tile([P, LAST * FRONT], U8, name="exp_front", align_bytes=64)
+        exp_rest = keep.tile([P, LAST * rest], U8, name="exp_rest", align_bytes=64)
+        codes_bank = keep.tile([P, BANK], U32, name="codes_bank", tag="codes_bank", align_bytes=64)
         codes_last = keep.tile([P, S], U32, name="codes_last", align_bytes=64)
         exp_last = keep.tile([P, S], U8, name="exp_last", align_bytes=64)
         d_exp = keep.tile([P, PASSES * T], U8, name="d_exp", align_bytes=64)
@@ -102,15 +101,15 @@ def tile_moe_bds_lin_none_kernel(tc, dyT, w_words, w_scales, gate, offs, pos1, p
         late = {}
 
         def slot_operand(a, m0):
-            if a == last:
-                return (codes_a if m0 < A2 else codes_last)[:, m0 : m0 + MM], exp_last[:, m0 : m0 + MM]
-            if m0 < HELD:
-                w = a * HELD + m0
-                return codes_main[:, w : w + MM], exp_main[:, w : w + MM]
-            w = ((m0 - HELD) // MM * last + a) * MM
-            if w < MID:
-                return late["codes_mid"][:, w : w + MM], exp_tail[:, w : w + MM]
-            return late["codes_tail"][:, w - MID : w - MID + MM], exp_tail[:, w : w + MM]
+            if a == LAST:
+                return (codes_bank if m0 < BANK else codes_last)[:, m0 : m0 + MM], exp_last[:, m0 : m0 + MM]
+            if m0 < FRONT:
+                w = a * FRONT + m0
+                return codes_front[:, w : w + MM], exp_front[:, w : w + MM]
+            w = ((m0 - FRONT) // MM * LAST + a) * MM
+            if w < opened:
+                return late["opened"][:, w : w + MM], exp_rest[:, w : w + MM]
+            return late["held"][:, w - opened : w - opened + MM], exp_rest[:, w : w + MM]
 
         def product(acc, e, h, operand, passes):
             for a in passes:
@@ -123,18 +122,15 @@ def tile_moe_bds_lin_none_kernel(tc, dyT, w_words, w_scales, gate, offs, pos1, p
                     rhs=codes.bitcast(FP8X4),
                     rhs_scale=exps,
                     start=(a == 0),
-                    stop=(a == last),
+                    stop=(a == LAST),
                 )
 
         def slot_product(acc, h, m0, passes):
             product(acc, m0 // C, h, lambda a: slot_operand(a, m0), passes)
 
-        def slot_sums(h, b0, b1, acc=None):
-            if acc is None:
-                acc = psum.tile([P, b1 - b0], F32, name="acc")
+        def slot_sums(acc, h, b0, b1):
             for m0 in range(b0, b1, MM):
                 slot_product(acc[:, m0 - b0 : m0 - b0 + MM], h, m0, range(PASSES))
-            return acc
 
         def leave(acc, h, b0, b1):
             nc.scalar.copy(out=dx[h][:, b0:b1], in_=acc[:])
@@ -152,6 +148,9 @@ def tile_moe_bds_lin_none_kernel(tc, dyT, w_words, w_scales, gate, offs, pos1, p
         def quantize(codes, exps, g_bf, w0, w1, first=0):
             nc.vector.quantize_mx(out=codes[:, w0:w1].bitcast(FP8X4), scales=exps[:, w0:w1], in_=g_bf[:, (w0 - first) * PACK : (w1 - first) * PACK])
 
+        def quantize_rest(codes, w0, w1, first):
+            nc.vector.quantize_mx(out=codes[:, w0 - first : w1 - first].bitcast(FP8X4), scales=exp_rest[:, w0:w1], in_=bf_rest[:, w0 * PACK : w1 * PACK])
+
         def round_tokens(a):
             nc.scalar.copy(
                 out=d_bf[:].rearrange("p (q a c i j) -> p q a c j i", a=PASSES, c=MM // 4, i=4, j=PACK)[:, :, a],
@@ -160,118 +159,126 @@ def tile_moe_bds_lin_none_kernel(tc, dyT, w_words, w_scales, gate, offs, pos1, p
 
         half_words = PASSES * HALF
 
-        def quantize_tokens(u, w0, w1):
+        def quantize_tokens(u):
             first = u * half_words
-            nc.vector.quantize_mx(out=late["d_codes", u][:, w0:w1].bitcast(FP8X4), scales=d_exp[:, first + w0 : first + w1], in_=d_bf[:, (first + w0) * PACK : (first + w1) * PACK])
+            for w0, w1 in spans((2 * MM, 4 * MM)):
+                nc.vector.quantize_mx(out=late["tokens", u][:, w0:w1].bitcast(FP8X4), scales=d_exp[:, first + w0 : first + w1], in_=d_bf[:, (first + w0) * PACK : (first + w1) * PACK])
 
-        def shared_products(acc, h, u):
+        def shared_sums(acc, h, u):
             for i in range(HALF // MM):
                 def operand(a):
                     w = (i * PASSES + a) * MM
-                    return late["d_codes", u][:, w : w + MM], d_exp[:, u * half_words + w : u * half_words + w + MM]
+                    return late["tokens", u][:, w : w + MM], d_exp[:, u * half_words + w : u * half_words + w + MM]
                 product(acc[:, i * MM : (i + 1) * MM], E, h, operand, range(PASSES))
 
-        for a, tile in enumerate((ga, gb)):
+        for a, tile in enumerate((gather_a, gather_b)):
             rows = tile[:].rearrange("p (j c) -> p j c", j=PACK)
             for j in ROW_ORDER:
                 for c0, c1 in spans(HEAD_CUTS if (a, j) == (0, ROW_ORDER[0]) else (S,)):
                     gather(rows, a, j, c0, c1, 0)
             if a == 0:
                 round_tokens(0)
-            round_slots(bf_main[:, a * HELD * PACK : (a + 1) * HELD * PACK], rows[:, :, :HELD])
+            round_slots(bf_front[:, a * FRONT * PACK : (a + 1) * FRONT * PACK], rows[:, :, :FRONT])
             nc.scalar.copy(
-                out=bf_tail[:].rearrange("p (m a c i j) -> p m a c j i", a=last, c=MM // 4, i=4, j=PACK)[:, :, a],
-                in_=rows[:, :, HELD:].rearrange("p j (m c i) -> p m c j i", c=MM // 4, i=4),
+                out=bf_rest[:].rearrange("p (m a c i j) -> p m a c j i", a=LAST, c=MM // 4, i=4, j=PACK)[:, :, a],
+                in_=rows[:, :, FRONT:].rearrange("p j (m c i) -> p m c j i", c=MM // 4, i=4),
             )
             if a == 0:
                 round_tokens(1)
                 round_tokens(2)
 
-        rows_a = ga[:, : PACK * A2].rearrange("p (j c) -> p j c", j=PACK)
+        rows_front = gather_a[:, : PACK * FRONT].rearrange("p (j c) -> p j c", j=PACK)
         for j in ROW_ORDER:
-            gather(rows_a, last, j, 0, A2, 0)
-        rows_b = ga[:, 256 : 256 + PACK * 1024].rearrange("p (j c) -> p j c", j=PACK)[:, :, : B_END - A2]
-        total_tile = keep.tile([P, 8 * T], F32, name="totals", tag="gb", align_bytes=64)
+            gather(rows_front, LAST, j, 0, FRONT, 0)
+        rows_middle = gather_a[:, 256 : 256 + PACK * 1024].rearrange("p (j c) -> p j c", j=PACK)[:, :, : MIDDLE - FRONT]
+        total_tile = keep.tile([P, 8 * T], F32, name="totals", tag="gather_b", align_bytes=64)
         ds_sb = [total_tile[:, (6 + h) * T : (7 + h) * T] for h in range(K // P)]
-        late["d_codes", 0] = keep.tile([P, half_words], U32, name="d_codes0", align_bytes=64)
-        for w0, w1 in spans((256, 512)):
-            quantize_tokens(0, w0, w1)
+
+        for w0, w1 in spans((1024, 512, 256)):
+            quantize(codes_front, exp_front, bf_front, w0, w1)
+        late["tokens", 0] = keep.tile([P, half_words], U32, name="d_codes0", tag="bf_front", align_bytes=64)
+        quantize_tokens(0)
         early = psum.tile([P, 2 * HALF], F32, name="acc")
         for h in range(K // P):
-            shared_products(early[:, h * HALF : (h + 1) * HALF], h, 0)
-        for w0, w1 in spans((1024, 512, 256)):
-            quantize(codes_main, exp_main, bf_main, w0, w1)
+            shared_sums(early[:, h * HALF : (h + 1) * HALF], h, 0)
 
-        bf_a = keep.tile([P, A2 * PACK], BF16, name="bf_a", tag="chain", align_bytes=64)
-        for i, (c0, c1) in enumerate(spans((512, 128, 256))):
-            round_slots(bf_a[:, c0 * PACK : c1 * PACK], rows_a[:, :, c0:c1])
-            quantize(codes_a, exp_last, bf_a, c0, c1)
+        bf_a = keep.tile([P, FRONT * PACK], BF16, name="bf_a", tag="chain", align_bytes=64)
+        for i, (c0, c1) in enumerate(spans(FRONT_CUTS)):
+            round_slots(bf_a[:, c0 * PACK : c1 * PACK], rows_front[:, :, c0:c1])
+            quantize(codes_bank if c0 < BANK else codes_last, exp_last, bf_a, c0, c1)
             if i == 1:
-                gather(rows_b, last, 0, A2, B_END, A2)
+                gather(rows_middle, LAST, 0, FRONT, MIDDLE, FRONT)
         nc.scalar.copy(
             out=total_tile[:, 6 * T :].rearrange("p (h t) -> p h t", h=2)[:, :, :HALF],
             in_=early[:].rearrange("p (h t) -> p h t", h=2),
         )
-        for j in (1, 2, 3):
-            gather(rows_b, last, j, A2, B_END, A2)
-        for b0, b1 in ((0, A1), (A1, A2)):
-            for h in range(K // P):
-                leave(slot_sums(h, b0, b1), h, b0, b1)
+        for j in range(1, PACK):
+            gather(rows_middle, LAST, j, FRONT, MIDDLE, FRONT)
+        for h in range(K // P):
+            acc = psum.tile([P, BANK], F32, name="acc")
+            slot_sums(acc, h, 0, BANK)
+            leave(acc, h, 0, BANK)
+        second = []
+        for h in range(K // P):
+            acc = psum.tile([P, FRONT - BANK], F32, name="acc")
+            slot_sums(acc, h, BANK, FRONT)
+            second.append(acc)
 
-        def quantize_held(codes, w0, w1, first):
-            nc.vector.quantize_mx(out=codes[:, w0 - first : w1 - first].bitcast(FP8X4), scales=exp_tail[:, w0:w1], in_=bf_tail[:, w0 * PACK : w1 * PACK])
-
-        gc = keep.tile([P, PACK * TAIL], F32, name="gc", tag="chain", align_bytes=64)
-        rows_c = gc[:].rearrange("p (j c) -> p j c", j=PACK)
+        gather_c = keep.tile([P, PACK * (S - MIDDLE)], F32, name="gather_c", tag="chain", align_bytes=64)
+        rows_back = gather_c[:].rearrange("p (j c) -> p j c", j=PACK)
         for j in ROW_ORDER:
-            gather(rows_c, last, j, B_END, S, B_END)
+            gather(rows_back, LAST, j, MIDDLE, S, MIDDLE)
             if j == ROW_ORDER[1]:
-                late["codes_mid"] = keep.tile([P, MID], U32, name="codes_mid", tag="window%d_%d" % (last, ROW_ORDER[0]), align_bytes=64)
-                quantize_held(late["codes_mid"], 0, MID, 0)
-        b1, b2, b3, c1, c2 = range(A2, S, MM)
-        x0 = psum_end.tile([P, MM], F32, name="x0", tag="x0")
-        y0 = psum_end.tile([P, 3 * MM], F32, name="y0")
-        z0 = psum_end.tile([P, MM], F32, name="z0")
-        x1 = psum_end.tile([P, MM], F32, name="x1")
-        y1 = psum_end.tile([P, MM], F32, name="y1")
-        slot_product(x0[:], 0, b1, range(last))
-        slot_product(y0[:, :MM], 0, b2, range(last))
-        slot_product(x1[:], 1, b1, range(last))
-        slot_product(y1[:], 1, b2, range(last))
+                late["opened"] = keep.tile([P, opened], U32, name="codes_opened", tag="window%d_%d" % (LAST, ROW_ORDER[0]), align_bytes=64)
+                quantize_rest(late["opened"], 0, opened, 0)
+        m1, m2, m3, m4, m5 = range(FRONT, S, MM)
+        sum0_m1 = psum_end.tile([P, MM], F32, name="sum0_m1", tag="sum0_m1")
+        sum0_m234 = psum_end.tile([P, 3 * MM], F32, name="sum0_m234")
+        sum0_m5 = psum_end.tile([P, MM], F32, name="sum0_m5")
+        sum1_m1 = psum_end.tile([P, MM], F32, name="sum1_m1")
+        sum1_m2 = psum_end.tile([P, MM], F32, name="sum1_m2")
+        slot_product(sum0_m1[:], 0, m1, range(LAST))
+        slot_product(sum0_m234[:, :MM], 0, m2, range(LAST))
+        slot_product(sum1_m1[:], 1, m1, range(LAST))
+        slot_product(sum1_m2[:], 1, m2, range(LAST))
 
-        bf_b = keep.tile([P, (B_END - A2) * PACK], BF16, name="bf_b", tag="codes_a", align_bytes=64)
-        round_slots(bf_b[:], rows_b)
-        bf_c = over.tile([P, TAIL * PACK], BF16, name="bf_c", align_bytes=64, offset=4096)
+        bf_b = keep.tile([P, (MIDDLE - FRONT) * PACK], BF16, name="bf_b", tag="codes_bank", align_bytes=64)
+        round_slots(bf_b[:], rows_middle)
+        for h in range(K // P):
+            leave(second[h], h, BANK, FRONT)
+        bf_c = over.tile([P, (S - MIDDLE) * PACK], BF16, name="bf_c", align_bytes=64, offset=4096)
         for u0, u1 in spans((MM, MM)):
-            round_slots(bf_c[:, u0 * PACK : u1 * PACK], rows_c[:, :, u0:u1])
-        quantize(codes_last, exp_last, bf_b, b1, b3, A2)
-        slot_product(x0[:], 0, b1, (last,))
-        leave(x0, 0, b1, b2)
-        slot_product(y0[:, :MM], 0, b2, (last,))
-        quantize(codes_last, exp_last, bf_b, b3, c1, A2)
-        late["codes_tail"] = over.tile([P, last * NH - MID], U32, name="codes_tail", align_bytes=64, offset=0)
-        quantize_held(late["codes_tail"], MID, MID + 512, MID)
-        slot_product(y0[:, MM : 2 * MM], 0, b3, range(PASSES))
-        quantize(codes_last, exp_last, bf_c, c1, c2, B_END)
-        slot_product(y0[:, 2 * MM :], 0, c1, range(PASSES))
-        leave(y0, 0, b2, c2)
-        quantize_held(late["codes_tail"], MID + 512, MID + 768, MID)
-        slot_product(z0[:], 0, c2, range(last))
-        quantize(codes_last, exp_last, bf_c, c2, S, B_END)
-        slot_product(z0[:], 0, c2, (last,))
-        leave(z0, 0, c2, S)
-        late["d_codes", 1] = keep.tile([P, half_words], U32, name="d_codes1", tag="chain", align_bytes=64)
-        for w0, w1 in spans((256, 512)):
-            quantize_tokens(1, w0, w1)
-        slot_product(x1[:], 1, b1, (last,))
-        leave(x1, 1, b1, b2)
-        slot_product(y1[:], 1, b2, (last,))
-        leave(y1, 1, b2, b3)
-        held = psum_end.tile([P, 3 * MM], F32, name="held", tag="x0")
-        leave(slot_sums(1, b3, S, held), 1, b3, S)
+            round_slots(bf_c[:, u0 * PACK : u1 * PACK], rows_back[:, :, u0:u1])
+
+        quantize(codes_last, exp_last, bf_b, m1, m3, FRONT)
+        slot_product(sum0_m1[:], 0, m1, (LAST,))
+        leave(sum0_m1, 0, m1, m2)
+        slot_product(sum0_m234[:, :MM], 0, m2, (LAST,))
+        quantize(codes_last, exp_last, bf_b, m3, m4, FRONT)
+        late["held"] = over.tile([P, LAST * rest - opened], U32, name="codes_held", align_bytes=64, offset=0)
+        quantize_rest(late["held"], opened, opened + 2 * LAST * MM, opened)
+        slot_product(sum0_m234[:, MM : 2 * MM], 0, m3, range(PASSES))
+        quantize(codes_last, exp_last, bf_c, m4, m5, MIDDLE)
+        slot_product(sum0_m234[:, 2 * MM :], 0, m4, range(PASSES))
+        leave(sum0_m234, 0, m2, m5)
+        quantize_rest(late["held"], opened + 2 * LAST * MM, LAST * rest, opened)
+        slot_product(sum0_m5[:], 0, m5, range(LAST))
+        quantize(codes_last, exp_last, bf_c, m5, S, MIDDLE)
+        slot_product(sum0_m5[:], 0, m5, (LAST,))
+        leave(sum0_m5, 0, m5, S)
+
+        late["tokens", 1] = keep.tile([P, half_words], U32, name="d_codes1", tag="chain", align_bytes=64)
+        quantize_tokens(1)
+        slot_product(sum1_m1[:], 1, m1, (LAST,))
+        leave(sum1_m1, 1, m1, m2)
+        slot_product(sum1_m2[:], 1, m2, (LAST,))
+        leave(sum1_m2, 1, m2, m3)
+        sum1_m345 = psum_end.tile([P, 3 * MM], F32, name="sum1_m345", tag="sum0_m1")
+        slot_sums(sum1_m345, 1, m3, S)
+        leave(sum1_m345, 1, m3, S)
         for h in range(K // P):
             acc = psum.tile([P, HALF], F32, name="acc")
-            shared_products(acc[:], h, 1)
+            shared_sums(acc[:], h, 1)
             nc.scalar.copy(out=ds_sb[h][:, HALF:], in_=acc[:])
 
         totals = [[total_tile[:, (3 * h + r) * T : (3 * h + r + 1) * T] for r in range(3)] for h in range(K // P)]

@@ -87,7 +87,7 @@ def tile_moe_bds_lin_none_kernel(tc, dyT, w_words, w_scales, gate, offs, pos1, p
         opened = 2 * LAST * MM
         gather_a = over.tile([P, PACK * S], F32, name="gather_a", align_bytes=64, offset=0)
         gather_b = keep.tile([P, PACK * S], F32, name="gather_b", tag="gather_b", align_bytes=64)
-        bf_front = keep.tile([P, LAST * FRONT * PACK], BF16, name="bf_front", tag="bf_front", align_bytes=64)
+        bf_front = keep.tile([P, LAST * FRONT * PACK], BF16, name="bf_front", align_bytes=64)
         bf_rest = keep.tile([P, LAST * rest * PACK], BF16, name="bf_rest", align_bytes=64)
         codes_front = keep.tile([P, LAST * FRONT], U32, name="codes_front", align_bytes=64)
         exp_front = keep.tile([P, LAST * FRONT], U8, name="exp_front", align_bytes=64)
@@ -191,16 +191,15 @@ def tile_moe_bds_lin_none_kernel(tc, dyT, w_words, w_scales, gate, offs, pos1, p
         for j in ROW_ORDER:
             gather(rows_front, LAST, j, 0, FRONT, 0)
         rows_middle = gather_a[:, 256 : 256 + PACK * 1024].rearrange("p (j c) -> p j c", j=PACK)[:, :, : MIDDLE - FRONT]
-        total_tile = keep.tile([P, 8 * T], F32, name="totals", tag="gather_b", align_bytes=64)
-        ds_sb = [total_tile[:, (6 + h) * T : (7 + h) * T] for h in range(K // P)]
-
         for w0, w1 in spans((1024, 512, 256)):
             quantize(codes_front, exp_front, bf_front, w0, w1)
-        late["tokens", 0] = keep.tile([P, half_words], U32, name="d_codes0", tag="bf_front", align_bytes=64)
+        late["tokens", 0] = keep.tile([P, half_words], U32, name="d_codes0", tag="gather_b", align_bytes=64)
         quantize_tokens(0)
         early = psum.tile([P, 2 * HALF], F32, name="acc")
         for h in range(K // P):
             shared_sums(early[:, h * HALF : (h + 1) * HALF], h, 0)
+        total_tile = keep.tile([P, 8 * T], F32, name="totals", tag="gather_b", align_bytes=64)
+        ds_sb = [total_tile[:, (6 + h) * T : (7 + h) * T] for h in range(K // P)]
 
         bf_a = keep.tile([P, FRONT * PACK], BF16, name="bf_a", tag="chain", align_bytes=64)
         for i, (c0, c1) in enumerate(spans(FRONT_CUTS)):

@@ -86,7 +86,8 @@ def tile_moe_bds_lin_none_kernel(tc, dyT, w_words, w_scales, gate, offs, pos1, p
         rest = S - FRONT
         opened = 2 * LAST * MM
         gather_a = over.tile([P, PACK * S], F32, name="gather_a", align_bytes=64, offset=0)
-        gather_b = keep.tile([P, PACK * S], F32, name="gather_b", tag="gather_b", align_bytes=64)
+        gather_bytes = PACK * S * 4
+        gather_b = over.tile([P, PACK * S], F32, name="gather_b", align_bytes=64, offset=gather_bytes)
         bf_front = keep.tile([P, LAST * FRONT * PACK], BF16, name="bf_front", align_bytes=64)
         bf_rest = keep.tile([P, LAST * rest * PACK], BF16, name="bf_rest", align_bytes=64)
         codes_front = keep.tile([P, LAST * FRONT], U32, name="codes_front", align_bytes=64)
@@ -157,19 +158,25 @@ def tile_moe_bds_lin_none_kernel(tc, dyT, w_words, w_scales, gate, offs, pos1, p
                 in_=dy_all[a][:].rearrange("p (j q c i) -> p q c j i", j=PACK, c=MM // 4, i=4),
             )
 
-        half_words = PASSES * HALF
+        ahead = 4 * MM
 
-        def quantize_tokens(u):
-            first = u * half_words
-            for w0, w1 in spans((2 * MM, 4 * MM)):
-                nc.vector.quantize_mx(out=late["tokens", u][:, w0:w1].bitcast(FP8X4), scales=d_exp[:, first + w0 : first + w1], in_=d_bf[:, (first + w0) * PACK : (first + w1) * PACK])
+        def token_codes(w0, w1):
+            return late["ahead"][:, w0:w1] if w0 < ahead else late["behind"][:, w0 - ahead : w1 - ahead]
 
-        def shared_sums(acc, h, u):
-            for i in range(HALF // MM):
+        def quantize_tokens(w0, w1):
+            nc.vector.quantize_mx(out=token_codes(w0, w1).bitcast(FP8X4), scales=d_exp[:, w0:w1], in_=d_bf[:, w0 * PACK : w1 * PACK])
+
+        def shared_products(acc, h, quarters):
+            for i, q in enumerate(quarters):
                 def operand(a):
-                    w = (i * PASSES + a) * MM
-                    return late["tokens", u][:, w : w + MM], d_exp[:, u * half_words + w : u * half_words + w + MM]
+                    w = (q * PASSES + a) * MM
+                    return token_codes(w, w + MM), d_exp[:, w : w + MM]
                 product(acc[:, i * MM : (i + 1) * MM], E, h, operand, range(PASSES))
+
+        def shared_sums(h, quarters):
+            acc = psum.tile([P, MM * len(quarters)], F32, name="acc")
+            shared_products(acc[:], h, quarters)
+            nc.scalar.copy(out=ds_sb[h][:, quarters[0] * MM : (quarters[-1] + 1) * MM], in_=acc[:])
 
         for a, tile in enumerate((gather_a, gather_b)):
             rows = tile[:].rearrange("p (j c) -> p j c", j=PACK)
@@ -193,12 +200,12 @@ def tile_moe_bds_lin_none_kernel(tc, dyT, w_words, w_scales, gate, offs, pos1, p
         rows_middle = gather_a[:, 256 : 256 + PACK * 1024].rearrange("p (j c) -> p j c", j=PACK)[:, :, : MIDDLE - FRONT]
         for w0, w1 in spans((1024, 512, 256)):
             quantize(codes_front, exp_front, bf_front, w0, w1)
-        late["tokens", 0] = keep.tile([P, half_words], U32, name="d_codes0", tag="gather_b", align_bytes=64)
-        quantize_tokens(0)
-        early = psum.tile([P, 2 * HALF], F32, name="acc")
+        late["ahead"] = over.tile([P, ahead], U32, name="d_codes0", align_bytes=64, offset=gather_bytes)
+        quantize_tokens(0, ahead)
+        early = psum.tile([P, 2 * MM], F32, name="acc")
         for h in range(K // P):
-            shared_sums(early[:, h * HALF : (h + 1) * HALF], h, 0)
-        total_tile = keep.tile([P, 8 * T], F32, name="totals", tag="gather_b", align_bytes=64)
+            shared_products(early[:, h * MM : (h + 1) * MM], h, (0,))
+        total_tile = over.tile([P, 8 * T], F32, name="totals", align_bytes=64, offset=gather_bytes + 4 * ahead)
         ds_sb = [total_tile[:, (6 + h) * T : (7 + h) * T] for h in range(K // P)]
 
         bf_a = keep.tile([P, FRONT * PACK], BF16, name="bf_a", tag="chain", align_bytes=64)
@@ -208,7 +215,7 @@ def tile_moe_bds_lin_none_kernel(tc, dyT, w_words, w_scales, gate, offs, pos1, p
             if i == 1:
                 gather(rows_middle, LAST, 0, FRONT, MIDDLE, FRONT)
         nc.scalar.copy(
-            out=total_tile[:, 6 * T :].rearrange("p (h t) -> p h t", h=2)[:, :, :HALF],
+            out=total_tile[:, 6 * T :].rearrange("p (h t) -> p h t", h=2)[:, :, :MM],
             in_=early[:].rearrange("p (h t) -> p h t", h=2),
         )
         for j in range(1, PACK):
@@ -266,8 +273,11 @@ def tile_moe_bds_lin_none_kernel(tc, dyT, w_words, w_scales, gate, offs, pos1, p
         slot_product(sum0_m5[:], 0, m5, (LAST,))
         leave(sum0_m5, 0, m5, S)
 
-        late["tokens", 1] = keep.tile([P, half_words], U32, name="d_codes1", tag="chain", align_bytes=64)
-        quantize_tokens(1)
+        late["behind"] = keep.tile([P, PASSES * T - ahead], U32, name="d_codes1", tag="chain", align_bytes=64)
+        quantize_tokens(ahead, PASSES * HALF)
+        shared_sums(0, (1,))
+        for w0, w1 in spans((2 * MM, 4 * MM), PASSES * HALF):
+            quantize_tokens(w0, w1)
         slot_product(sum1_m1[:], 1, m1, (LAST,))
         leave(sum1_m1, 1, m1, m2)
         slot_product(sum1_m2[:], 1, m2, (LAST,))
@@ -275,10 +285,9 @@ def tile_moe_bds_lin_none_kernel(tc, dyT, w_words, w_scales, gate, offs, pos1, p
         sum1_m345 = psum_end.tile([P, 3 * MM], F32, name="sum1_m345", tag="sum0_m1")
         slot_sums(sum1_m345, 1, m3, S)
         leave(sum1_m345, 1, m3, S)
+        shared_sums(1, (1,))
         for h in range(K // P):
-            acc = psum.tile([P, HALF], F32, name="acc")
-            shared_sums(acc[:], h, 1)
-            nc.scalar.copy(out=ds_sb[h][:, HALF:], in_=acc[:])
+            shared_sums(h, (2, 3))
 
         totals = [[total_tile[:, (3 * h + r) * T : (3 * h + r + 1) * T] for r in range(3)] for h in range(K // P)]
 
@@ -289,13 +298,13 @@ def tile_moe_bds_lin_none_kernel(tc, dyT, w_words, w_scales, gate, offs, pos1, p
             if r == 2:
                 nc.sync.dma_start(out=out[P * h : P * (h + 1), t0:t1], in_=totals[h][r][:, t0:t1])
 
-        for t0, t1 in spans((MM, MM)):
-            combine(0, 0, t0, t1)
-        combine(0, 1, 0, MM)
+        for r in range(2):
+            for t0, t1 in spans((MM, MM)):
+                combine(0, r, t0, t1)
         combine(1, 0, 0, HALF)
         for h in range(K // P):
             combine(h, 0, HALF, T)
-        combine(0, 1, MM, T)
+        combine(0, 1, HALF, T)
         combine(1, 1, 0, T)
         combine(0, 2, 0, T)
         for t0, t1 in spans(TAIL_CUTS):

@@ -7,7 +7,6 @@ S = E * C
 P = 128
 PACK = 4
 PASSES = N // (P * PACK)
-MM = 128
 FLOPS = 2 * K * N * (S + T)
 BYTES = N * T * 4 + (E + 1) * PASSES * (P * 512 + 16 * K) + P * S * 4 + P * (S + 3 * T) // 16 * 2 + K * T * 4
 
@@ -21,23 +20,14 @@ FP8X4 = mybir.dt.float8_e4m3fn_x4
 FP4X4 = mybir.dt.float4_e2m1fn_x4
 MULT = mybir.AluOpType.mult
 ADD = mybir.AluOpType.add
+COPY = mybir.ActivationFunctionType.Copy
 
 HALF = T // 2
 LAST = PASSES - 1
-HEAD_CUTS = (128, 192, 288, 416, 512)
-ROW_ORDER = (1, 2, 3, 0)
-FRONT, MIDDLE = 896, 1280
-FRONT_CUTS = (512, 128, 256)
-BANK = FRONT_CUTS[0]
-TAIL_CUTS = (256, 128, 128)
-
-
-def spans(widths, first=0):
-    res = []
-    for w in widths:
-        res.append((first, first + w))
-        first += w
-    return res
+HALVES = K // P
+RUN = 2
+OWN = E - 1
+END = E - 2
 
 
 def tile_moe_bds_lin_none_kernel(tc, dyT, w_words, w_scales, gate, offs, pos1, pos2, pos3, out):
@@ -45,9 +35,8 @@ def tile_moe_bds_lin_none_kernel(tc, dyT, w_words, w_scales, gate, offs, pos1, p
     with ExitStack() as ctx:
         lists = ctx.enter_context(tc.tile_pool(name="lists", bufs=1))
         keep = ctx.enter_context(tc.tile_pool(name="keep", bufs=1))
-        over = ctx.enter_context(tc.tile_pool(name="over", bufs=1))
-        psum = ctx.enter_context(tc.psum_pool(name="psum", bufs=3))
-        psum_end = ctx.enter_context(tc.psum_pool(name="psum_end", bufs=1))
+        ring = ctx.enter_context(tc.tile_pool(name="ring", bufs=3))
+        psum = ctx.enter_context(tc.psum_pool(name="psum", bufs=1))
 
         slot_token = lists.tile([P, S // 16], U16, name="slot_token")
         token_slot = [lists.tile([P, T // 16], U16, name="token_slot%d" % r) for r in range(3)]
@@ -61,18 +50,25 @@ def tile_moe_bds_lin_none_kernel(tc, dyT, w_words, w_scales, gate, offs, pos1, p
         dy_all = [keep.tile([P, PACK * T], F32, name="dy_all%d" % a) for a in range(PASSES)]
         window = {}
         for a in range(PASSES):
-            window[a, 0] = dy_all[a]
-            for j in range(1, PACK):
-                window[a, j] = keep.tile([P, (S if a < LAST else FRONT) + 16], F32, name="window%d_%d" % (a, j), tag="window%d_%d" % (a, j), align_bytes=64)
+            for j in range(PACK):
+                window[a, j] = keep.tile([P, T + 16], F32, name="window%d_%d" % (a, j))
 
-        for a in range(PASSES):
-            for j in range(1, PACK):
-                nc.sync.dma_start(out=window[a, j][:, 0:T], in_=dy_rows[a, :, j, :])
-                if (a, j) == (0, ROW_ORDER[0]):
-                    nc.sync.dma_start(slot_token[:], offs)
-                    for c0, c1 in spans(HEAD_CUTS):
-                        nc.sync.dma_start(out=gates[:, c0:c1], in_=gate[0:P, c0:c1])
+        def load_gates(c0, c1):
+            nc.sync.dma_start(out=gates[:, c0:c1], in_=gate[0:P, c0:c1])
+
+        def load_tokens(a):
             nc.sync.dma_start(out=dy_all[a][:], in_=dy_rows[a].rearrange("p j t -> p (j t)"))
+
+        nc.sync.dma_start(slot_token[:], offs)
+        for a in range(PASSES):
+            for j in range(PACK):
+                nc.sync.dma_start(out=window[a, j][:, 0:T], in_=dy_rows[a, :, j, :])
+                if (a, j) == (0, 0):
+                    load_gates(OWN * C, S)
+        load_gates(0, 2 * C)
+        for a in range(PASSES):
+            load_tokens(a)
+        load_gates(2 * C, OWN * C)
         w_src = w_words.rearrange("e a p b -> p (e a) b")
         for e in range(E + 1):
             g = slice(e * PASSES, (e + 1) * PASSES)
@@ -83,229 +79,176 @@ def tile_moe_bds_lin_none_kernel(tc, dyT, w_words, w_scales, gate, offs, pos1, p
         for r, src in enumerate((pos1, pos2, pos3)):
             nc.sync.dma_start(token_slot[r][:], src)
 
-        rest = S - FRONT
-        opened = 2 * LAST * MM
-        gather_a = over.tile([P, PACK * S], F32, name="gather_a", align_bytes=64, offset=0)
-        gather_bytes = PACK * S * 4
-        gather_b = over.tile([P, PACK * S], F32, name="gather_b", align_bytes=64, offset=gather_bytes)
-        bf_front = keep.tile([P, LAST * FRONT * PACK], BF16, name="bf_front", align_bytes=64)
-        bf_rest = keep.tile([P, LAST * rest * PACK], BF16, name="bf_rest", align_bytes=64)
-        codes_front = keep.tile([P, LAST * FRONT], U32, name="codes_front", align_bytes=64)
-        exp_front = keep.tile([P, LAST * FRONT], U8, name="exp_front", align_bytes=64)
-        exp_rest = keep.tile([P, LAST * rest], U8, name="exp_rest", align_bytes=64)
-        codes_bank = keep.tile([P, BANK], U32, name="codes_bank", tag="codes_bank", align_bytes=64)
-        codes_last = keep.tile([P, S], U32, name="codes_last", align_bytes=64)
-        exp_last = keep.tile([P, S], U8, name="exp_last", align_bytes=64)
-        d_exp = keep.tile([P, PASSES * T], U8, name="d_exp", align_bytes=64)
+        dx = [keep.tile([P, S], F32, name="dx%d" % h) for h in range(HALVES)]
+        codes = [keep.tile([P, S], U32, name="codes%d" % a, align_bytes=64) for a in range(PASSES)]
+        exps = [keep.tile([P, S], U8, name="exps%d" % a, align_bytes=64) for a in range(PASSES)]
         d_bf = keep.tile([P, PASSES * T * PACK], BF16, name="d_bf", align_bytes=64)
-        dx = [keep.tile([P, S], F32, name="dx%d" % h) for h in range(K // P)]
-        late = {}
+        d_codes = keep.tile([P, PASSES * T], U32, name="d_codes", align_bytes=64)
+        d_exp = keep.tile([P, PASSES * T], U8, name="d_exp", align_bytes=64)
 
-        def slot_operand(a, m0):
-            if a == LAST:
-                return (codes_bank if m0 < BANK else codes_last)[:, m0 : m0 + MM], exp_last[:, m0 : m0 + MM]
-            if m0 < FRONT:
-                w = a * FRONT + m0
-                return codes_front[:, w : w + MM], exp_front[:, w : w + MM]
-            w = ((m0 - FRONT) // MM * LAST + a) * MM
-            if w < opened:
-                return late["opened"][:, w : w + MM], exp_rest[:, w : w + MM]
-            return late["held"][:, w - opened : w - opened + MM], exp_rest[:, w : w + MM]
-
-        def product(acc, e, h, operand, passes):
-            for a in passes:
-                g = e * PASSES + a
-                codes, exps = operand(a)
-                nc.tensor.matmul_mx(
-                    out=acc,
-                    lhsT=w_codes[:, g, 2 * P * h : 2 * P * (h + 1)].bitcast(FP4X4),
-                    lhsT_scale=w_exp[:, g, P * h : P * (h + 1)],
-                    rhs=codes.bitcast(FP8X4),
-                    rhs_scale=exps,
-                    start=(a == 0),
-                    stop=(a == LAST),
-                )
-
-        def slot_product(acc, h, m0, passes):
-            product(acc, m0 // C, h, lambda a: slot_operand(a, m0), passes)
-
-        def slot_sums(acc, h, b0, b1):
-            for m0 in range(b0, b1, MM):
-                slot_product(acc[:, m0 - b0 : m0 - b0 + MM], h, m0, range(PASSES))
-
-        def leave(acc, h, b0, b1):
-            nc.scalar.copy(out=dx[h][:, b0:b1], in_=acc[:])
-
-        def gather(rows, a, j, c0, c1, first):
-            picked = window[a, j][:].indirect(slot_token[:, c0 // 16 : c1 // 16])
-            nc.vector.tensor_tensor(rows[:, j, c0 - first : c1 - first], picked, gates[:, c0:c1], MULT)
-
-        def round_slots(g_bf, rows):
-            nc.scalar.copy(
-                out=g_bf.rearrange("p (c i j) -> p c j i", i=4, j=PACK),
-                in_=rows.rearrange("p j (c i) -> p c j i", i=4),
+        def product(acc, e, h, a, rhs, rhs_exp, start, stop):
+            g = e * PASSES + a
+            nc.tensor.matmul_mx(
+                out=acc,
+                lhsT=w_codes[:, g, 2 * P * h : 2 * P * (h + 1)].bitcast(FP4X4),
+                lhsT_scale=w_exp[:, g, P * h : P * (h + 1)],
+                rhs=rhs.bitcast(FP8X4),
+                rhs_scale=rhs_exp,
+                start=start,
+                stop=stop,
             )
 
-        def quantize(codes, exps, g_bf, w0, w1, first=0):
-            nc.vector.quantize_mx(out=codes[:, w0:w1].bitcast(FP8X4), scales=exps[:, w0:w1], in_=g_bf[:, (w0 - first) * PACK : (w1 - first) * PACK])
+        def expert_sums(acc, e, h):
+            for a in range(PASSES):
+                product(acc, e, h, a, codes[a][:, e * C : (e + 1) * C], exps[a][:, e * C : (e + 1) * C], a == 0, a == LAST)
 
-        def quantize_rest(codes, w0, w1, first):
-            nc.vector.quantize_mx(out=codes[:, w0 - first : w1 - first].bitcast(FP8X4), scales=exp_rest[:, w0:w1], in_=bf_rest[:, w0 * PACK : w1 * PACK])
+        def picked(a, j, c0, c1):
+            return window[a, j][:].indirect(slot_token[:, c0 // 16 : c1 // 16])
+
+        def woven(g_bf):
+            return g_bf.rearrange("p (c i j) -> p c j i", i=RUN, j=PACK)
+
+        def by_runs(rows):
+            return rows.rearrange("p j (c i) -> p c j i", i=RUN)
+
+        def scalar_gather(a, c0, c1, pool, name):
+            rows = pool.tile([P, PACK, c1 - c0], F32, name=name)
+            for j in range(PACK):
+                nc.scalar.activation(rows[:, j, :], picked(a, j, c0, c1), COPY)
+            return rows
+
+        def gate_and_round(rows, c0, c1):
+            g_bf = ring.tile([P, 2 * C * PACK], BF16, name="g_bf", align_bytes=64)
+            n = c1 - c0
+            weights = gates[:, c0:c1].rearrange("p (c i) -> p c i", i=RUN).unsqueeze(2).to_broadcast([P, n // RUN, PACK, RUN])
+            nc.vector.tensor_tensor(woven(g_bf[:, : n * PACK]), by_runs(rows[:]), weights, MULT)
+            return g_bf
+
+        def vector_gather(a):
+            rows = keep.tile([P, PACK, C], F32, name="own_rows%d" % a)
+            for j in range(PACK):
+                nc.vector.tensor_tensor(rows[:, j, :], picked(a, j, OWN * C, S), gates[:, OWN * C :], MULT)
+            return rows
+
+        def round_own(rows):
+            g_bf = ring.tile([P, 2 * C * PACK], BF16, name="g_bf", align_bytes=64)
+            nc.vector.tensor_copy(woven(g_bf[:, : C * PACK]), by_runs(rows[:]))
+            return g_bf
+
+        def quantize(g_bf, a, c0, c1):
+            nc.vector.quantize_mx(out=codes[a][:, c0:c1].bitcast(FP8X4), scales=exps[a][:, c0:c1], in_=g_bf[:, : (c1 - c0) * PACK])
 
         def round_tokens(a):
-            nc.scalar.copy(
-                out=d_bf[:].rearrange("p (q a c i j) -> p q a c j i", a=PASSES, c=MM // 4, i=4, j=PACK)[:, :, a],
-                in_=dy_all[a][:].rearrange("p (j q c i) -> p q c j i", j=PACK, c=MM // 4, i=4),
+            nc.vector.tensor_copy(
+                d_bf[:].rearrange("p (q a c i j) -> p q a c j i", a=PASSES, c=HALF // RUN, i=RUN, j=PACK)[:, :, a],
+                dy_all[a][:].rearrange("p (j q c i) -> p q c j i", j=PACK, c=HALF // RUN, i=RUN),
             )
-
-        ahead = 4 * MM
-
-        def token_codes(w0, w1):
-            return late["ahead"][:, w0:w1] if w0 < ahead else late["behind"][:, w0 - ahead : w1 - ahead]
 
         def quantize_tokens(w0, w1):
-            nc.vector.quantize_mx(out=token_codes(w0, w1).bitcast(FP8X4), scales=d_exp[:, w0:w1], in_=d_bf[:, w0 * PACK : w1 * PACK])
+            nc.vector.quantize_mx(out=d_codes[:, w0:w1].bitcast(FP8X4), scales=d_exp[:, w0:w1], in_=d_bf[:, w0 * PACK : w1 * PACK])
 
-        def shared_products(acc, h, quarters):
-            for i, q in enumerate(quarters):
-                def operand(a):
-                    w = (q * PASSES + a) * MM
-                    return token_codes(w, w + MM), d_exp[:, w : w + MM]
-                product(acc[:, i * MM : (i + 1) * MM], E, h, operand, range(PASSES))
+        def shared_sums(acc, q):
+            for h in range(HALVES):
+                for a in range(PASSES):
+                    w = (q * PASSES + a) * HALF
+                    product(acc[:, h * HALF : (h + 1) * HALF], E, h, a, d_codes[:, w : w + HALF], d_exp[:, w : w + HALF], a == 0, a == LAST)
 
-        def shared_sums(h, quarters):
-            acc = psum.tile([P, MM * len(quarters)], F32, name="acc")
-            shared_products(acc[:], h, quarters)
-            nc.scalar.copy(out=ds_sb[h][:, quarters[0] * MM : (quarters[-1] + 1) * MM], in_=acc[:])
+        def pair_sums(e0):
+            for h in range(HALVES):
+                acc = psum.tile([P, 2 * C], F32, name="pair%d_%d" % (e0, h))
+                for i in range(2):
+                    expert_sums(acc[:, i * C : (i + 1) * C], e0 + i, h)
+                nc.scalar.copy(out=dx[h][:, e0 * C : (e0 + 2) * C], in_=acc[:])
 
-        for a, tile in enumerate((gather_a, gather_b)):
-            rows = tile[:].rearrange("p (j c) -> p j c", j=PACK)
-            for j in ROW_ORDER:
-                for c0, c1 in spans(HEAD_CUTS if (a, j) == (0, ROW_ORDER[0]) else (S,)):
-                    gather(rows, a, j, c0, c1, 0)
+        first = [scalar_gather(a, 0, 2 * C, keep, "first_rows%d" % a) for a in range(PASSES)]
+        own_bf = None
+        for a in range(PASSES):
+            rows = vector_gather(a)
+            if a > 0:
+                quantize(own_bf, a - 1, OWN * C, S)
+            own_bf = round_own(rows)
+        for a in range(PASSES):
+            g_bf = gate_and_round(first[a], 0, 2 * C)
             if a == 0:
-                round_tokens(0)
-            round_slots(bf_front[:, a * FRONT * PACK : (a + 1) * FRONT * PACK], rows[:, :, :FRONT])
-            nc.scalar.copy(
-                out=bf_rest[:].rearrange("p (m a c i j) -> p m a c j i", a=LAST, c=MM // 4, i=4, j=PACK)[:, :, a],
-                in_=rows[:, :, FRONT:].rearrange("p j (m c i) -> p m c j i", c=MM // 4, i=4),
-            )
-            if a == 0:
-                round_tokens(1)
-                round_tokens(2)
+                quantize(own_bf, LAST, OWN * C, S)
+            round_tokens(a)
+            quantize(g_bf, a, 0, 2 * C)
+        own_acc = psum.tile([P, HALVES * C], F32, name="own_acc", tag="own_acc")
+        for h in range(HALVES):
+            expert_sums(own_acc[:, h * C : (h + 1) * C], OWN, h)
+        for h in range(HALVES):
+            nc.scalar.copy(out=dx[h][:, OWN * C :], in_=own_acc[:, h * C : (h + 1) * C])
+        pair_sums(0)
 
-        rows_front = gather_a[:, : PACK * FRONT].rearrange("p (j c) -> p j c", j=PACK)
-        for j in ROW_ORDER:
-            gather(rows_front, LAST, j, 0, FRONT, 0)
-        rows_middle = gather_a[:, 256 : 256 + PACK * 1024].rearrange("p (j c) -> p j c", j=PACK)[:, :, : MIDDLE - FRONT]
-        for w0, w1 in spans((1024, 512, 256)):
-            quantize(codes_front, exp_front, bf_front, w0, w1)
-        late["ahead"] = over.tile([P, ahead], U32, name="d_codes0", align_bytes=64, offset=gather_bytes)
-        quantize_tokens(0, ahead)
-        early = psum.tile([P, 2 * MM], F32, name="acc")
-        for h in range(K // P):
-            shared_products(early[:, h * MM : (h + 1) * MM], h, (0,))
-        total_tile = over.tile([P, 8 * T], F32, name="totals", align_bytes=64, offset=gather_bytes + 4 * ahead)
-        ds_sb = [total_tile[:, (6 + h) * T : (7 + h) * T] for h in range(K // P)]
+        units = [(a, 2 * C, 4 * C) for a in range(PASSES)] + [(a, END * C, OWN * C) for a in range(LAST)]
+        units = units + [(LAST, END * C, END * C + C // 2), (LAST, END * C + C // 2, OWN * C)]
+        end_acc = [psum.tile([P, C], F32, name="end_acc%d" % h) for h in range(HALVES)]
+        ds_first = keep.tile([P, HALVES, HALF], F32, name="ds_first")
 
-        bf_a = keep.tile([P, FRONT * PACK], BF16, name="bf_a", tag="chain", align_bytes=64)
-        for i, (c0, c1) in enumerate(spans(FRONT_CUTS)):
-            round_slots(bf_a[:, c0 * PACK : c1 * PACK], rows_front[:, :, c0:c1])
-            quantize(codes_bank if c0 < BANK else codes_last, exp_last, bf_a, c0, c1)
-            if i == 1:
-                gather(rows_middle, LAST, 0, FRONT, MIDDLE, FRONT)
-        nc.scalar.copy(
-            out=total_tile[:, 6 * T :].rearrange("p (h t) -> p h t", h=2)[:, :, :MM],
-            in_=early[:].rearrange("p (h t) -> p h t", h=2),
-        )
-        for j in range(1, PACK):
-            gather(rows_middle, LAST, j, FRONT, MIDDLE, FRONT)
-        for h in range(K // P):
-            acc = psum.tile([P, BANK], F32, name="acc")
-            slot_sums(acc, h, 0, BANK)
-            leave(acc, h, 0, BANK)
-        second = []
-        for h in range(K // P):
-            acc = psum.tile([P, FRONT - BANK], F32, name="acc")
-            slot_sums(acc, h, BANK, FRONT)
-            second.append(acc)
+        def finish(g_bf, a, c0, c1):
+            quantize(g_bf, a, c0, c1)
+            if c0 < END * C:
+                if a == LAST:
+                    pair_sums(2)
+                return
+            for h in range(HALVES):
+                product(end_acc[h][:, c0 - END * C : c1 - END * C], END, h, a, codes[a][:, c0:c1], exps[a][:, c0:c1], a == 0, a == LAST and c1 == OWN * C)
 
-        gather_c = keep.tile([P, PACK * (S - MIDDLE)], F32, name="gather_c", tag="chain", align_bytes=64)
-        rows_back = gather_c[:].rearrange("p (j c) -> p j c", j=PACK)
-        for j in ROW_ORDER:
-            gather(rows_back, LAST, j, MIDDLE, S, MIDDLE)
-            if j == ROW_ORDER[1]:
-                late["opened"] = keep.tile([P, opened], U32, name="codes_opened", tag="window%d_%d" % (LAST, ROW_ORDER[0]), align_bytes=64)
-                quantize_rest(late["opened"], 0, opened, 0)
-        m1, m2, m3, m4, m5 = range(FRONT, S, MM)
-        sum0_m1 = psum_end.tile([P, MM], F32, name="sum0_m1", tag="sum0_m1")
-        sum0_m234 = psum_end.tile([P, 3 * MM], F32, name="sum0_m234")
-        sum0_m5 = psum_end.tile([P, MM], F32, name="sum0_m5")
-        sum1_m1 = psum_end.tile([P, MM], F32, name="sum1_m1")
-        sum1_m2 = psum_end.tile([P, MM], F32, name="sum1_m2")
-        slot_product(sum0_m1[:], 0, m1, range(LAST))
-        slot_product(sum0_m234[:, :MM], 0, m2, range(LAST))
-        slot_product(sum1_m1[:], 1, m1, range(LAST))
-        slot_product(sum1_m2[:], 1, m2, range(LAST))
+        waiting = None
+        for i, (a, c0, c1) in enumerate(units):
+            rows = scalar_gather(a, c0, c1, keep, "rows%d" % i)
+            g_bf = gate_and_round(rows, c0, c1)
+            if waiting is None:
+                quantize_tokens(0, 2 * HALF)
+                quantize_tokens(2 * HALF, 3 * HALF)
+                acc = psum.tile([P, HALVES * HALF], F32, name="ds_first_acc")
+                shared_sums(acc, 0)
+                nc.scalar.copy(out=ds_first[:].rearrange("p h t -> p (h t)"), in_=acc[:])
+            else:
+                finish(*waiting)
+            waiting = (g_bf, a, c0, c1)
+        quantize_tokens(3 * HALF, 4 * HALF)
+        finish(*waiting)
+        for h in range(HALVES):
+            nc.scalar.copy(out=dx[h][:, END * C : OWN * C], in_=end_acc[h][:])
+        quantize_tokens(4 * HALF, 6 * HALF)
+        ds_second = psum.tile([P, HALVES * HALF], F32, name="ds_second", tag="own_acc")
+        shared_sums(ds_second, 1)
 
-        bf_b = keep.tile([P, (MIDDLE - FRONT) * PACK], BF16, name="bf_b", tag="codes_bank", align_bytes=64)
-        round_slots(bf_b[:], rows_middle)
-        for h in range(K // P):
-            leave(second[h], h, BANK, FRONT)
-        bf_c = over.tile([P, (S - MIDDLE) * PACK], BF16, name="bf_c", align_bytes=64, offset=4096)
-        for u0, u1 in spans((MM, MM)):
-            round_slots(bf_c[:, u0 * PACK : u1 * PACK], rows_back[:, :, u0:u1])
+        def fetch(r, h, q):
+            got = keep.tile([P, HALF], F32, name="got%d_%d_%d" % (r, h, q))
+            nc.scalar.activation(got[:], dx[h][:].indirect(token_slot[r][:, q * HALF // 16 : (q + 1) * HALF // 16]), COPY)
+            return got
 
-        quantize(codes_last, exp_last, bf_b, m1, m3, FRONT)
-        slot_product(sum0_m1[:], 0, m1, (LAST,))
-        leave(sum0_m1, 0, m1, m2)
-        slot_product(sum0_m234[:, :MM], 0, m2, (LAST,))
-        quantize(codes_last, exp_last, bf_b, m3, m4, FRONT)
-        late["held"] = over.tile([P, LAST * rest - opened], U32, name="codes_held", align_bytes=64, offset=0)
-        quantize_rest(late["held"], opened, opened + 2 * LAST * MM, opened)
-        slot_product(sum0_m234[:, MM : 2 * MM], 0, m3, range(PASSES))
-        quantize(codes_last, exp_last, bf_c, m4, m5, MIDDLE)
-        slot_product(sum0_m234[:, 2 * MM :], 0, m4, range(PASSES))
-        leave(sum0_m234, 0, m2, m5)
-        quantize_rest(late["held"], opened + 2 * LAST * MM, LAST * rest, opened)
-        slot_product(sum0_m5[:], 0, m5, range(LAST))
-        quantize(codes_last, exp_last, bf_c, m5, S, MIDDLE)
-        slot_product(sum0_m5[:], 0, m5, (LAST,))
-        leave(sum0_m5, 0, m5, S)
+        def fetch_add(h, q, before):
+            total = keep.tile([P, HALF], F32, name="third%d_%d" % (h, q))
+            nc.vector.tensor_tensor(total[:], dx[h][:].indirect(token_slot[2][:, q * HALF // 16 : (q + 1) * HALF // 16]), before, ADD)
+            return total
 
-        late["behind"] = keep.tile([P, PASSES * T - ahead], U32, name="d_codes1", tag="chain", align_bytes=64)
-        quantize_tokens(ahead, PASSES * HALF)
-        shared_sums(0, (1,))
-        for w0, w1 in spans((2 * MM, 4 * MM), PASSES * HALF):
-            quantize_tokens(w0, w1)
-        slot_product(sum1_m1[:], 1, m1, (LAST,))
-        leave(sum1_m1, 1, m1, m2)
-        slot_product(sum1_m2[:], 1, m2, (LAST,))
-        leave(sum1_m2, 1, m2, m3)
-        sum1_m345 = psum_end.tile([P, 3 * MM], F32, name="sum1_m345", tag="sum0_m1")
-        slot_sums(sum1_m345, 1, m3, S)
-        leave(sum1_m345, 1, m3, S)
-        shared_sums(1, (1,))
-        for h in range(K // P):
-            shared_sums(h, (2, 3))
+        def add(x, y, name):
+            total = keep.tile([P, HALF], F32, name=name)
+            nc.vector.tensor_tensor(total[:], x, y, ADD)
+            return total
 
-        totals = [[total_tile[:, (3 * h + r) * T : (3 * h + r + 1) * T] for r in range(3)] for h in range(K // P)]
+        def store(total, h, q):
+            nc.sync.dma_start(out=out[P * h : P * (h + 1), q * HALF : (q + 1) * HALF], in_=total[:])
 
-        def combine(h, r, t0, t1):
-            before = ds_sb[h] if r == 0 else totals[h][r - 1]
-            picked = dx[h][:].indirect(token_slot[r][:, t0 // 16 : t1 // 16])
-            nc.vector.tensor_tensor(totals[h][r][:, t0:t1], picked, before[:, t0:t1], ADD)
-            if r == 2:
-                nc.sync.dma_start(out=out[P * h : P * (h + 1), t0:t1], in_=totals[h][r][:, t0:t1])
-
-        for r in range(2):
-            for t0, t1 in spans((MM, MM)):
-                combine(0, r, t0, t1)
-        combine(1, 0, 0, HALF)
-        for h in range(K // P):
-            combine(h, 0, HALF, T)
-        combine(0, 1, HALF, T)
-        combine(1, 1, 0, T)
-        combine(0, 2, 0, T)
-        for t0, t1 in spans(TAIL_CUTS):
-            combine(1, 2, t0, t1)
+        got = {}
+        for r, h, q in ((0, 0, 1), (0, 1, 1), (0, 0, 0), (1, 0, 0), (0, 1, 0), (1, 1, 0), (1, 0, 1), (1, 1, 1)):
+            got[r, h, q] = fetch(r, h, q)
+        a0 = fetch_add(0, 0, ds_first[:, 0, :])
+        a1 = fetch_add(1, 0, ds_first[:, 1, :])
+        b0 = fetch_add(0, 1, got[0, 0, 1][:])
+        b1 = fetch_add(1, 1, got[0, 1, 1][:])
+        a0 = add(a0[:], got[0, 0, 0][:], "a0x")
+        b0 = add(ds_second[:, :HALF], b0[:], "b0x")
+        a0 = add(a0[:], got[1, 0, 0][:], "a0y")
+        store(a0, 0, 0)
+        a1 = add(a1[:], got[0, 1, 0][:], "a1x")
+        b1 = add(ds_second[:, HALF:], b1[:], "b1x")
+        a1 = add(a1[:], got[1, 1, 0][:], "a1y")
+        store(a1, 1, 0)
+        b0 = add(b0[:], got[1, 0, 1][:], "b0y")
+        store(b0, 0, 1)
+        b1 = add(b1[:], got[1, 1, 1][:], "b1y")
+        store(b1, 1, 1)

@@ -46,6 +46,9 @@ def tile_moe_bds_lin_none_kernel(tc, dyT, w_words, w_scales, gate, offs, pos1, p
         w_exp = keep.tile([P, (E + 1) * PASSES, K], U8, name="w_exp", align_bytes=64)
         nc.vector.memset(w_exp[:].rearrange("p g k -> p (g k)").bitcast(I32), 0)
 
+        warm = keep.tile([P, 2], F32, name="warm")
+        nc.vector.memset(warm[:, 0:1], 0.0)
+        nc.scalar.activation(warm[:, 1:2], warm[:, 0:1], COPY)
         gates = keep.tile([P, S], F32, name="gates")
         dy_all = [keep.tile([P, PACK * T], F32, name="dy_all%d" % a) for a in range(PASSES)]
         window = {}

@@ -1,6 +1,7 @@
 from contextlib import ExitStack
 
 import concourse.mybir as mybir
+from concourse.masks import make_identity
 
 K, T, E, C, N = 256, 512, 6, 256, 1536
 S = E * C
@@ -26,8 +27,10 @@ HALF = T // 2
 LAST = PASSES - 1
 HALVES = K // P
 RUN = 2
-OWN = E - 1
-END = E - 2
+BANK = 512
+SPLIT = 2 * BANK
+OWN = SPLIT + P
+MOST = 3 * P
 
 
 def tile_moe_bds_lin_none_kernel(tc, dyT, w_words, w_scales, gate, offs, pos1, pos2, pos3, out):
@@ -35,7 +38,6 @@ def tile_moe_bds_lin_none_kernel(tc, dyT, w_words, w_scales, gate, offs, pos1, p
     with ExitStack() as ctx:
         lists = ctx.enter_context(tc.tile_pool(name="lists", bufs=1))
         keep = ctx.enter_context(tc.tile_pool(name="keep", bufs=1))
-        ring = ctx.enter_context(tc.tile_pool(name="ring", bufs=3))
         psum = ctx.enter_context(tc.psum_pool(name="psum", bufs=1))
 
         slot_token = lists.tile([P, S // 16], U16, name="slot_token")
@@ -49,29 +51,27 @@ def tile_moe_bds_lin_none_kernel(tc, dyT, w_words, w_scales, gate, offs, pos1, p
         warm = keep.tile([P, 2], F32, name="warm")
         nc.vector.memset(warm[:, 0:1], 0.0)
         nc.scalar.activation(warm[:, 1:2], warm[:, 0:1], COPY)
-        gates = keep.tile([P, S], F32, name="gates")
-        dy_all = [keep.tile([P, PACK * T], F32, name="dy_all%d" % a) for a in range(PASSES)]
+        ident = keep.tile([P, P], F32, name="ident")
+        make_identity(nc, ident[:])
+
+        gates = keep.tile([P, S - SPLIT], F32, name="gates")
+        gate_cols = keep.tile([P, SPLIT // P], F32, name="gate_cols")
+        dy_all = keep.tile([P, PASSES, PACK * T], F32, name="dy_all")
         window = {}
         for a in range(PASSES):
             for j in range(PACK):
                 window[a, j] = keep.tile([P, T + 16], F32, name="window%d_%d" % (a, j))
-
-        def load_gates(c0, c1):
-            nc.sync.dma_start(out=gates[:, c0:c1], in_=gate[0:P, c0:c1])
-
-        def load_tokens(a):
-            nc.sync.dma_start(out=dy_all[a][:], in_=dy_rows[a].rearrange("p j t -> p (j t)"))
 
         nc.sync.dma_start(slot_token[:], offs)
         for a in range(PASSES):
             for j in range(PACK):
                 nc.sync.dma_start(out=window[a, j][:, 0:T], in_=dy_rows[a, :, j, :])
                 if (a, j) == (0, 0):
-                    load_gates(OWN * C, S)
-        load_gates(0, 2 * C)
+                    nc.sync.dma_start(out=gates[:], in_=gate[0:P, SPLIT:S])
+        with nc.allow_non_contiguous_dma(reason="one gate value a partition"):
+            nc.sync.dma_start(out=gate_cols[:], in_=gate[0, 0:SPLIT].rearrange("(b p) -> p b", p=P))
         for a in range(PASSES):
-            load_tokens(a)
-        load_gates(2 * C, OWN * C)
+            nc.sync.dma_start(out=dy_all[:, a, :], in_=dy_rows[a].rearrange("p j t -> p (j t)"))
         w_src = w_words.rearrange("e a p b -> p (e a) b")
         for e in range(E + 1):
             g = slice(e * PASSES, (e + 1) * PASSES)
@@ -82,12 +82,22 @@ def tile_moe_bds_lin_none_kernel(tc, dyT, w_words, w_scales, gate, offs, pos1, p
         for r, src in enumerate((pos1, pos2, pos3)):
             nc.sync.dma_start(token_slot[r][:], src)
 
+        gate_bank = []
+        for b in range(2):
+            bank = psum.tile([P, BANK], F32, name="gate_bank%d" % b, tag="gate_bank%d" % b)
+            for m in range(BANK // P):
+                col = b * BANK // P + m
+                nc.tensor.transpose(bank[:, m * P : (m + 1) * P], gate_cols[:, col : col + 1].to_broadcast([P, P]), ident[:])
+            gate_bank.append(bank)
+
         dx = [keep.tile([P, S], F32, name="dx%d" % h) for h in range(HALVES)]
         codes = [keep.tile([P, S], U32, name="codes%d" % a, align_bytes=64) for a in range(PASSES)]
         exps = [keep.tile([P, S], U8, name="exps%d" % a, align_bytes=64) for a in range(PASSES)]
-        d_bf = keep.tile([P, PASSES * T * PACK], BF16, name="d_bf", align_bytes=64)
-        d_codes = keep.tile([P, PASSES * T], U32, name="d_codes", align_bytes=64)
-        d_exp = keep.tile([P, PASSES * T], U8, name="d_exp", align_bytes=64)
+        d_codes = [keep.tile([P, MOST], U32, name="d_codes%d" % a, align_bytes=64) for a in range(PASSES)]
+        d_exp = [keep.tile([P, MOST], U8, name="d_exp%d" % a, align_bytes=64) for a in range(PASSES)]
+        q_bf = keep.tile([P, PASSES * P * PACK], BF16, name="q_bf", align_bytes=64)
+        q_codes = keep.tile([P, PASSES * P], U32, name="q_codes", align_bytes=64)
+        q_exp = keep.tile([P, PASSES * P], U8, name="q_exp", align_bytes=64)
 
         def product(acc, e, h, a, rhs, rhs_exp, start, stop):
             g = e * PASSES + a
@@ -101,9 +111,8 @@ def tile_moe_bds_lin_none_kernel(tc, dyT, w_words, w_scales, gate, offs, pos1, p
                 stop=stop,
             )
 
-        def expert_sums(acc, e, h):
-            for a in range(PASSES):
-                product(acc, e, h, a, codes[a][:, e * C : (e + 1) * C], exps[a][:, e * C : (e + 1) * C], a == 0, a == LAST)
+        def slot_product(acc, h, a, c0, c1, start, stop):
+            product(acc, c0 // C, h, a, codes[a][:, c0:c1], exps[a][:, c0:c1], start, stop)
 
         def picked(a, j, c0, c1):
             return window[a, j][:].indirect(slot_token[:, c0 // 16 : c1 // 16])
@@ -114,109 +123,133 @@ def tile_moe_bds_lin_none_kernel(tc, dyT, w_words, w_scales, gate, offs, pos1, p
         def by_runs(rows):
             return rows.rearrange("p j (c i) -> p c j i", i=RUN)
 
-        def scalar_gather(a, c0, c1, pool, name):
-            rows = pool.tile([P, PACK, c1 - c0], F32, name=name)
+        def bf_tile(n, name, tag):
+            return keep.tile([P, n * PACK], BF16, name=name, tag=tag, align_bytes=64)
+
+        def scalar_gather(a, c0, c1):
+            rows = keep.tile([P, PACK, c1 - c0], F32, name="rows%d_%d" % (a, c0))
             for j in range(PACK):
                 nc.scalar.activation(rows[:, j, :], picked(a, j, c0, c1), COPY)
             return rows
 
-        def gate_and_round(rows, c0, c1):
-            g_bf = ring.tile([P, 2 * C * PACK], BF16, name="g_bf", align_bytes=64)
-            n = c1 - c0
-            weights = gates[:, c0:c1].rearrange("p (c i) -> p c i", i=RUN).unsqueeze(2).to_broadcast([P, n // RUN, PACK, RUN])
-            nc.vector.tensor_tensor(woven(g_bf[:, : n * PACK]), by_runs(rows[:]), weights, MULT)
+        def gate_and_round(rows, weights, name):
+            n = rows.shape[2]
+            g_bf = bf_tile(n, name, name)
+            spread = weights.rearrange("p (c i) -> p c i", i=RUN).unsqueeze(2).to_broadcast([P, n // RUN, PACK, RUN])
+            nc.vector.tensor_tensor(woven(g_bf[:]), by_runs(rows[:]), spread, MULT)
             return g_bf
 
         def vector_gather(a):
-            rows = keep.tile([P, PACK, C], F32, name="own_rows%d" % a)
+            rows = keep.tile([P, PACK, S - OWN], F32, name="own_rows%d" % a, tag="own_rows%d" % a, align_bytes=64)
             for j in range(PACK):
-                nc.vector.tensor_tensor(rows[:, j, :], picked(a, j, OWN * C, S), gates[:, OWN * C :], MULT)
+                nc.vector.tensor_tensor(rows[:, j, :], picked(a, j, OWN, S), gates[:, OWN - SPLIT :], MULT)
             return rows
 
-        def round_own(rows):
-            g_bf = ring.tile([P, 2 * C * PACK], BF16, name="g_bf", align_bytes=64)
-            nc.vector.tensor_copy(woven(g_bf[:, : C * PACK]), by_runs(rows[:]))
+        def gpsimd_round(rows, name, tag):
+            g_bf = bf_tile(rows.shape[2], name, tag)
+            nc.gpsimd.tensor_scalar(g_bf[:].rearrange("p (c j) -> p c j", j=PACK), rows.rearrange("p j c -> p c j"), 1.0, 0.0, MULT, ADD)
             return g_bf
 
+        def token_rows(a):
+            return dy_all[:, a, :].rearrange("p (j t) -> p j t", j=PACK)[:, :, :MOST]
+
         def quantize(g_bf, a, c0, c1):
-            nc.vector.quantize_mx(out=codes[a][:, c0:c1].bitcast(FP8X4), scales=exps[a][:, c0:c1], in_=g_bf[:, : (c1 - c0) * PACK])
+            nc.vector.quantize_mx(out=codes[a][:, c0:c1].bitcast(FP8X4), scales=exps[a][:, c0:c1], in_=g_bf[:])
 
-        def round_tokens(a):
-            nc.vector.tensor_copy(
-                d_bf[:].rearrange("p (q a c i j) -> p q a c j i", a=PASSES, c=HALF // RUN, i=RUN, j=PACK)[:, :, a],
-                dy_all[a][:].rearrange("p (j q c i) -> p q c j i", j=PACK, c=HALF // RUN, i=RUN),
-            )
+        def quantize_tokens(t_bf, a, t0, t1):
+            nc.vector.quantize_mx(out=d_codes[a][:, t0:t1].bitcast(FP8X4), scales=d_exp[a][:, t0:t1], in_=t_bf[:, t0 * PACK : t1 * PACK])
 
-        def quantize_tokens(w0, w1):
-            nc.vector.quantize_mx(out=d_codes[:, w0:w1].bitcast(FP8X4), scales=d_exp[:, w0:w1], in_=d_bf[:, w0 * PACK : w1 * PACK])
+        first = [scalar_gather(a, 0, BANK) for a in range(PASSES)]
+        second = [scalar_gather(a, BANK, SPLIT) for a in range(PASSES)]
+        third = [scalar_gather(a, SPLIT, OWN) for a in range(PASSES)]
+        own = [vector_gather(a) for a in range(PASSES)]
 
-        def shared_sums(acc, q):
-            for h in range(HALVES):
+        own_bf2 = gpsimd_round(own[2][:], "own_bf2", "own_bf2")
+        own_bf0 = gpsimd_round(own[0][:], "own_bf0", "own_rows2")
+        a0 = gate_and_round(first[0], gate_bank[0][:], "a0")
+        a1 = gate_and_round(first[1], gate_bank[0][:], "a1")
+        quantize(own_bf2, 2, OWN, S)
+        quantize(a0, 0, 0, BANK)
+        quantize(own_bf0, 0, OWN, S)
+        quantize(a1, 1, 0, BANK)
+
+        own_bf1 = gpsimd_round(own[1][:], "own_bf1", "a1")
+        t0 = gpsimd_round(token_rows(0), "t0", "own_rows1")
+        a2 = gate_and_round(first[2], gate_bank[0][:], "a2")
+        b0 = gate_and_round(second[0], gate_bank[1][:], "b0")
+        quantize(own_bf1, 1, OWN, S)
+        quantize(a2, 2, 0, BANK)
+        quantize_tokens(t0, 0, 0, MOST)
+        quantize(b0, 0, BANK, SPLIT)
+
+        for h in range(HALVES):
+            acc = psum.tile([P, S - OWN], F32, name="own_acc%d" % h, tag="own_acc%d" % h)
+            for c0, c1 in ((OWN, OWN + P), (OWN + P, S)):
                 for a in range(PASSES):
-                    w = (q * PASSES + a) * HALF
-                    product(acc[:, h * HALF : (h + 1) * HALF], E, h, a, d_codes[:, w : w + HALF], d_exp[:, w : w + HALF], a == 0, a == LAST)
+                    slot_product(acc[:, c0 - OWN : c1 - OWN], h, a, c0, c1, a == 0, a == LAST)
+            nc.scalar.copy(out=dx[h][:, OWN:], in_=acc[:])
+        for h in range(HALVES):
+            acc = psum.tile([P, BANK], F32, name="first_acc%d" % h)
+            for c0 in (0, C):
+                for a in range(PASSES):
+                    slot_product(acc[:, c0 : c0 + C], h, a, c0, c0 + C, a == 0, a == LAST)
+            nc.scalar.copy(out=dx[h][:, :BANK], in_=acc[:])
+        second_acc = [psum.tile([P, BANK], F32, name="second_acc0"), psum.tile([P, BANK], F32, name="second_acc1", tag="gate_bank0")]
 
-        def pair_sums(e0):
+        def second_pass(a):
             for h in range(HALVES):
-                acc = psum.tile([P, 2 * C], F32, name="pair%d_%d" % (e0, h))
                 for i in range(2):
-                    expert_sums(acc[:, i * C : (i + 1) * C], e0 + i, h)
-                nc.scalar.copy(out=dx[h][:, e0 * C : (e0 + 2) * C], in_=acc[:])
+                    c0 = BANK + i * C
+                    slot_product(second_acc[h][:, i * C : (i + 1) * C], h, a, c0, c0 + C, a == 0 and i == 0, a == LAST and i == 1)
 
-        first = [scalar_gather(a, 0, 2 * C, keep, "first_rows%d" % a) for a in range(PASSES)]
-        own_bf = None
-        for a in range(PASSES):
-            rows = vector_gather(a)
-            if a > 0:
-                quantize(own_bf, a - 1, OWN * C, S)
-            own_bf = round_own(rows)
-        for a in range(PASSES):
-            g_bf = gate_and_round(first[a], 0, 2 * C)
-            if a == 0:
-                quantize(own_bf, LAST, OWN * C, S)
-            round_tokens(a)
-            quantize(g_bf, a, 0, 2 * C)
-        own_acc = psum.tile([P, HALVES * C], F32, name="own_acc", tag="own_acc")
-        for h in range(HALVES):
-            expert_sums(own_acc[:, h * C : (h + 1) * C], OWN, h)
-        for h in range(HALVES):
-            nc.scalar.copy(out=dx[h][:, OWN * C :], in_=own_acc[:, h * C : (h + 1) * C])
-        pair_sums(0)
+        second_pass(0)
+        t1 = gpsimd_round(token_rows(1), "t1", "b0")
+        b1 = gate_and_round(second[1], gate_bank[1][:], "b1")
+        nc.vector.tensor_copy(
+            q_bf[:].rearrange("p (a c i j) -> p a c j i", a=PASSES, i=RUN, j=PACK),
+            dy_all[:].rearrange("p a (j t) -> p a j t", j=PACK)[:, :, :, MOST:].rearrange("p a j (c i) -> p a c j i", i=RUN),
+        )
+        quantize_tokens(t1, 1, 0, MOST)
+        quantize(b1, 1, BANK, SPLIT)
+        second_pass(1)
 
-        units = [(a, 2 * C, 4 * C) for a in range(PASSES)] + [(a, END * C, OWN * C) for a in range(LAST)]
-        units = units + [(LAST, END * C, END * C + C // 2), (LAST, END * C + C // 2, OWN * C)]
-        end_acc = [psum.tile([P, C], F32, name="end_acc%d" % h) for h in range(HALVES)]
-        ds_first = keep.tile([P, HALVES, HALF], F32, name="ds_first")
+        t2 = gpsimd_round(token_rows(2), "t2", "b1")
+        b2 = gate_and_round(second[2], gate_bank[1][:], "b2")
+        third_acc = psum.tile([P, HALVES * P], F32, name="third_acc")
 
-        def finish(g_bf, a, c0, c1):
-            quantize(g_bf, a, c0, c1)
-            if c0 < END * C:
-                if a == LAST:
-                    pair_sums(2)
-                return
+        def third_pass(g_bf, a):
+            quantize(g_bf, a, SPLIT, OWN)
             for h in range(HALVES):
-                product(end_acc[h][:, c0 - END * C : c1 - END * C], END, h, a, codes[a][:, c0:c1], exps[a][:, c0:c1], a == 0, a == LAST and c1 == OWN * C)
+                slot_product(third_acc[:, h * P : (h + 1) * P], h, a, SPLIT, OWN, a == 0 and h == 0, a == LAST and h == HALVES - 1)
 
-        waiting = None
-        for i, (a, c0, c1) in enumerate(units):
-            rows = scalar_gather(a, c0, c1, keep, "rows%d" % i)
-            g_bf = gate_and_round(rows, c0, c1)
-            if waiting is None:
-                quantize_tokens(0, 2 * HALF)
-                quantize_tokens(2 * HALF, 3 * HALF)
-                acc = psum.tile([P, HALVES * HALF], F32, name="ds_first_acc")
-                shared_sums(acc, 0)
-                nc.scalar.copy(out=ds_first[:].rearrange("p h t -> p (h t)"), in_=acc[:])
-            else:
-                finish(*waiting)
-            waiting = (g_bf, a, c0, c1)
-        quantize_tokens(3 * HALF, 4 * HALF)
-        finish(*waiting)
+        c_gates = gates[:, : OWN - SPLIT]
+        c0_bf = gate_and_round(third[0], c_gates, "c0")
+        quantize(b2, 2, BANK, SPLIT)
+        second_pass(2)
         for h in range(HALVES):
-            nc.scalar.copy(out=dx[h][:, END * C : OWN * C], in_=end_acc[h][:])
-        quantize_tokens(4 * HALF, 6 * HALF)
-        ds_second = psum.tile([P, HALVES * HALF], F32, name="ds_second", tag="own_acc")
-        shared_sums(ds_second, 1)
+            nc.scalar.copy(out=dx[h][:, BANK:SPLIT], in_=second_acc[h][:])
+        c1_bf = gate_and_round(third[1], c_gates, "c1")
+        quantize_tokens(t2, 2, 0, HALF)
+        ds_first = keep.tile([P, HALVES, HALF], F32, name="ds_first")
+        acc = psum.tile([P, HALVES * HALF], F32, name="ds_first_acc", tag="gate_bank1")
+        for h in range(HALVES):
+            for a in range(PASSES):
+                product(acc[:, h * HALF : (h + 1) * HALF], E, h, a, d_codes[a][:, :HALF], d_exp[a][:, :HALF], a == 0, a == LAST)
+        nc.scalar.copy(out=ds_first[:].rearrange("p h t -> p (h t)"), in_=acc[:])
+        third_pass(c0_bf, 0)
+        c2_bf = gate_and_round(third[2], c_gates, "c2")
+        third_pass(c1_bf, 1)
+        quantize_tokens(t2, 2, HALF, MOST)
+        third_pass(c2_bf, 2)
+        for h in range(HALVES):
+            nc.scalar.copy(out=dx[h][:, SPLIT:OWN], in_=third_acc[:, h * P : (h + 1) * P])
+        nc.vector.quantize_mx(out=q_codes[:].bitcast(FP8X4), scales=q_exp[:], in_=q_bf[:])
+        ds_second = psum.tile([P, HALVES * HALF], F32, name="ds_second", tag="own_acc0")
+        for h in range(HALVES):
+            for a in range(PASSES):
+                product(ds_second[:, h * HALF : h * HALF + P], E, h, a, d_codes[a][:, HALF:], d_exp[a][:, HALF:], a == 0, a == LAST)
+            for a in range(PASSES):
+                product(ds_second[:, h * HALF + P : (h + 1) * HALF], E, h, a, q_codes[:, a * P : (a + 1) * P], q_exp[:, a * P : (a + 1) * P], a == 0, a == LAST)
 
         def fetch(r, h, q):
             got = keep.tile([P, HALF], F32, name="got%d_%d_%d" % (r, h, q))

@@ -38,6 +38,7 @@ def tile_moe_bds_lin_none_kernel(tc, dyT, w_words, w_scales, gate, offs, pos1, p
     with ExitStack() as ctx:
         lists = ctx.enter_context(tc.tile_pool(name="lists", bufs=1))
         keep = ctx.enter_context(tc.tile_pool(name="keep", bufs=1))
+        over = ctx.enter_context(tc.tile_pool(name="over", bufs=1))
         psum = ctx.enter_context(tc.psum_pool(name="psum", bufs=1))
 
         slot_token = lists.tile([P, S // 16], U16, name="slot_token")
@@ -56,29 +57,33 @@ def tile_moe_bds_lin_none_kernel(tc, dyT, w_words, w_scales, gate, offs, pos1, p
 
         gates = keep.tile([P, S - SPLIT], F32, name="gates")
         gate_cols = keep.tile([P, SPLIT // P], F32, name="gate_cols")
-        dy_all = keep.tile([P, PASSES, PACK * T], F32, name="dy_all")
+        dy_most = keep.tile([P, PASSES, PACK, MOST], F32, name="dy_most")
+        dy_last = keep.tile([P, PASSES, PACK, T - MOST], F32, name="dy_last")
         window = {}
         for a in range(PASSES):
             for j in range(PACK):
-                window[a, j] = keep.tile([P, T + 16], F32, name="window%d_%d" % (a, j))
+                window[a, j] = keep.tile([P, (OWN if a == 0 else T) + 16], F32, name="window%d_%d" % (a, j))
 
         nc.sync.dma_start(slot_token[:], offs)
         for a in range(PASSES):
             for j in range(PACK):
                 nc.sync.dma_start(out=window[a, j][:, 0:T], in_=dy_rows[a, :, j, :])
-                if (a, j) == (0, 0):
-                    nc.sync.dma_start(out=gates[:], in_=gate[0:P, SPLIT:S])
-        with nc.allow_non_contiguous_dma(reason="one gate value a partition"):
-            nc.sync.dma_start(out=gate_cols[:], in_=gate[0, 0:SPLIT].rearrange("(b p) -> p b", p=P))
+            if a == 0:
+                nc.sync.dma_start(out=gates[:], in_=gate[0:P, SPLIT:S])
+            if a == LAST:
+                with nc.allow_non_contiguous_dma(reason="one gate value a partition"):
+                    nc.sync.dma_start(out=gate_cols[:], in_=gate[0, 0:SPLIT].rearrange("(b p) -> p b", p=P))
         for a in range(PASSES):
-            nc.sync.dma_start(out=dy_all[:, a, :], in_=dy_rows[a].rearrange("p j t -> p (j t)"))
+            nc.sync.dma_start(out=dy_last[:, a], in_=dy_rows[a, :, :, MOST:])
+        s_src = w_scales.rearrange("e a f k -> f (e a) k")
+        for q in range(4):
+            nc.sync.dma_start(out=w_exp[32 * q : 32 * q + 4, :, :].bitcast(I32), in_=s_src[4 * q : 4 * q + 4].bitcast(I32))
         w_src = w_words.rearrange("e a p b -> p (e a) b")
         for e in range(E + 1):
             g = slice(e * PASSES, (e + 1) * PASSES)
             nc.sync.dma_start(out=w_codes[:, g, :].bitcast(I32), in_=w_src[:, g, :].bitcast(I32))
-        s_src = w_scales.rearrange("e a f k -> f (e a) k")
-        for q in range(4):
-            nc.sync.dma_start(out=w_exp[32 * q : 32 * q + 4, :, :].bitcast(I32), in_=s_src[4 * q : 4 * q + 4].bitcast(I32))
+        for a in range(PASSES):
+            nc.sync.dma_start(out=dy_most[:, a], in_=dy_rows[a, :, :, :MOST])
         for r, src in enumerate((pos1, pos2, pos3)):
             nc.sync.dma_start(token_slot[r][:], src)
 
@@ -95,7 +100,6 @@ def tile_moe_bds_lin_none_kernel(tc, dyT, w_words, w_scales, gate, offs, pos1, p
         exps = [keep.tile([P, S], U8, name="exps%d" % a, align_bytes=64) for a in range(PASSES)]
         d_codes = [keep.tile([P, MOST], U32, name="d_codes%d" % a, align_bytes=64) for a in range(PASSES)]
         d_exp = [keep.tile([P, MOST], U8, name="d_exp%d" % a, align_bytes=64) for a in range(PASSES)]
-        q_bf = keep.tile([P, PASSES * P * PACK], BF16, name="q_bf", align_bytes=64)
         q_codes = keep.tile([P, PASSES * P], U32, name="q_codes", align_bytes=64)
         q_exp = keep.tile([P, PASSES * P], U8, name="q_exp", align_bytes=64)
 
@@ -123,168 +127,165 @@ def tile_moe_bds_lin_none_kernel(tc, dyT, w_words, w_scales, gate, offs, pos1, p
         def by_runs(rows):
             return rows.rearrange("p j (c i) -> p c j i", i=RUN)
 
+        placed = {"a1": 0, "t01": 0, "own_bf2": 6144, "b1": 9216, "t2": 8192}
+
+        reused = {"c0": "own_bf0", "c1": "b0", "c2": "a2"}
+
         def bf_tile(n, name, tag):
+            if name in placed:
+                return over.tile([P, n * PACK], BF16, name=name, align_bytes=64, offset=placed[name])
             return keep.tile([P, n * PACK], BF16, name=name, tag=tag, align_bytes=64)
 
         def scalar_gather(a, c0, c1):
-            rows = keep.tile([P, PACK, c1 - c0], F32, name="rows%d_%d" % (a, c0))
+            rows = keep.tile([P, PACK, c1 - c0], F32, name="rows%d_%d" % (a, c0), tag="rows%d_%d" % (a, c0))
             for j in range(PACK):
                 nc.scalar.activation(rows[:, j, :], picked(a, j, c0, c1), COPY)
             return rows
 
-        def gate_and_round(rows, weights, name):
+        def gate_and_round(rows, weights, name, engine=nc.vector):
             n = rows.shape[2]
-            g_bf = bf_tile(n, name, name)
+            g_bf = bf_tile(n, name, reused.get(name, name))
+            if name.startswith("own"):
+                spread = weights.unsqueeze(2).to_broadcast([P, n, PACK])
+                engine.tensor_tensor(g_bf[:].rearrange("p (c j) -> p c j", j=PACK), rows.rearrange("p j c -> p c j"), spread, MULT)
+                return g_bf
             spread = weights.rearrange("p (c i) -> p c i", i=RUN).unsqueeze(2).to_broadcast([P, n // RUN, PACK, RUN])
-            nc.vector.tensor_tensor(woven(g_bf[:]), by_runs(rows[:]), spread, MULT)
+            engine.tensor_tensor(woven(g_bf[:]), by_runs(rows), spread, MULT)
             return g_bf
 
         def vector_gather(a):
             rows = keep.tile([P, PACK, S - OWN], F32, name="own_rows%d" % a, tag="own_rows%d" % a, align_bytes=64)
             for j in range(PACK):
-                nc.vector.tensor_tensor(rows[:, j, :], picked(a, j, OWN, S), gates[:, OWN - SPLIT :], MULT)
+                nc.vector.tensor_copy(rows[:, j, :], picked(a, j, OWN, S))
             return rows
 
         def gpsimd_round(rows, name, tag):
-            g_bf = bf_tile(rows.shape[2], name, tag)
-            nc.gpsimd.tensor_scalar(g_bf[:].rearrange("p (c j) -> p c j", j=PACK), rows.rearrange("p j c -> p c j"), 1.0, 0.0, MULT, ADD)
-            return g_bf
-
-        def token_rows(a):
-            return dy_all[:, a, :].rearrange("p (j t) -> p j t", j=PACK)[:, :, :MOST]
+            t_bf = bf_tile(rows.shape[1] * rows.shape[3], name, tag)
+            nc.gpsimd.tensor_scalar(t_bf[:].rearrange("p (a t j) -> p a t j", a=rows.shape[1], j=PACK), rows.rearrange("p a j t -> p a t j"), 1.0, 0.0, MULT, ADD)
+            return t_bf
 
         def quantize(g_bf, a, c0, c1):
             nc.vector.quantize_mx(out=codes[a][:, c0:c1].bitcast(FP8X4), scales=exps[a][:, c0:c1], in_=g_bf[:])
 
-        def quantize_tokens(t_bf, a, t0, t1):
-            nc.vector.quantize_mx(out=d_codes[a][:, t0:t1].bitcast(FP8X4), scales=d_exp[a][:, t0:t1], in_=t_bf[:, t0 * PACK : t1 * PACK])
+        def quantize_tokens(t_bf, a):
+            nc.vector.quantize_mx(out=d_codes[a][:].bitcast(FP8X4), scales=d_exp[a][:], in_=t_bf)
 
-        first = [scalar_gather(a, 0, BANK) for a in range(PASSES)]
-        second = [scalar_gather(a, BANK, SPLIT) for a in range(PASSES)]
-        third = [scalar_gather(a, SPLIT, OWN) for a in range(PASSES)]
-        own = [vector_gather(a) for a in range(PASSES)]
+        pass0 = scalar_gather(0, 0, OWN)
+        rows_a1 = scalar_gather(1, 0, BANK)
+        rows_a2 = scalar_gather(2, 0, BANK)
+        rows_b1 = scalar_gather(1, BANK, SPLIT)
+        rows_c1 = scalar_gather(1, SPLIT, OWN)
+        rows_b2 = [scalar_gather(2, c0, c0 + C) for c0 in (BANK, BANK + C)]
+        rows_c2 = scalar_gather(2, SPLIT, OWN)
+        own_bf = []
+        for a in range(PASSES):
+            rows = vector_gather(a)
+            own_bf.append(gate_and_round(rows[:], gates[:, OWN - SPLIT :], "own_bf%d" % a, nc.gpsimd))
+        q_bf = gpsimd_round(dy_last[:], "q_bf", "own_rows2")
 
-        own_bf2 = gpsimd_round(own[2][:], "own_bf2", "own_bf2")
-        own_bf0 = gpsimd_round(own[0][:], "own_bf0", "own_rows2")
-        a0 = gate_and_round(first[0], gate_bank[0][:], "a0")
-        a1 = gate_and_round(first[1], gate_bank[0][:], "a1")
-        quantize(own_bf2, 2, OWN, S)
+        c_gates = gates[:, : OWN - SPLIT]
+        first_acc = [psum.tile([P, BANK], F32, name="first_acc%d" % h) for h in range(HALVES)]
+        third_acc = psum.tile([P, HALVES * P], F32, name="third_acc")
+
+        def first_pass(a):
+            for h in range(HALVES):
+                for i in range(2):
+                    slot_product(first_acc[h][:, i * C : (i + 1) * C], h, a, i * C, (i + 1) * C, a == 0 and i == 0, a == LAST and i == 1)
+
+        def both_halves(acc, a, c0, c1):
+            for h in range(HALVES):
+                slot_product(acc[:, h * (c1 - c0) : (h + 1) * (c1 - c0)], h, a, c0, c1, a == 0 and h == 0, a == LAST and h == HALVES - 1)
+
+        def leave(acc, c0, c1):
+            for h in range(HALVES):
+                nc.scalar.copy(out=dx[h][:, c0:c1], in_=acc[:, h * (c1 - c0) : (h + 1) * (c1 - c0)])
+
+        a0 = gate_and_round(pass0[:, :, :BANK], gate_bank[0][:], "a0")
+        b0 = gate_and_round(pass0[:, :, BANK:SPLIT], gate_bank[1][:], "b0")
+        a1 = gate_and_round(rows_a1[:], gate_bank[0][:], "a1")
+        quantize(own_bf[0], 0, OWN, S)
         quantize(a0, 0, 0, BANK)
-        quantize(own_bf0, 0, OWN, S)
-        quantize(a1, 1, 0, BANK)
-
-        own_bf1 = gpsimd_round(own[1][:], "own_bf1", "a1")
-        t0 = gpsimd_round(token_rows(0), "t0", "own_rows1")
-        a2 = gate_and_round(first[2], gate_bank[0][:], "a2")
-        b0 = gate_and_round(second[0], gate_bank[1][:], "b0")
-        quantize(own_bf1, 1, OWN, S)
-        quantize(a2, 2, 0, BANK)
-        quantize_tokens(t0, 0, 0, MOST)
+        c0_bf = gate_and_round(pass0[:, :, SPLIT:], c_gates, "c0")
+        quantize(own_bf[1], 1, OWN, S)
         quantize(b0, 0, BANK, SPLIT)
+        quantize(c0_bf, 0, SPLIT, OWN)
+        quantize(a1, 1, 0, BANK)
+        first_pass(0)
+        first_pass(1)
+        both_halves(third_acc, 0, SPLIT, OWN)
 
+        t01 = gpsimd_round(dy_most[:, 0:2], "t01", "t01")
+        a2 = gate_and_round(rows_a2[:], gate_bank[0][:], "a2")
+        b1 = gate_and_round(rows_b1[:], gate_bank[1][:], "b1")
+        quantize(own_bf[2], 2, OWN, S)
+        c1_bf = gate_and_round(rows_c1[:], c_gates, "c1")
+        own_acc = []
         for h in range(HALVES):
             acc = psum.tile([P, S - OWN], F32, name="own_acc%d" % h, tag="own_acc%d" % h)
             for c0, c1 in ((OWN, OWN + P), (OWN + P, S)):
                 for a in range(PASSES):
                     slot_product(acc[:, c0 - OWN : c1 - OWN], h, a, c0, c1, a == 0, a == LAST)
-            nc.scalar.copy(out=dx[h][:, OWN:], in_=acc[:])
+            own_acc.append(acc)
+        quantize(a2, 2, 0, BANK)
+        first_pass(2)
         for h in range(HALVES):
-            acc = psum.tile([P, BANK], F32, name="first_acc%d" % h)
-            for c0 in (0, C):
-                for a in range(PASSES):
-                    slot_product(acc[:, c0 : c0 + C], h, a, c0, c0 + C, a == 0, a == LAST)
-            nc.scalar.copy(out=dx[h][:, :BANK], in_=acc[:])
-        second_acc = [psum.tile([P, BANK], F32, name="second_acc0"), psum.tile([P, BANK], F32, name="second_acc1", tag="gate_bank0")]
-
-        def second_pass(a):
-            for h in range(HALVES):
-                for i in range(2):
-                    c0 = BANK + i * C
-                    slot_product(second_acc[h][:, i * C : (i + 1) * C], h, a, c0, c0 + C, a == 0 and i == 0, a == LAST and i == 1)
-
-        second_pass(0)
-        t1 = gpsimd_round(token_rows(1), "t1", "b0")
-        b1 = gate_and_round(second[1], gate_bank[1][:], "b1")
-        nc.vector.tensor_copy(
-            q_bf[:].rearrange("p (a c i j) -> p a c j i", a=PASSES, i=RUN, j=PACK),
-            dy_all[:].rearrange("p a (j t) -> p a j t", j=PACK)[:, :, :, MOST:].rearrange("p a j (c i) -> p a c j i", i=RUN),
-        )
-        quantize_tokens(t1, 1, 0, MOST)
+            nc.scalar.copy(out=dx[h][:, :BANK], in_=first_acc[h][:])
+        nc.scalar.copy(out=dx[1][:, OWN:], in_=own_acc[1][:])
+        quantize(c1_bf, 1, SPLIT, OWN)
         quantize(b1, 1, BANK, SPLIT)
-        second_pass(1)
+        second_acc = [psum.tile([P, BANK], F32, name="second_acc0"), psum.tile([P, BANK], F32, name="second_acc1", tag="gate_bank0")]
+        for i in range(2):
+            for a in range(LAST):
+                both_halves(second_acc[i], a, BANK + i * C, BANK + (i + 1) * C)
+        both_halves(third_acc, 1, SPLIT, OWN)
 
-        t2 = gpsimd_round(token_rows(2), "t2", "b1")
-        b2 = gate_and_round(second[2], gate_bank[1][:], "b2")
-        third_acc = psum.tile([P, HALVES * P], F32, name="third_acc")
-
-        def third_pass(g_bf, a):
-            quantize(g_bf, a, SPLIT, OWN)
-            for h in range(HALVES):
-                slot_product(third_acc[:, h * P : (h + 1) * P], h, a, SPLIT, OWN, a == 0 and h == 0, a == LAST and h == HALVES - 1)
-
-        c_gates = gates[:, : OWN - SPLIT]
-        c0_bf = gate_and_round(third[0], c_gates, "c0")
-        quantize(b2, 2, BANK, SPLIT)
-        second_pass(2)
-        for h in range(HALVES):
-            nc.scalar.copy(out=dx[h][:, BANK:SPLIT], in_=second_acc[h][:])
-        c1_bf = gate_and_round(third[1], c_gates, "c1")
-        quantize_tokens(t2, 2, 0, HALF)
-        ds_first = keep.tile([P, HALVES, HALF], F32, name="ds_first")
-        acc = psum.tile([P, HALVES * HALF], F32, name="ds_first_acc", tag="gate_bank1")
-        for h in range(HALVES):
-            for a in range(PASSES):
-                product(acc[:, h * HALF : (h + 1) * HALF], E, h, a, d_codes[a][:, :HALF], d_exp[a][:, :HALF], a == 0, a == LAST)
-        nc.scalar.copy(out=ds_first[:].rearrange("p h t -> p (h t)"), in_=acc[:])
-        third_pass(c0_bf, 0)
-        c2_bf = gate_and_round(third[2], c_gates, "c2")
-        third_pass(c1_bf, 1)
-        quantize_tokens(t2, 2, HALF, MOST)
-        third_pass(c2_bf, 2)
-        for h in range(HALVES):
-            nc.scalar.copy(out=dx[h][:, SPLIT:OWN], in_=third_acc[:, h * P : (h + 1) * P])
+        t2 = gpsimd_round(dy_most[:, 2:3], "t2", "t2")
+        b2 = [gate_and_round(rows_b2[0][:], gate_bank[1][:, :C], "b2_0")]
+        nc.vector.tensor_copy(dx[0][:, OWN:], own_acc[0][:])
+        b2.append(gate_and_round(rows_b2[1][:], gate_bank[1][:, C:], "b2_1"))
+        quantize(b2[0], 2, BANK, BANK + C)
+        both_halves(second_acc[0], LAST, BANK, BANK + C)
+        leave(second_acc[0], BANK, BANK + C)
+        c2_bf = gate_and_round(rows_c2[:], c_gates, "c2")
+        quantize(b2[1], 2, BANK + C, SPLIT)
+        both_halves(second_acc[1], LAST, BANK + C, SPLIT)
+        leave(second_acc[1], BANK + C, SPLIT)
+        quantize(c2_bf, 2, SPLIT, OWN)
+        both_halves(third_acc, LAST, SPLIT, OWN)
+        leave(third_acc, SPLIT, OWN)
+        quantize_tokens(t01[:, : MOST * PACK], 0)
+        quantize_tokens(t01[:, MOST * PACK :], 1)
+        quantize_tokens(t2[:], 2)
         nc.vector.quantize_mx(out=q_codes[:].bitcast(FP8X4), scales=q_exp[:], in_=q_bf[:])
-        ds_second = psum.tile([P, HALVES * HALF], F32, name="ds_second", tag="own_acc0")
+        ds = [psum.tile([P, HALVES, HALF], F32, name="ds%d" % q, tag=tag) for q, tag in enumerate(("gate_bank1", "own_acc0"))]
         for h in range(HALVES):
             for a in range(PASSES):
-                product(ds_second[:, h * HALF : h * HALF + P], E, h, a, d_codes[a][:, HALF:], d_exp[a][:, HALF:], a == 0, a == LAST)
+                product(ds[0][:, h, :], E, h, a, d_codes[a][:, :HALF], d_exp[a][:, :HALF], a == 0, a == LAST)
+
+        def fetched(r, h, q):
+            return dx[h][:].indirect(token_slot[r][:, q * HALF // 16 : (q + 1) * HALF // 16])
+
+        got_all = keep.tile([P, 4, HALVES, HALF], F32, name="got_all", tag="rows1_0")
+        got = [[got_all[:, 2 * r + q] for q in range(2)] for r in range(2)]
+        opening = over.tile([P, 3, 2, HALVES, HALF], F32, name="opening", align_bytes=64, offset=0)
+        sums = [[opening[:, r, q] for q in range(2)] for r in range(3)]
+        for r in range(2):
+            for q in range(2):
+                for h in range(HALVES):
+                    nc.scalar.activation(got[r][q][:, h, :], fetched(r, h, q), COPY)
+        for q in range(2):
+            for h in range(HALVES):
+                nc.vector.tensor_tensor(sums[0][q][:, h, :], fetched(2, h, q), got[0][q][:, h, :], ADD)
+        for h in range(HALVES):
             for a in range(PASSES):
-                product(ds_second[:, h * HALF + P : (h + 1) * HALF], E, h, a, q_codes[:, a * P : (a + 1) * P], q_exp[:, a * P : (a + 1) * P], a == 0, a == LAST)
-
-        def fetch(r, h, q):
-            got = keep.tile([P, HALF], F32, name="got%d_%d_%d" % (r, h, q))
-            nc.scalar.activation(got[:], dx[h][:].indirect(token_slot[r][:, q * HALF // 16 : (q + 1) * HALF // 16]), COPY)
-            return got
-
-        def fetch_add(h, q, before):
-            total = keep.tile([P, HALF], F32, name="third%d_%d" % (h, q))
-            nc.vector.tensor_tensor(total[:], dx[h][:].indirect(token_slot[2][:, q * HALF // 16 : (q + 1) * HALF // 16]), before, ADD)
-            return total
-
-        def add(x, y, name):
-            total = keep.tile([P, HALF], F32, name=name)
-            nc.vector.tensor_tensor(total[:], x, y, ADD)
-            return total
-
-        def store(total, h, q):
-            nc.sync.dma_start(out=out[P * h : P * (h + 1), q * HALF : (q + 1) * HALF], in_=total[:])
-
-        got = {}
-        for r, h, q in ((0, 0, 1), (0, 1, 1), (0, 0, 0), (1, 0, 0), (0, 1, 0), (1, 1, 0), (1, 0, 1), (1, 1, 1)):
-            got[r, h, q] = fetch(r, h, q)
-        a0 = fetch_add(0, 0, ds_first[:, 0, :])
-        a1 = fetch_add(1, 0, ds_first[:, 1, :])
-        b0 = fetch_add(0, 1, got[0, 0, 1][:])
-        b1 = fetch_add(1, 1, got[0, 1, 1][:])
-        a0 = add(a0[:], got[0, 0, 0][:], "a0x")
-        b0 = add(ds_second[:, :HALF], b0[:], "b0x")
-        a0 = add(a0[:], got[1, 0, 0][:], "a0y")
-        store(a0, 0, 0)
-        a1 = add(a1[:], got[0, 1, 0][:], "a1x")
-        b1 = add(ds_second[:, HALF:], b1[:], "b1x")
-        a1 = add(a1[:], got[1, 1, 0][:], "a1y")
-        store(a1, 1, 0)
-        b0 = add(b0[:], got[1, 0, 1][:], "b0y")
-        store(b0, 0, 1)
-        b1 = add(b1[:], got[1, 1, 1][:], "b1y")
-        store(b1, 1, 1)
+                product(ds[1][:, h, :P], E, h, a, d_codes[a][:, HALF:], d_exp[a][:, HALF:], a == 0, a == LAST)
+            for a in range(PASSES):
+                product(ds[1][:, h, P:], E, h, a, q_codes[:, a * P : (a + 1) * P], q_exp[:, a * P : (a + 1) * P], a == 0, a == LAST)
+        out_rows = out.rearrange("(h p) t -> p h t", p=P)
+        for q in range(2):
+            nc.vector.tensor_tensor(sums[1][q], ds[q][:], sums[0][q], ADD)
+        nc.vector.tensor_tensor(sums[2][0], sums[1][0], got[1][0], ADD)
+        nc.sync.dma_start(out=out_rows[:, :, :HALF], in_=sums[2][0])
+        for h in range(HALVES):
+            nc.vector.tensor_tensor(sums[2][1][:, h, :], sums[1][1][:, h, :], got[1][1][:, h, :], ADD)
+            nc.sync.dma_start(out=out_rows[:, h, HALF:], in_=sums[2][1][:, h, :])

@@ -68,11 +68,12 @@ def tile_moe_bds_lin_none_kernel(tc, dyT, w_words, w_scales, gate, offs, pos1, p
         for a in range(PASSES):
             for j in range(PACK):
                 nc.sync.dma_start(out=window[a, j][:, 0:T], in_=dy_rows[a, :, j, :])
-            if a == 0:
-                nc.sync.dma_start(out=gates[:], in_=gate[0:P, SPLIT:S])
+                if (a, j) == (0, 0):
+                    nc.sync.dma_start(out=gates[:, OWN - SPLIT :], in_=gate[0:P, OWN:S])
             if a == LAST:
                 with nc.allow_non_contiguous_dma(reason="one gate value a partition"):
                     nc.sync.dma_start(out=gate_cols[:], in_=gate[0, 0:SPLIT].rearrange("(b p) -> p b", p=P))
+        nc.sync.dma_start(out=gates[:, : OWN - SPLIT], in_=gate[0:P, SPLIT:OWN])
         for a in range(PASSES):
             nc.sync.dma_start(out=dy_last[:, a], in_=dy_rows[a, :, :, MOST:])
         s_src = w_scales.rearrange("e a f k -> f (e a) k")
@@ -127,9 +128,9 @@ def tile_moe_bds_lin_none_kernel(tc, dyT, w_words, w_scales, gate, offs, pos1, p
         def by_runs(rows):
             return rows.rearrange("p j (c i) -> p c j i", i=RUN)
 
-        placed = {"a1": 0, "t01": 0, "own_bf2": 6144, "b1": 9216, "t2": 8192}
+        placed = {"a1": 0, "t01": 0, "b1": 9216, "t2": 9216}
 
-        reused = {"c0": "own_bf0", "c1": "b0", "c2": "a2"}
+        reused = {"c0": "own_bf2", "c1": "b0", "c2": "a2"}
 
         def bf_tile(n, name, tag):
             if name in placed:
@@ -142,21 +143,17 @@ def tile_moe_bds_lin_none_kernel(tc, dyT, w_words, w_scales, gate, offs, pos1, p
                 nc.scalar.activation(rows[:, j, :], picked(a, j, c0, c1), COPY)
             return rows
 
-        def gate_and_round(rows, weights, name, engine=nc.vector):
+        def gate_and_round(rows, weights, name):
             n = rows.shape[2]
             g_bf = bf_tile(n, name, reused.get(name, name))
-            if name.startswith("own"):
-                spread = weights.unsqueeze(2).to_broadcast([P, n, PACK])
-                engine.tensor_tensor(g_bf[:].rearrange("p (c j) -> p c j", j=PACK), rows.rearrange("p j c -> p c j"), spread, MULT)
-                return g_bf
             spread = weights.rearrange("p (c i) -> p c i", i=RUN).unsqueeze(2).to_broadcast([P, n // RUN, PACK, RUN])
-            engine.tensor_tensor(woven(g_bf[:]), by_runs(rows), spread, MULT)
+            nc.vector.tensor_tensor(woven(g_bf[:]), by_runs(rows), spread, MULT)
             return g_bf
 
         def vector_gather(a):
             rows = keep.tile([P, PACK, S - OWN], F32, name="own_rows%d" % a, tag="own_rows%d" % a, align_bytes=64)
             for j in range(PACK):
-                nc.vector.tensor_copy(rows[:, j, :], picked(a, j, OWN, S))
+                nc.vector.tensor_tensor(rows[:, j, :], picked(a, j, OWN, S), gates[:, OWN - SPLIT :], MULT)
             return rows
 
         def gpsimd_round(rows, name, tag):
@@ -177,11 +174,10 @@ def tile_moe_bds_lin_none_kernel(tc, dyT, w_words, w_scales, gate, offs, pos1, p
         rows_c1 = scalar_gather(1, SPLIT, OWN)
         rows_b2 = [scalar_gather(2, c0, c0 + C) for c0 in (BANK, BANK + C)]
         rows_c2 = scalar_gather(2, SPLIT, OWN)
-        own_bf = []
-        for a in range(PASSES):
-            rows = vector_gather(a)
-            own_bf.append(gate_and_round(rows[:], gates[:, OWN - SPLIT :], "own_bf%d" % a, nc.gpsimd))
-        q_bf = gpsimd_round(dy_last[:], "q_bf", "own_rows2")
+        own = [vector_gather(a) for a in range(PASSES)]
+        own_bf = {}
+        for a, tag in ((2, "own_bf2"), (0, "own_rows2"), (1, "own_rows0")):
+            own_bf[a] = gpsimd_round(own[a][:].unsqueeze(1), "own_bf%d" % a, tag)
 
         c_gates = gates[:, : OWN - SPLIT]
         first_acc = [psum.tile([P, BANK], F32, name="first_acc%d" % h) for h in range(HALVES)]
@@ -203,11 +199,16 @@ def tile_moe_bds_lin_none_kernel(tc, dyT, w_words, w_scales, gate, offs, pos1, p
         a0 = gate_and_round(pass0[:, :, :BANK], gate_bank[0][:], "a0")
         b0 = gate_and_round(pass0[:, :, BANK:SPLIT], gate_bank[1][:], "b0")
         a1 = gate_and_round(rows_a1[:], gate_bank[0][:], "a1")
-        quantize(own_bf[0], 0, OWN, S)
+        quantize(own_bf[2], 2, OWN, S)
         quantize(a0, 0, 0, BANK)
         c0_bf = gate_and_round(pass0[:, :, SPLIT:], c_gates, "c0")
-        quantize(own_bf[1], 1, OWN, S)
+        quantize(own_bf[0], 0, OWN, S)
         quantize(b0, 0, BANK, SPLIT)
+        q_bf = bf_tile(PASSES * P, "q_bf", "a0")
+        nc.vector.tensor_copy(
+            q_bf[:].rearrange("p (a c i j) -> p a c j i", a=PASSES, i=RUN, j=PACK),
+            dy_last[:].rearrange("p a j (c i) -> p a c j i", i=RUN),
+        )
         quantize(c0_bf, 0, SPLIT, OWN)
         quantize(a1, 1, 0, BANK)
         first_pass(0)
@@ -217,7 +218,7 @@ def tile_moe_bds_lin_none_kernel(tc, dyT, w_words, w_scales, gate, offs, pos1, p
         t01 = gpsimd_round(dy_most[:, 0:2], "t01", "t01")
         a2 = gate_and_round(rows_a2[:], gate_bank[0][:], "a2")
         b1 = gate_and_round(rows_b1[:], gate_bank[1][:], "b1")
-        quantize(own_bf[2], 2, OWN, S)
+        quantize(own_bf[1], 1, OWN, S)
         c1_bf = gate_and_round(rows_c1[:], c_gates, "c1")
         own_acc = []
         for h in range(HALVES):

@@ -55,8 +55,8 @@ def tile_moe_bds_lin_none_kernel(tc, dyT, w_words, w_scales, gate, offs, pos1, p
         ident = keep.tile([P, P], F32, name="ident")
         make_identity(nc, ident[:])
 
-        gates = keep.tile([P, S - SPLIT], F32, name="gates")
-        gate_cols = keep.tile([P, SPLIT // P], F32, name="gate_cols")
+        gates = keep.tile([P, S - OWN], F32, name="gates")
+        gate_cols = keep.tile([P, OWN // P], F32, name="gate_cols")
         dy_most = keep.tile([P, PASSES, PACK, MOST], F32, name="dy_most")
         dy_last = keep.tile([P, PASSES, PACK, T - MOST], F32, name="dy_last")
         window = {}
@@ -69,22 +69,19 @@ def tile_moe_bds_lin_none_kernel(tc, dyT, w_words, w_scales, gate, offs, pos1, p
             for j in range(PACK):
                 nc.sync.dma_start(out=window[a, j][:, 0:T], in_=dy_rows[a, :, j, :])
                 if (a, j) == (0, 0):
-                    nc.sync.dma_start(out=gates[:, OWN - SPLIT :], in_=gate[0:P, OWN:S])
+                    nc.sync.dma_start(out=gates[:], in_=gate[0:P, OWN:S])
             if a == LAST:
                 with nc.allow_non_contiguous_dma(reason="one gate value a partition"):
-                    nc.sync.dma_start(out=gate_cols[:], in_=gate[0, 0:SPLIT].rearrange("(b p) -> p b", p=P))
-        nc.sync.dma_start(out=gates[:, : OWN - SPLIT], in_=gate[0:P, SPLIT:OWN])
+                    nc.sync.dma_start(out=gate_cols[:], in_=gate[0, 0:OWN].rearrange("(b p) -> p b", p=P))
         for a in range(PASSES):
             nc.sync.dma_start(out=dy_last[:, a], in_=dy_rows[a, :, :, MOST:])
         s_src = w_scales.rearrange("e a f k -> f (e a) k")
         for q in range(4):
             nc.sync.dma_start(out=w_exp[32 * q : 32 * q + 4, :, :].bitcast(I32), in_=s_src[4 * q : 4 * q + 4].bitcast(I32))
         w_src = w_words.rearrange("e a p b -> p (e a) b")
-        for e in range(E + 1):
-            g = slice(e * PASSES, (e + 1) * PASSES)
-            nc.sync.dma_start(out=w_codes[:, g, :].bitcast(I32), in_=w_src[:, g, :].bitcast(I32))
         for a in range(PASSES):
             nc.sync.dma_start(out=dy_most[:, a], in_=dy_rows[a, :, :, :MOST])
+        nc.sync.dma_start(out=w_codes[:].bitcast(I32), in_=w_src.bitcast(I32))
         for r, src in enumerate((pos1, pos2, pos3)):
             nc.sync.dma_start(token_slot[r][:], src)
 
@@ -95,13 +92,14 @@ def tile_moe_bds_lin_none_kernel(tc, dyT, w_words, w_scales, gate, offs, pos1, p
                 col = b * BANK // P + m
                 nc.tensor.transpose(bank[:, m * P : (m + 1) * P], gate_cols[:, col : col + 1].to_broadcast([P, P]), ident[:])
             gate_bank.append(bank)
+        own_acc = [psum.tile([P, BANK], F32, name="own_acc%d" % h, tag="own_acc%d" % h) for h in range(HALVES)]
+        c_gates = own_acc[0][:, S - OWN :]
+        nc.tensor.transpose(c_gates, gate_cols[:, SPLIT // P :].to_broadcast([P, P]), ident[:])
 
         dx = [keep.tile([P, S], F32, name="dx%d" % h) for h in range(HALVES)]
         codes = [keep.tile([P, S], U32, name="codes%d" % a, align_bytes=64) for a in range(PASSES)]
         exps = [keep.tile([P, S], U8, name="exps%d" % a, align_bytes=64) for a in range(PASSES)]
-        d_codes = [keep.tile([P, MOST], U32, name="d_codes%d" % a, align_bytes=64) for a in range(PASSES)]
         d_exp = [keep.tile([P, MOST], U8, name="d_exp%d" % a, align_bytes=64) for a in range(PASSES)]
-        q_codes = keep.tile([P, PASSES * P], U32, name="q_codes", align_bytes=64)
         q_exp = keep.tile([P, PASSES * P], U8, name="q_exp", align_bytes=64)
 
         def product(acc, e, h, a, rhs, rhs_exp, start, stop):
@@ -130,7 +128,7 @@ def tile_moe_bds_lin_none_kernel(tc, dyT, w_words, w_scales, gate, offs, pos1, p
 
         placed = {"a1": 0, "t01": 0, "b1": 9216, "t2": 9216}
 
-        reused = {"c0": "own_bf2", "c1": "b0", "c2": "a2"}
+        reused = {"c1": "b0", "c2": "a2"}
 
         def bf_tile(n, name, tag):
             if name in placed:
@@ -138,7 +136,7 @@ def tile_moe_bds_lin_none_kernel(tc, dyT, w_words, w_scales, gate, offs, pos1, p
             return keep.tile([P, n * PACK], BF16, name=name, tag=tag, align_bytes=64)
 
         def scalar_gather(a, c0, c1):
-            rows = keep.tile([P, PACK, c1 - c0], F32, name="rows%d_%d" % (a, c0), tag="rows%d_%d" % (a, c0))
+            rows = keep.tile([P, PACK, c1 - c0], F32, name="rows%d_%d" % (a, c0), tag="rows%d_%d" % (a, c0), align_bytes=64)
             for j in range(PACK):
                 nc.scalar.activation(rows[:, j, :], picked(a, j, c0, c1), COPY)
             return rows
@@ -153,7 +151,7 @@ def tile_moe_bds_lin_none_kernel(tc, dyT, w_words, w_scales, gate, offs, pos1, p
         def vector_gather(a):
             rows = keep.tile([P, PACK, S - OWN], F32, name="own_rows%d" % a, tag="own_rows%d" % a, align_bytes=64)
             for j in range(PACK):
-                nc.vector.tensor_tensor(rows[:, j, :], picked(a, j, OWN, S), gates[:, OWN - SPLIT :], MULT)
+                nc.vector.tensor_tensor(rows[:, j, :], picked(a, j, OWN, S), gates[:], MULT)
             return rows
 
         def gpsimd_round(rows, name, tag):
@@ -165,7 +163,7 @@ def tile_moe_bds_lin_none_kernel(tc, dyT, w_words, w_scales, gate, offs, pos1, p
             nc.vector.quantize_mx(out=codes[a][:, c0:c1].bitcast(FP8X4), scales=exps[a][:, c0:c1], in_=g_bf[:])
 
         def quantize_tokens(t_bf, a):
-            nc.vector.quantize_mx(out=d_codes[a][:].bitcast(FP8X4), scales=d_exp[a][:], in_=t_bf)
+            nc.vector.quantize_mx(out=d_codes[a].bitcast(FP8X4), scales=d_exp[a][:], in_=t_bf)
 
         pass0 = scalar_gather(0, 0, OWN)
         rows_a1 = scalar_gather(1, 0, BANK)
@@ -179,7 +177,6 @@ def tile_moe_bds_lin_none_kernel(tc, dyT, w_words, w_scales, gate, offs, pos1, p
         for a, tag in ((2, "own_bf2"), (0, "own_rows2"), (1, "own_rows0")):
             own_bf[a] = gpsimd_round(own[a][:].unsqueeze(1), "own_bf%d" % a, tag)
 
-        c_gates = gates[:, : OWN - SPLIT]
         first_acc = [psum.tile([P, BANK], F32, name="first_acc%d" % h) for h in range(HALVES)]
         third_acc = psum.tile([P, HALVES * P], F32, name="third_acc")
 
@@ -198,10 +195,10 @@ def tile_moe_bds_lin_none_kernel(tc, dyT, w_words, w_scales, gate, offs, pos1, p
 
         a0 = gate_and_round(pass0[:, :, :BANK], gate_bank[0][:], "a0")
         b0 = gate_and_round(pass0[:, :, BANK:SPLIT], gate_bank[1][:], "b0")
+        c0_bf = gate_and_round(pass0[:, :, SPLIT:], c_gates, "c0")
         a1 = gate_and_round(rows_a1[:], gate_bank[0][:], "a1")
         quantize(own_bf[2], 2, OWN, S)
         quantize(a0, 0, 0, BANK)
-        c0_bf = gate_and_round(pass0[:, :, SPLIT:], c_gates, "c0")
         quantize(own_bf[0], 0, OWN, S)
         quantize(b0, 0, BANK, SPLIT)
         q_bf = bf_tile(PASSES * P, "q_bf", "a0")
@@ -218,20 +215,17 @@ def tile_moe_bds_lin_none_kernel(tc, dyT, w_words, w_scales, gate, offs, pos1, p
         t01 = gpsimd_round(dy_most[:, 0:2], "t01", "t01")
         a2 = gate_and_round(rows_a2[:], gate_bank[0][:], "a2")
         b1 = gate_and_round(rows_b1[:], gate_bank[1][:], "b1")
-        quantize(own_bf[1], 1, OWN, S)
         c1_bf = gate_and_round(rows_c1[:], c_gates, "c1")
-        own_acc = []
+        quantize(own_bf[1], 1, OWN, S)
         for h in range(HALVES):
-            acc = psum.tile([P, S - OWN], F32, name="own_acc%d" % h, tag="own_acc%d" % h)
             for c0, c1 in ((OWN, OWN + P), (OWN + P, S)):
                 for a in range(PASSES):
-                    slot_product(acc[:, c0 - OWN : c1 - OWN], h, a, c0, c1, a == 0, a == LAST)
-            own_acc.append(acc)
+                    slot_product(own_acc[h][:, c0 - OWN : c1 - OWN], h, a, c0, c1, a == 0, a == LAST)
         quantize(a2, 2, 0, BANK)
         first_pass(2)
         for h in range(HALVES):
             nc.scalar.copy(out=dx[h][:, :BANK], in_=first_acc[h][:])
-        nc.scalar.copy(out=dx[1][:, OWN:], in_=own_acc[1][:])
+        nc.scalar.copy(out=dx[1][:, OWN:], in_=own_acc[1][:, : S - OWN])
         quantize(c1_bf, 1, SPLIT, OWN)
         quantize(b1, 1, BANK, SPLIT)
         second_acc = [psum.tile([P, BANK], F32, name="second_acc0"), psum.tile([P, BANK], F32, name="second_acc1", tag="gate_bank0")]
@@ -242,22 +236,25 @@ def tile_moe_bds_lin_none_kernel(tc, dyT, w_words, w_scales, gate, offs, pos1, p
 
         t2 = gpsimd_round(dy_most[:, 2:3], "t2", "t2")
         b2 = [gate_and_round(rows_b2[0][:], gate_bank[1][:, :C], "b2_0")]
-        nc.vector.tensor_copy(dx[0][:, OWN:], own_acc[0][:])
         b2.append(gate_and_round(rows_b2[1][:], gate_bank[1][:, C:], "b2_1"))
         quantize(b2[0], 2, BANK, BANK + C)
         both_halves(second_acc[0], LAST, BANK, BANK + C)
         leave(second_acc[0], BANK, BANK + C)
-        c2_bf = gate_and_round(rows_c2[:], c_gates, "c2")
         quantize(b2[1], 2, BANK + C, SPLIT)
         both_halves(second_acc[1], LAST, BANK + C, SPLIT)
         leave(second_acc[1], BANK + C, SPLIT)
+        c2_bf = gate_and_round(rows_c2[:], c_gates, "c2")
+        nc.vector.tensor_copy(dx[0][:, OWN:], own_acc[0][:, : S - OWN])
         quantize(c2_bf, 2, SPLIT, OWN)
         both_halves(third_acc, LAST, SPLIT, OWN)
         leave(third_acc, SPLIT, OWN)
+        t_codes = keep.tile([P, (PASSES + 1) * MOST], U32, name="t_codes", tag="rows%d_%d" % (LAST, SPLIT), align_bytes=64)
+        d_codes = [t_codes[:, a * MOST : (a + 1) * MOST] for a in range(PASSES)]
+        q_codes = t_codes[:, PASSES * MOST :]
         quantize_tokens(t01[:, : MOST * PACK], 0)
         quantize_tokens(t01[:, MOST * PACK :], 1)
         quantize_tokens(t2[:], 2)
-        nc.vector.quantize_mx(out=q_codes[:].bitcast(FP8X4), scales=q_exp[:], in_=q_bf[:])
+        nc.vector.quantize_mx(out=q_codes.bitcast(FP8X4), scales=q_exp[:], in_=q_bf[:])
         ds = [psum.tile([P, HALVES, HALF], F32, name="ds%d" % q, tag=tag) for q, tag in enumerate(("gate_bank1", "own_acc0"))]
         for h in range(HALVES):
             for a in range(PASSES):
@@ -266,7 +263,7 @@ def tile_moe_bds_lin_none_kernel(tc, dyT, w_words, w_scales, gate, offs, pos1, p
         def fetched(r, h, q):
             return dx[h][:].indirect(token_slot[r][:, q * HALF // 16 : (q + 1) * HALF // 16])
 
-        got_all = keep.tile([P, 4, HALVES, HALF], F32, name="got_all", tag="rows1_0")
+        got_all = keep.tile([P, 4, HALVES, HALF], F32, name="got_all", tag="rows1_0", align_bytes=64)
         got = [[got_all[:, 2 * r + q] for q in range(2)] for r in range(2)]
         opening = over.tile([P, 3, 2, HALVES, HALF], F32, name="opening", align_bytes=64, offset=0)
         sums = [[opening[:, r, q] for q in range(2)] for r in range(3)]

@@ -23,14 +23,15 @@ MULT = mybir.AluOpType.mult
 ADD = mybir.AluOpType.add
 COPY = mybir.ActivationFunctionType.Copy
 
-HALF = T // 2
 LAST = PASSES - 1
 HALVES = K // P
+HALF = T // 2
 RUN = 2
 BANK = 512
-SPLIT = 2 * BANK
-OWN = SPLIT + P
-MOST = 3 * P
+OWN = 5 * C
+SPARE = 16
+ROW_STEP = 704
+LAST_WIDTH = (PACK - 1) * ROW_STEP + 2 * T
 
 
 def tile_moe_bds_lin_none_kernel(tc, dyT, w_words, w_scales, gate, offs, pos1, pos2, pos3, out):
@@ -38,7 +39,6 @@ def tile_moe_bds_lin_none_kernel(tc, dyT, w_words, w_scales, gate, offs, pos1, p
     with ExitStack() as ctx:
         lists = ctx.enter_context(tc.tile_pool(name="lists", bufs=1))
         keep = ctx.enter_context(tc.tile_pool(name="keep", bufs=1))
-        over = ctx.enter_context(tc.tile_pool(name="over", bufs=1))
         psum = ctx.enter_context(tc.psum_pool(name="psum", bufs=1))
 
         slot_token = lists.tile([P, S // 16], U16, name="slot_token")
@@ -55,235 +55,208 @@ def tile_moe_bds_lin_none_kernel(tc, dyT, w_words, w_scales, gate, offs, pos1, p
         ident = keep.tile([P, P], F32, name="ident")
         make_identity(nc, ident[:])
 
-        gates = keep.tile([P, S - OWN], F32, name="gates")
-        gate_cols = keep.tile([P, OWN // P], F32, name="gate_cols")
-        dy_most = keep.tile([P, PASSES, PACK, MOST], F32, name="dy_most")
-        dy_last = keep.tile([P, PASSES, PACK, T - MOST], F32, name="dy_last")
+        last_rows = keep.tile([P, LAST_WIDTH], F32, name="last_rows")
         window = {}
-        for a in range(PASSES):
+        for a, most in ((0, 2 * BANK), (1, BANK)):
             for j in range(PACK):
-                window[a, j] = keep.tile([P, (OWN if a == 0 else T) + 16], F32, name="window%d_%d" % (a, j))
+                window[a, j] = keep.tile([P, most + SPARE], F32, name="window%d_%d" % (a, j))
+        tokens = [keep.tile([P, PACK, T], F32, name="tokens%d" % a, tag="tokens%d" % a, align_bytes=64) for a in range(LAST)]
+        gates = [keep.tile([P, BANK], F32, name="gates0"), keep.tile([P, OWN - BANK], F32, name="gates1")]
+        gate_cols = keep.tile([P, S // P], F32, name="gate_cols")
 
         nc.sync.dma_start(slot_token[:], offs)
-        for a in range(PASSES):
-            for j in range(PACK):
-                nc.sync.dma_start(out=window[a, j][:, 0:T], in_=dy_rows[a, :, j, :])
-                if (a, j) == (0, 0):
-                    nc.sync.dma_start(out=gates[:], in_=gate[0:P, OWN:S])
-            if a == LAST:
-                with nc.allow_non_contiguous_dma(reason="one gate value a partition"):
-                    nc.sync.dma_start(out=gate_cols[:], in_=gate[0, 0:OWN].rearrange("(b p) -> p b", p=P))
-        for a in range(PASSES):
-            nc.sync.dma_start(out=dy_last[:, a], in_=dy_rows[a, :, :, MOST:])
+        for j in range(PACK):
+            nc.sync.dma_start(out=last_rows[:, j * ROW_STEP : j * ROW_STEP + T], in_=dy_rows[LAST, :, j, :])
+        for j in range(PACK):
+            nc.sync.dma_start(out=window[0, j][:, 0:T], in_=dy_rows[0, :, j, :])
+            if j == 0:
+                nc.sync.dma_start(out=gates[0][:], in_=gate[0:P, 0:BANK])
+        nc.sync.dma_start(out=tokens[0][:], in_=dy_rows[0])
+        with nc.allow_non_contiguous_dma(reason="one gate value a partition"):
+            nc.sync.dma_start(out=gate_cols[:], in_=gate[0, :].rearrange("(b p) -> p b", p=P))
+        for j in range(PACK):
+            nc.sync.dma_start(out=window[1, j][:, 0:T], in_=dy_rows[1, :, j, :])
+        nc.sync.dma_start(out=tokens[1][:], in_=dy_rows[1])
+        nc.sync.dma_start(out=gates[1][:], in_=gate[0:P, BANK:OWN])
         s_src = w_scales.rearrange("e a f k -> f (e a) k")
         for q in range(4):
             nc.sync.dma_start(out=w_exp[32 * q : 32 * q + 4, :, :].bitcast(I32), in_=s_src[4 * q : 4 * q + 4].bitcast(I32))
-        w_src = w_words.rearrange("e a p b -> p (e a) b")
-        for a in range(PASSES):
-            nc.sync.dma_start(out=dy_most[:, a], in_=dy_rows[a, :, :, :MOST])
-        nc.sync.dma_start(out=w_codes[:].bitcast(I32), in_=w_src.bitcast(I32))
+        nc.sync.dma_start(out=w_codes[:].bitcast(I32), in_=w_words.rearrange("e a p b -> p (e a) b").bitcast(I32))
         for r, src in enumerate((pos1, pos2, pos3)):
             nc.sync.dma_start(token_slot[r][:], src)
 
-        gate_bank = []
-        for b in range(2):
-            bank = psum.tile([P, BANK], F32, name="gate_bank%d" % b, tag="gate_bank%d" % b)
+        gate_bank = {}
+        for b in range(S // BANK):
+            gate_bank[b] = psum.tile([P, BANK], F32, name="gate_bank%d" % b, tag="gate_bank%d" % b)
             for m in range(BANK // P):
                 col = b * BANK // P + m
-                nc.tensor.transpose(bank[:, m * P : (m + 1) * P], gate_cols[:, col : col + 1].to_broadcast([P, P]), ident[:])
-            gate_bank.append(bank)
-        own_acc = [psum.tile([P, BANK], F32, name="own_acc%d" % h, tag="own_acc%d" % h) for h in range(HALVES)]
-        c_gates = own_acc[0][:, S - OWN :]
-        nc.tensor.transpose(c_gates, gate_cols[:, SPLIT // P :].to_broadcast([P, P]), ident[:])
+                nc.tensor.transpose(gate_bank[b][:, m * P : (m + 1) * P], gate_cols[:, col : col + 1].to_broadcast([P, P]), ident[:])
 
-        dx = [keep.tile([P, S], F32, name="dx%d" % h) for h in range(HALVES)]
-        codes = [keep.tile([P, S], U32, name="codes%d" % a, align_bytes=64) for a in range(PASSES)]
-        exps = [keep.tile([P, S], U8, name="exps%d" % a, align_bytes=64) for a in range(PASSES)]
-        d_exp = [keep.tile([P, MOST], U8, name="d_exp%d" % a, align_bytes=64) for a in range(PASSES)]
-        q_exp = keep.tile([P, PASSES * P], U8, name="q_exp", align_bytes=64)
+        def picked(a, j, c0, c1, width):
+            source = last_rows[:, j * ROW_STEP : j * ROW_STEP + width] if a == LAST else window[a, j][:]
+            return source.indirect(slot_token[:, c0 // 16 : c1 // 16])
 
-        def product(acc, e, h, a, rhs, rhs_exp, start, stop):
+        def rows_tile(a, c0, c1, tag):
+            return keep.tile([P, PACK, c1 - c0], F32, name="rows%d_%d" % (a, c0), tag=tag, align_bytes=64)
+
+        def scalar_gather(a, c0, c1, tag):
+            rows = rows_tile(a, c0, c1, tag)
+            for j in range(PACK):
+                nc.scalar.activation(rows[:, j, :], picked(a, j, c0, c1, T), COPY)
+            return rows
+
+        def vector_gather(c0, c1):
+            rows = rows_tile(LAST, c0, c1, "own%d" % c0)
+            for j in range(PACK):
+                nc.vector.tensor_copy(rows[:, j, :], picked(LAST, j, c0, c1, ROW_STEP if c0 == 0 else LAST_WIDTH - j * ROW_STEP))
+            return rows
+
+        def rounded_tile(n, name, tag):
+            return keep.tile([P, n * PACK], BF16, name=name, tag=tag, align_bytes=64)
+
+        def vector_product(rows, c0, target):
+            n = rows.shape[2]
+            weights = gate_bank[c0 // BANK][:, c0 % BANK : c0 % BANK + n]
+            spread = weights.rearrange("p (c i) -> p c i", i=RUN).unsqueeze(2).to_broadcast([P, n // RUN, PACK, RUN])
+            woven = target.rearrange("p (c i j) -> p c j i", i=RUN, j=PACK)
+            nc.vector.tensor_tensor(woven, rows.rearrange("p j (c i) -> p c j i", i=RUN), spread, MULT)
+
+        def gpsimd_product(rows, weights, name, tag):
+            n = rows.shape[2]
+            target = rounded_tile(n, name, tag)
+            spread = weights.unsqueeze(2).to_broadcast([P, n, PACK])
+            nc.gpsimd.tensor_tensor(target[:].rearrange("p (c j) -> p c j", j=PACK), rows.rearrange("p j c -> p c j"), spread, MULT)
+            return target
+
+        token_bf = [rounded_tile(T, "token_bf%d" % a, "token_bf%d" % a) for a in range(PASSES)]
+
+        def gpsimd_round(a, rows):
+            nc.gpsimd.tensor_scalar(token_bf[a][:].rearrange("p (t j) -> p t j", j=PACK), rows.rearrange("p j t -> p t j"), 1.0, 0.0, MULT, ADD)
+
+        coded = {}
+
+        def quantize(source, name, parts, tag=None):
+            n = source.shape[1] // PACK
+            codes = keep.tile([P, n], U32, name="codes_" + name, tag=tag or "codes_" + name, align_bytes=64)
+            exps = keep.tile([P, n], U8, name="exps_" + name, align_bytes=64)
+            nc.vector.quantize_mx(out=codes[:].bitcast(FP8X4), scales=exps[:], in_=source)
+            width = n // len(parts)
+            for i, part in enumerate(parts):
+                coded[part] = (codes[:, i * width : (i + 1) * width], exps[:, i * width : (i + 1) * width])
+
+        def product(acc, e, h, a, start, stop):
             g = e * PASSES + a
             nc.tensor.matmul_mx(
                 out=acc,
                 lhsT=w_codes[:, g, 2 * P * h : 2 * P * (h + 1)].bitcast(FP4X4),
                 lhsT_scale=w_exp[:, g, P * h : P * (h + 1)],
-                rhs=rhs.bitcast(FP8X4),
-                rhs_scale=rhs_exp,
+                rhs=coded[a, e][0].bitcast(FP8X4),
+                rhs_scale=coded[a, e][1],
                 start=start,
                 stop=stop,
             )
 
-        def slot_product(acc, h, a, c0, c1, start, stop):
-            product(acc, c0 // C, h, a, codes[a][:, c0:c1], exps[a][:, c0:c1], start, stop)
-
-        def picked(a, j, c0, c1):
-            return window[a, j][:].indirect(slot_token[:, c0 // 16 : c1 // 16])
-
-        def woven(g_bf):
-            return g_bf.rearrange("p (c i j) -> p c j i", i=RUN, j=PACK)
-
-        def by_runs(rows):
-            return rows.rearrange("p j (c i) -> p c j i", i=RUN)
-
-        placed = {"a1": 0, "t01": 0, "b1": 9216, "t2": 9216}
-
-        reused = {"c1": "b0", "c2": "a2"}
-
-        def bf_tile(n, name, tag):
-            if name in placed:
-                return over.tile([P, n * PACK], BF16, name=name, align_bytes=64, offset=placed[name])
-            return keep.tile([P, n * PACK], BF16, name=name, tag=tag, align_bytes=64)
-
-        def scalar_gather(a, c0, c1):
-            rows = keep.tile([P, PACK, c1 - c0], F32, name="rows%d_%d" % (a, c0), tag="rows%d_%d" % (a, c0), align_bytes=64)
-            for j in range(PACK):
-                nc.scalar.activation(rows[:, j, :], picked(a, j, c0, c1), COPY)
-            return rows
-
-        def gate_and_round(rows, weights, name):
-            n = rows.shape[2]
-            g_bf = bf_tile(n, name, reused.get(name, name))
-            spread = weights.rearrange("p (c i) -> p c i", i=RUN).unsqueeze(2).to_broadcast([P, n // RUN, PACK, RUN])
-            nc.vector.tensor_tensor(woven(g_bf[:]), by_runs(rows), spread, MULT)
-            return g_bf
-
-        def vector_gather(a):
-            rows = keep.tile([P, PACK, S - OWN], F32, name="own_rows%d" % a, tag="own_rows%d" % a, align_bytes=64)
-            for j in range(PACK):
-                nc.vector.tensor_tensor(rows[:, j, :], picked(a, j, OWN, S), gates[:], MULT)
-            return rows
-
-        def gpsimd_round(rows, name, tag):
-            t_bf = bf_tile(rows.shape[1] * rows.shape[3], name, tag)
-            nc.gpsimd.tensor_scalar(t_bf[:].rearrange("p (a t j) -> p a t j", a=rows.shape[1], j=PACK), rows.rearrange("p a j t -> p a t j"), 1.0, 0.0, MULT, ADD)
-            return t_bf
-
-        def quantize(g_bf, a, c0, c1):
-            nc.vector.quantize_mx(out=codes[a][:, c0:c1].bitcast(FP8X4), scales=exps[a][:, c0:c1], in_=g_bf[:])
-
-        def quantize_tokens(t_bf, a):
-            nc.vector.quantize_mx(out=d_codes[a].bitcast(FP8X4), scales=d_exp[a][:], in_=t_bf)
-
-        pass0 = scalar_gather(0, 0, OWN)
-        rows_a1 = scalar_gather(1, 0, BANK)
-        rows_a2 = scalar_gather(2, 0, BANK)
-        rows_b1 = scalar_gather(1, BANK, SPLIT)
-        rows_c1 = scalar_gather(1, SPLIT, OWN)
-        rows_b2 = [scalar_gather(2, c0, c0 + C) for c0 in (BANK, BANK + C)]
-        rows_c2 = scalar_gather(2, SPLIT, OWN)
-        own = [vector_gather(a) for a in range(PASSES)]
-        own_bf = {}
-        for a, tag in ((2, "own_bf2"), (0, "own_rows2"), (1, "own_rows0")):
-            own_bf[a] = gpsimd_round(own[a][:].unsqueeze(1), "own_bf%d" % a, tag)
-
-        first_acc = [psum.tile([P, BANK], F32, name="first_acc%d" % h) for h in range(HALVES)]
-        third_acc = psum.tile([P, HALVES * P], F32, name="third_acc")
-
-        def first_pass(a):
+        def pair_pass(acc, e0, a, start, stop):
             for h in range(HALVES):
                 for i in range(2):
-                    slot_product(first_acc[h][:, i * C : (i + 1) * C], h, a, i * C, (i + 1) * C, a == 0 and i == 0, a == LAST and i == 1)
+                    product(acc[h][:, i * C : (i + 1) * C], e0 + i, h, a, start and i == 0, stop and i == 1)
 
-        def both_halves(acc, a, c0, c1):
+        def expert_pass(acc, e, a, start, stop):
             for h in range(HALVES):
-                slot_product(acc[:, h * (c1 - c0) : (h + 1) * (c1 - c0)], h, a, c0, c1, a == 0 and h == 0, a == LAST and h == HALVES - 1)
+                product(acc[:, h * C : (h + 1) * C], e, h, a, start and h == 0, stop and h == HALVES - 1)
 
-        def leave(acc, c0, c1):
-            for h in range(HALVES):
-                nc.scalar.copy(out=dx[h][:, c0:c1], in_=acc[:, h * (c1 - c0) : (h + 1) * (c1 - c0)])
+        rows_f = scalar_gather(LAST, OWN, S, "rows_f")
+        rows_a = scalar_gather(0, 0, 2 * BANK, "rows_a")
+        rows_b = scalar_gather(1, 0, BANK, "rows_b")
+        own = [vector_gather(0, BANK), vector_gather(BANK, OWN)]
 
-        a0 = gate_and_round(pass0[:, :, :BANK], gate_bank[0][:], "a0")
-        b0 = gate_and_round(pass0[:, :, BANK:SPLIT], gate_bank[1][:], "b0")
-        c0_bf = gate_and_round(pass0[:, :, SPLIT:], c_gates, "c0")
-        a1 = gate_and_round(rows_a1[:], gate_bank[0][:], "a1")
-        quantize(own_bf[2], 2, OWN, S)
-        quantize(a0, 0, 0, BANK)
-        quantize(own_bf[0], 0, OWN, S)
-        quantize(b0, 0, BANK, SPLIT)
-        q_bf = bf_tile(PASSES * P, "q_bf", "a0")
-        nc.vector.tensor_copy(
-            q_bf[:].rearrange("p (a c i j) -> p a c j i", a=PASSES, i=RUN, j=PACK),
-            dy_last[:].rearrange("p a j (c i) -> p a c j i", i=RUN),
-        )
-        quantize(c0_bf, 0, SPLIT, OWN)
-        quantize(a1, 1, 0, BANK)
-        first_pass(0)
-        first_pass(1)
-        both_halves(third_acc, 0, SPLIT, OWN)
+        gpsimd_round(LAST, last_rows[:, : PACK * ROW_STEP].rearrange("p (j w) -> p j w", j=PACK)[:, :, 0:T])
+        own_0 = gpsimd_product(own[0][:], gates[0][:], "own_0", "own_0")
+        gpsimd_round(0, tokens[0][:])
+        gpsimd_round(1, tokens[1][:])
+        rows_c = scalar_gather(1, BANK, 2 * BANK, "tokens0")
+        own_2 = gpsimd_product(own[1][:, :, 0:C], gates[1][:, 0:C], "own_2", "own_2")
 
-        t01 = gpsimd_round(dy_most[:, 0:2], "t01", "t01")
-        a2 = gate_and_round(rows_a2[:], gate_bank[0][:], "a2")
-        b1 = gate_and_round(rows_b1[:], gate_bank[1][:], "b1")
-        c1_bf = gate_and_round(rows_c1[:], c_gates, "c1")
-        quantize(own_bf[1], 1, OWN, S)
-        for h in range(HALVES):
-            for c0, c1 in ((OWN, OWN + P), (OWN + P, S)):
-                for a in range(PASSES):
-                    slot_product(own_acc[h][:, c0 - OWN : c1 - OWN], h, a, c0, c1, a == 0, a == LAST)
-        quantize(a2, 2, 0, BANK)
-        first_pass(2)
-        for h in range(HALVES):
-            nc.scalar.copy(out=dx[h][:, :BANK], in_=first_acc[h][:])
-        nc.scalar.copy(out=dx[1][:, OWN:], in_=own_acc[1][:, : S - OWN])
-        quantize(c1_bf, 1, SPLIT, OWN)
-        quantize(b1, 1, BANK, SPLIT)
-        second_acc = [psum.tile([P, BANK], F32, name="second_acc0"), psum.tile([P, BANK], F32, name="second_acc1", tag="gate_bank0")]
+        bf_a = rounded_tile(2 * BANK, "bf_a", "bf_a")
+        bf_b = rounded_tile(BANK, "bf_b", "bf_b")
         for i in range(2):
-            for a in range(LAST):
-                both_halves(second_acc[i], a, BANK + i * C, BANK + (i + 1) * C)
-        both_halves(third_acc, 1, SPLIT, OWN)
+            vector_product(rows_a[:, :, i * BANK : (i + 1) * BANK], i * BANK, bf_a[:, i * BANK * PACK : (i + 1) * BANK * PACK])
+        vector_product(rows_b[:], 0, bf_b[:])
+        rows_d = scalar_gather(0, 2 * BANK, S, "rows_a")
+        rows_e = [scalar_gather(1, 4 * C, 5 * C, "rows_b")]
+        quantize(own_2[:], "own_2", [(2, 2)])
+        quantize(bf_a[:], "a", [(0, 0), (0, 1), (0, 2), (0, 3)])
+        quantize(own_0[:], "own_0", [(2, 0), (2, 1)])
+        quantize(bf_b[:], "b", [(1, 0), (1, 1)])
+        first_acc = [psum.tile([P, BANK], F32, name="first_acc%d" % h, tag="first_acc%d" % h) for h in range(HALVES)]
+        second_acc = [psum.tile([P, BANK], F32, name="second_acc%d" % h) for h in range(HALVES)]
+        for a in (0, 2, 1):
+            pair_pass(first_acc, 0, a, a == 0, a == 1)
+        pair_pass(second_acc, 2, 0, True, False)
 
-        t2 = gpsimd_round(dy_most[:, 2:3], "t2", "t2")
-        b2 = [gate_and_round(rows_b2[0][:], gate_bank[1][:, :C], "b2_0")]
-        b2.append(gate_and_round(rows_b2[1][:], gate_bank[1][:, C:], "b2_1"))
-        quantize(b2[0], 2, BANK, BANK + C)
-        both_halves(second_acc[0], LAST, BANK, BANK + C)
-        leave(second_acc[0], BANK, BANK + C)
-        quantize(b2[1], 2, BANK + C, SPLIT)
-        both_halves(second_acc[1], LAST, BANK + C, SPLIT)
-        leave(second_acc[1], BANK + C, SPLIT)
-        c2_bf = gate_and_round(rows_c2[:], c_gates, "c2")
-        nc.vector.tensor_copy(dx[0][:, OWN:], own_acc[0][:, : S - OWN])
-        quantize(c2_bf, 2, SPLIT, OWN)
-        both_halves(third_acc, LAST, SPLIT, OWN)
-        leave(third_acc, SPLIT, OWN)
-        t_codes = keep.tile([P, (PASSES + 1) * MOST], U32, name="t_codes", tag="rows%d_%d" % (LAST, SPLIT), align_bytes=64)
-        d_codes = [t_codes[:, a * MOST : (a + 1) * MOST] for a in range(PASSES)]
-        q_codes = t_codes[:, PASSES * MOST :]
-        quantize_tokens(t01[:, : MOST * PACK], 0)
-        quantize_tokens(t01[:, MOST * PACK :], 1)
-        quantize_tokens(t2[:], 2)
-        nc.vector.quantize_mx(out=q_codes.bitcast(FP8X4), scales=q_exp[:], in_=q_bf[:])
-        ds = [psum.tile([P, HALVES, HALF], F32, name="ds%d" % q, tag=tag) for q, tag in enumerate(("gate_bank1", "own_acc0"))]
-        for h in range(HALVES):
-            for a in range(PASSES):
-                product(ds[0][:, h, :], E, h, a, d_codes[a][:, :HALF], d_exp[a][:, :HALF], a == 0, a == LAST)
+        own_3 = gpsimd_product(own[1][:, :, C:BANK], gates[1][:, C:BANK], "own_3", "bf_b")
+        bf_c = rounded_tile(BANK, "bf_c", "own_2")
+        bf_fe = rounded_tile(BANK, "bf_fe", "own_0")
+        vector_product(rows_c[:], BANK, bf_c[:])
+        rows_e.append(scalar_gather(1, 5 * C, S, "tokens0"))
+        vector_product(rows_f[:], OWN, bf_fe[:, : C * PACK])
+        quantize(own_3[:], "own_3", [(2, 3)])
+        quantize(token_bf[LAST][:], "t2", [(LAST, E)], "bf_a")
+        quantize(bf_c[:], "c", [(1, 2), (1, 3)])
+        for a in (2, 1):
+            pair_pass(second_acc, 2, a, False, a == 1)
+        ds = [psum.tile([P, T], F32, name="ds0", tag="gate_bank1")]
+        product(ds[0][:], E, 0, LAST, True, False)
 
-        def fetched(r, h, q):
-            return dx[h][:].indirect(token_slot[r][:, q * HALF // 16 : (q + 1) * HALF // 16])
+        own_4 = gpsimd_product(own[1][:, :, BANK:], gates[1][:, BANK:], "own_4", "own_2")
+        bf_d = rounded_tile(BANK, "bf_d", "bf_b")
+        vector_product(rows_d[:], 2 * BANK, bf_d[:])
+        vector_product(rows_e[0][:], 4 * C, bf_fe[:, C * PACK :])
+        quantize(own_4[:], "own_4", [(2, 4)])
+        quantize(bf_d[:], "d", [(0, 4), (0, 5)])
+        quantize(bf_fe[:], "fe", [(2, 5), (1, 4)])
+        late_acc = [psum.tile([P, BANK], F32, name="late_acc0"), psum.tile([P, BANK], F32, name="late_acc1", tag="gate_bank0")]
+        for a in (2, 0, 1):
+            expert_pass(late_acc[0], 4, a, a == 2, a == 1)
+        for a in (0, 2):
+            expert_pass(late_acc[1], 5, a, a == 0, False)
 
-        got_all = keep.tile([P, 4, HALVES, HALF], F32, name="got_all", tag="rows1_0", align_bytes=64)
-        got = [[got_all[:, 2 * r + q] for q in range(2)] for r in range(2)]
-        opening = over.tile([P, 3, 2, HALVES, HALF], F32, name="opening", align_bytes=64, offset=0)
-        sums = [[opening[:, r, q] for q in range(2)] for r in range(3)]
-        for r in range(2):
-            for q in range(2):
-                for h in range(HALVES):
-                    nc.scalar.activation(got[r][q][:, h, :], fetched(r, h, q), COPY)
-        for q in range(2):
+        dx = [keep.tile([P, S], F32, name="dx%d" % h, tag=tag, align_bytes=64) for h, tag in enumerate(("own0", "tokens1"))]
+        for i, acc in enumerate((first_acc, second_acc)):
             for h in range(HALVES):
-                nc.vector.tensor_tensor(sums[0][q][:, h, :], fetched(2, h, q), got[0][q][:, h, :], ADD)
+                nc.scalar.copy(out=dx[h][:, i * BANK : (i + 1) * BANK], in_=acc[h][:])
         for h in range(HALVES):
-            for a in range(PASSES):
-                product(ds[1][:, h, :P], E, h, a, d_codes[a][:, HALF:], d_exp[a][:, HALF:], a == 0, a == LAST)
-            for a in range(PASSES):
-                product(ds[1][:, h, P:], E, h, a, q_codes[:, a * P : (a + 1) * P], q_exp[:, a * P : (a + 1) * P], a == 0, a == LAST)
+            nc.scalar.copy(out=dx[h][:, 4 * C : 5 * C], in_=late_acc[0][:, h * C : (h + 1) * C])
+
+        bf_g = rounded_tile(C, "bf_g", "own_2")
+        vector_product(rows_e[1][:], 5 * C, bf_g[:])
+        quantize(token_bf[0][:], "t0", [(0, E)], "bf_b")
+        quantize(bf_g[:], "g", [(1, 5)])
+        quantize(token_bf[1][:], "t1", [(1, E)], "own_0")
+        expert_pass(late_acc[1], 5, 1, False, True)
+        for h in range(HALVES):
+            nc.scalar.copy(out=dx[h][:, 5 * C :], in_=late_acc[1][:, h * C : (h + 1) * C])
+        ds.append(psum.tile([P, T], F32, name="ds1", tag="first_acc0"))
+        product(ds[0][:], E, 0, 0, False, False)
+        product(ds[0][:], E, 0, 1, False, True)
+        for a in range(PASSES):
+            product(ds[1][:], E, 1, a, a == 0, a == LAST)
+
+        def fetched(r, h, t0, t1):
+            return dx[h][:].indirect(token_slot[r][:, t0 // 16 : t1 // 16])
+
+        got = keep.tile([P, 2, HALVES, T], F32, name="got", tag="rows_b", align_bytes=64)
+        sums = keep.tile([P, 3, HALVES, T], F32, name="sums", tag="rows_a", align_bytes=64)
         out_rows = out.rearrange("(h p) t -> p h t", p=P)
-        for q in range(2):
-            nc.vector.tensor_tensor(sums[1][q], ds[q][:], sums[0][q], ADD)
-        nc.vector.tensor_tensor(sums[2][0], sums[1][0], got[1][0], ADD)
-        nc.sync.dma_start(out=out_rows[:, :, :HALF], in_=sums[2][0])
+        quarters = [(h, t0, t0 + HALF) for h in range(HALVES) for t0 in (0, HALF)]
+        closing = [(0, 0, T)] + quarters[2:]
+        for r, pieces in enumerate((quarters, closing)):
+            for h, t0, t1 in pieces:
+                nc.scalar.activation(got[:, r, h, t0:t1], fetched(r, h, t0, t1), COPY)
+        for h, t0, t1 in quarters:
+            nc.vector.tensor_tensor(sums[:, 0, h, t0:t1], fetched(2, h, t0, t1), got[:, 0, h, t0:t1], ADD)
         for h in range(HALVES):
-            nc.vector.tensor_tensor(sums[2][1][:, h, :], sums[1][1][:, h, :], got[1][1][:, h, :], ADD)
-            nc.sync.dma_start(out=out_rows[:, h, HALF:], in_=sums[2][1][:, h, :])
+            nc.vector.tensor_tensor(sums[:, 1, h, :], ds[h][:], sums[:, 0, h, :], ADD)
+        for h, t0, t1 in closing:
+            nc.vector.tensor_tensor(sums[:, 2, h, t0:t1], sums[:, 1, h, t0:t1], got[:, 1, h, t0:t1], ADD)
+            nc.sync.dma_start(out=out_rows[:, h, t0:t1], in_=sums[:, 2, h, t0:t1])

@@ -61,7 +61,7 @@ def tile_moe_bds_lin_none_kernel(tc, dyT, w_words, w_scales, gate, offs, pos1, p
             for j in range(PACK):
                 window[a, j] = keep.tile([P, most + SPARE], F32, name="window%d_%d" % (a, j))
         tokens = [keep.tile([P, PACK, T], F32, name="tokens%d" % a, tag="tokens%d" % a, align_bytes=64) for a in range(LAST)]
-        gates = [keep.tile([P, BANK], F32, name="gates0"), keep.tile([P, OWN - BANK], F32, name="gates1")]
+        gates = [keep.tile([P, BANK], F32, name="gates0"), keep.tile([P, OWN + P - BANK], F32, name="gates1")]
         gate_cols = keep.tile([P, S // P], F32, name="gate_cols")
 
         nc.sync.dma_start(slot_token[:], offs)
@@ -77,7 +77,7 @@ def tile_moe_bds_lin_none_kernel(tc, dyT, w_words, w_scales, gate, offs, pos1, p
         for j in range(PACK):
             nc.sync.dma_start(out=window[1, j][:, 0:T], in_=dy_rows[1, :, j, :])
         nc.sync.dma_start(out=tokens[1][:], in_=dy_rows[1])
-        nc.sync.dma_start(out=gates[1][:], in_=gate[0:P, BANK:OWN])
+        nc.sync.dma_start(out=gates[1][:], in_=gate[0:P, BANK : OWN + P])
         s_src = w_scales.rearrange("e a f k -> f (e a) k")
         for q in range(4):
             nc.sync.dma_start(out=w_exp[32 * q : 32 * q + 4, :, :].bitcast(I32), in_=s_src[4 * q : 4 * q + 4].bitcast(I32))
@@ -105,10 +105,10 @@ def tile_moe_bds_lin_none_kernel(tc, dyT, w_words, w_scales, gate, offs, pos1, p
                 nc.scalar.activation(rows[:, j, :], picked(a, j, c0, c1, T), COPY)
             return rows
 
-        def vector_gather(c0, c1):
-            rows = rows_tile(LAST, c0, c1, "own%d" % c0)
+        def vector_gather(a, c0, c1):
+            rows = rows_tile(a, c0, c1, "own%d" % c0)
             for j in range(PACK):
-                nc.vector.tensor_copy(rows[:, j, :], picked(LAST, j, c0, c1, ROW_STEP if c0 == 0 else LAST_WIDTH - j * ROW_STEP))
+                nc.vector.tensor_copy(rows[:, j, :], picked(a, j, c0, c1, ROW_STEP if c0 == 0 else LAST_WIDTH - j * ROW_STEP))
             return rows
 
         def rounded_tile(n, name, tag):
@@ -121,17 +121,18 @@ def tile_moe_bds_lin_none_kernel(tc, dyT, w_words, w_scales, gate, offs, pos1, p
             woven = target.rearrange("p (c i j) -> p c j i", i=RUN, j=PACK)
             nc.vector.tensor_tensor(woven, rows.rearrange("p j (c i) -> p c j i", i=RUN), spread, MULT)
 
-        def gpsimd_product(rows, weights, name, tag):
-            n = rows.shape[2]
-            target = rounded_tile(n, name, tag)
-            spread = weights.unsqueeze(2).to_broadcast([P, n, PACK])
-            nc.gpsimd.tensor_tensor(target[:].rearrange("p (c j) -> p c j", j=PACK), rows.rearrange("p j c -> p c j"), spread, MULT)
-            return target
+        def gpsimd_product(rows, weights, target):
+            spread = weights.unsqueeze(2).to_broadcast([P, rows.shape[2], PACK])
+            nc.gpsimd.tensor_tensor(target.rearrange("p (c j) -> p c j", j=PACK), rows.rearrange("p j c -> p c j"), spread, MULT)
 
-        token_bf = [rounded_tile(T, "token_bf%d" % a, "token_bf%d" % a) for a in range(PASSES)]
+        token_bf = rounded_tile(PASSES * T, "token_bf", "token_bf")
+
+        def token_part(q, a0, a1):
+            return token_bf[:, (q * PASSES + a0) * HALF * PACK : (q * PASSES + a1) * HALF * PACK]
 
         def gpsimd_round(a, rows):
-            nc.gpsimd.tensor_scalar(token_bf[a][:].rearrange("p (t j) -> p t j", j=PACK), rows.rearrange("p j t -> p t j"), 1.0, 0.0, MULT, ADD)
+            target = token_bf[:].rearrange("p (q a t j) -> p a q t j", q=2, a=PASSES, j=PACK)[:, a]
+            nc.gpsimd.tensor_scalar(target, rows.rearrange("p j (q t) -> p q t j", q=2), 1.0, 0.0, MULT, ADD)
 
         coded = {}
 
@@ -140,42 +141,51 @@ def tile_moe_bds_lin_none_kernel(tc, dyT, w_words, w_scales, gate, offs, pos1, p
             codes = keep.tile([P, n], U32, name="codes_" + name, tag=tag or "codes_" + name, align_bytes=64)
             exps = keep.tile([P, n], U8, name="exps_" + name, align_bytes=64)
             nc.vector.quantize_mx(out=codes[:].bitcast(FP8X4), scales=exps[:], in_=source)
-            width = n // len(parts)
-            for i, part in enumerate(parts):
-                coded[part] = (codes[:, i * width : (i + 1) * width], exps[:, i * width : (i + 1) * width])
+            place = 0
+            for a, b0, b1 in parts:
+                for b in range(b0, b1):
+                    coded[a, b] = (codes, exps, place)
+                    place = place + P
 
-        def product(acc, e, h, a, start, stop):
-            g = e * PASSES + a
+        def product(acc, h, a, b0, b1, start, stop):
+            g = min(b0 // 2, E) * PASSES + a
+            codes, exps, place = coded[a, b0]
+            cols = slice(place, place + (b1 - b0) * P)
             nc.tensor.matmul_mx(
                 out=acc,
                 lhsT=w_codes[:, g, 2 * P * h : 2 * P * (h + 1)].bitcast(FP4X4),
                 lhsT_scale=w_exp[:, g, P * h : P * (h + 1)],
-                rhs=coded[a, e][0].bitcast(FP8X4),
-                rhs_scale=coded[a, e][1],
+                rhs=codes[:, cols].bitcast(FP8X4),
+                rhs_scale=exps[:, cols],
                 start=start,
                 stop=stop,
             )
 
-        def pair_pass(acc, e0, a, start, stop):
+        def halves_apart(acc, base, a, b0, b1, start, stop):
+            cuts = [(b, min(b + 2, b1)) for b in range(b0, b1, 2)]
             for h in range(HALVES):
-                for i in range(2):
-                    product(acc[h][:, i * C : (i + 1) * C], e0 + i, h, a, start and i == 0, stop and i == 1)
+                for c0, c1 in cuts:
+                    product(acc[h][:, (c0 - base) * P : (c1 - base) * P], h, a, c0, c1, start and c0 == b0, stop and c1 == b1)
 
-        def expert_pass(acc, e, a, start, stop):
+        def halves_together(acc, a, b0, b1, start, stop):
+            n = (b1 - b0) * P
             for h in range(HALVES):
-                product(acc[:, h * C : (h + 1) * C], e, h, a, start and h == 0, stop and h == HALVES - 1)
+                product(acc[:, h * n : (h + 1) * n], h, a, b0, b1, start and h == 0, stop and h == HALVES - 1)
 
         rows_f = scalar_gather(LAST, OWN, S, "rows_f")
         rows_a = scalar_gather(0, 0, 2 * BANK, "rows_a")
         rows_b = scalar_gather(1, 0, BANK, "rows_b")
-        own = [vector_gather(0, BANK), vector_gather(BANK, OWN)]
+        own = [vector_gather(LAST, 0, BANK), vector_gather(LAST, BANK, OWN), vector_gather(1, OWN, OWN + P)]
 
         gpsimd_round(LAST, last_rows[:, : PACK * ROW_STEP].rearrange("p (j w) -> p j w", j=PACK)[:, :, 0:T])
-        own_0 = gpsimd_product(own[0][:], gates[0][:], "own_0", "own_0")
+        own_0 = rounded_tile(BANK, "own_0", "own_0")
+        gpsimd_product(own[0][:], gates[0][:], own_0[:])
         gpsimd_round(0, tokens[0][:])
         gpsimd_round(1, tokens[1][:])
         rows_c = scalar_gather(1, BANK, 2 * BANK, "tokens0")
-        own_2 = gpsimd_product(own[1][:, :, 0:C], gates[1][:, 0:C], "own_2", "own_2")
+        own_2 = rounded_tile(C + P, "own_2", "own_2")
+        gpsimd_product(own[1][:, :, 0:C], gates[1][:, 0:C], own_2[:, : C * PACK])
+        gpsimd_product(own[2][:], gates[1][:, OWN - BANK :], own_2[:, C * PACK :])
 
         bf_a = rounded_tile(2 * BANK, "bf_a", "bf_a")
         bf_b = rounded_tile(BANK, "bf_b", "bf_b")
@@ -183,80 +193,92 @@ def tile_moe_bds_lin_none_kernel(tc, dyT, w_words, w_scales, gate, offs, pos1, p
             vector_product(rows_a[:, :, i * BANK : (i + 1) * BANK], i * BANK, bf_a[:, i * BANK * PACK : (i + 1) * BANK * PACK])
         vector_product(rows_b[:], 0, bf_b[:])
         rows_d = scalar_gather(0, 2 * BANK, S, "rows_a")
-        rows_e = [scalar_gather(1, 4 * C, 5 * C, "rows_b")]
-        quantize(own_2[:], "own_2", [(2, 2)])
-        quantize(bf_a[:], "a", [(0, 0), (0, 1), (0, 2), (0, 3)])
-        quantize(own_0[:], "own_0", [(2, 0), (2, 1)])
-        quantize(bf_b[:], "b", [(1, 0), (1, 1)])
+        rows_e = scalar_gather(1, 4 * C, 5 * C, "rows_b")
+        quantize(own_2[:], "own_2", [(2, 4, 6), (1, 10, 11)])
+        quantize(bf_a[:], "a", [(0, 0, 8)])
+        quantize(own_0[:], "own_0", [(2, 0, 4)])
+        quantize(bf_b[:], "b", [(1, 0, 4)])
         first_acc = [psum.tile([P, BANK], F32, name="first_acc%d" % h, tag="first_acc%d" % h) for h in range(HALVES)]
         second_acc = [psum.tile([P, BANK], F32, name="second_acc%d" % h) for h in range(HALVES)]
         for a in (0, 2, 1):
-            pair_pass(first_acc, 0, a, a == 0, a == 1)
-        pair_pass(second_acc, 2, 0, True, False)
+            halves_apart(first_acc, 0, a, 0, 4, a == 0, a == 1)
+        halves_apart(second_acc, 4, 0, 4, 8, True, False)
 
-        own_3 = gpsimd_product(own[1][:, :, C:BANK], gates[1][:, C:BANK], "own_3", "bf_b")
+        own_3 = rounded_tile(C, "own_3", "bf_b")
+        gpsimd_product(own[1][:, :, C:BANK], gates[1][:, C:BANK], own_3[:])
         bf_c = rounded_tile(BANK, "bf_c", "own_2")
-        bf_fe = rounded_tile(BANK, "bf_fe", "own_0")
+        bf_f = rounded_tile(C, "bf_f", "own_0")
         vector_product(rows_c[:], BANK, bf_c[:])
-        rows_e.append(scalar_gather(1, 5 * C, S, "tokens0"))
-        vector_product(rows_f[:], OWN, bf_fe[:, : C * PACK])
-        quantize(own_3[:], "own_3", [(2, 3)])
-        quantize(token_bf[LAST][:], "t2", [(LAST, E)], "bf_a")
-        quantize(bf_c[:], "c", [(1, 2), (1, 3)])
+        rows_z = scalar_gather(1, OWN + P, S, "tokens0")
+        vector_product(rows_f[:], OWN, bf_f[:])
+        quantize(own_3[:], "own_3", [(2, 6, 8)])
+        quantize(token_part(0, 2, 3), "t02", [(2, 12, 14)], "rows_f")
+        quantize(token_part(0, 0, 2), "t00", [(0, 12, 14), (1, 12, 14)], "bf_a")
+        quantize(bf_f[:], "f", [(2, 10, 12)])
+        quantize(bf_c[:], "c", [(1, 4, 8)])
         for a in (2, 1):
-            pair_pass(second_acc, 2, a, False, a == 1)
-        ds = [psum.tile([P, T], F32, name="ds0", tag="gate_bank1")]
-        product(ds[0][:], E, 0, LAST, True, False)
+            halves_apart(second_acc, 4, a, 4, 8, False, a == 1)
+        ds = [psum.tile([P, BANK], F32, name="ds0", tag="gate_bank1")]
+        for a in range(PASSES):
+            halves_together(ds[0], a, 12, 14, a == 0, a == LAST)
+        last_acc = psum.tile([P, HALVES * P], F32, name="last_acc", tag="gate_bank0")
+        halves_together(last_acc, 2, 11, 12, True, False)
 
-        own_4 = gpsimd_product(own[1][:, :, BANK:], gates[1][:, BANK:], "own_4", "own_2")
+        own_4 = rounded_tile(C, "own_4", "own_2")
+        gpsimd_product(own[1][:, :, BANK:], gates[1][:, BANK : OWN - BANK], own_4[:])
         bf_d = rounded_tile(BANK, "bf_d", "bf_b")
+        bf_e = rounded_tile(C, "bf_e", "own_0")
         vector_product(rows_d[:], 2 * BANK, bf_d[:])
-        vector_product(rows_e[0][:], 4 * C, bf_fe[:, C * PACK :])
-        quantize(own_4[:], "own_4", [(2, 4)])
-        quantize(bf_d[:], "d", [(0, 4), (0, 5)])
-        quantize(bf_fe[:], "fe", [(2, 5), (1, 4)])
-        late_acc = [psum.tile([P, BANK], F32, name="late_acc0"), psum.tile([P, BANK], F32, name="late_acc1", tag="gate_bank0")]
-        for a in (2, 0, 1):
-            expert_pass(late_acc[0], 4, a, a == 2, a == 1)
-        for a in (0, 2):
-            expert_pass(late_acc[1], 5, a, a == 0, False)
+        vector_product(rows_e[:], 4 * C, bf_e[:])
 
         dx = [keep.tile([P, S], F32, name="dx%d" % h, tag=tag, align_bytes=64) for h, tag in enumerate(("own0", "tokens1"))]
-        for i, acc in enumerate((first_acc, second_acc)):
-            for h in range(HALVES):
-                nc.scalar.copy(out=dx[h][:, i * BANK : (i + 1) * BANK], in_=acc[h][:])
+        for h in (1, 0):
+            nc.scalar.copy(out=dx[h][:, :BANK], in_=first_acc[h][:])
         for h in range(HALVES):
-            nc.scalar.copy(out=dx[h][:, 4 * C : 5 * C], in_=late_acc[0][:, h * C : (h + 1) * C])
+            nc.scalar.copy(out=dx[h][:, BANK : 2 * BANK], in_=second_acc[h][:])
+        opening = keep.tile([P, HALVES, HALF], F32, name="opening", align_bytes=64)
+        nc.scalar.copy(out=opening[:].rearrange("p h t -> p (h t)"), in_=ds[0][:])
+        third_acc = [psum.tile([P, C + P], F32, name="third_acc0"), psum.tile([P, C + P], F32, name="third_acc1", tag="first_acc1")]
+        halves_apart(third_acc, 8, 2, 10, 11, True, False)
+        halves_apart(third_acc, 8, 1, 10, 11, False, False)
 
-        bf_g = rounded_tile(C, "bf_g", "own_2")
-        vector_product(rows_e[1][:], 5 * C, bf_g[:])
-        quantize(token_bf[0][:], "t0", [(0, E)], "bf_b")
-        quantize(bf_g[:], "g", [(1, 5)])
-        quantize(token_bf[1][:], "t1", [(1, E)], "own_0")
-        expert_pass(late_acc[1], 5, 1, False, True)
+        quantize(own_4[:], "own_4", [(2, 8, 10)])
+        quantize(bf_d[:], "d", [(0, 8, 12)])
+        quantize(bf_e[:], "e", [(1, 8, 10)])
+        halves_apart(third_acc, 8, 2, 8, 10, False, False)
+        halves_apart(third_acc, 8, 0, 8, 11, False, False)
+        halves_apart(third_acc, 8, 1, 8, 10, False, True)
+        halves_together(last_acc, 0, 11, 12, False, False)
         for h in range(HALVES):
-            nc.scalar.copy(out=dx[h][:, 5 * C :], in_=late_acc[1][:, h * C : (h + 1) * C])
-        ds.append(psum.tile([P, T], F32, name="ds1", tag="first_acc0"))
-        product(ds[0][:], E, 0, 0, False, False)
-        product(ds[0][:], E, 0, 1, False, True)
-        for a in range(PASSES):
-            product(ds[1][:], E, 1, a, a == 0, a == LAST)
+            nc.scalar.copy(out=dx[h][:, 2 * BANK : OWN + P], in_=third_acc[h][:])
+
+        bf_z = rounded_tile(P, "bf_z", "own_2")
+        vector_product(rows_z[:], OWN + P, bf_z[:])
+        quantize(token_part(1, 2, 3), "t12", [(2, 14, 16)], "bf_b")
+        quantize(bf_z[:], "z", [(1, 11, 12)])
+        quantize(token_part(1, 0, 2), "t10", [(0, 14, 16), (1, 14, 16)], "own_0")
+        halves_together(last_acc, 1, 11, 12, False, True)
+        for h in range(HALVES):
+            nc.scalar.copy(out=dx[h][:, OWN + P :], in_=last_acc[:, h * P : (h + 1) * P])
+        ds.append(psum.tile([P, BANK], F32, name="ds1", tag="first_acc0"))
+        for a in (2, 0, 1):
+            halves_together(ds[1], a, 14, 16, a == 2, a == 1)
 
         def fetched(r, h, t0, t1):
             return dx[h][:].indirect(token_slot[r][:, t0 // 16 : t1 // 16])
 
-        got = keep.tile([P, 2, HALVES, T], F32, name="got", tag="rows_b", align_bytes=64)
+        got = keep.tile([P, 2, HALVES, T], F32, name="got", tag="own%d" % BANK, align_bytes=64)
         sums = keep.tile([P, 3, HALVES, T], F32, name="sums", tag="rows_a", align_bytes=64)
         out_rows = out.rearrange("(h p) t -> p h t", p=P)
-        quarters = [(h, t0, t0 + HALF) for h in range(HALVES) for t0 in (0, HALF)]
-        closing = [(0, 0, T)] + quarters[2:]
-        for r, pieces in enumerate((quarters, closing)):
-            for h, t0, t1 in pieces:
-                nc.scalar.activation(got[:, r, h, t0:t1], fetched(r, h, t0, t1), COPY)
-        for h, t0, t1 in quarters:
-            nc.vector.tensor_tensor(sums[:, 0, h, t0:t1], fetched(2, h, t0, t1), got[:, 0, h, t0:t1], ADD)
+        for r, h, t0, t1 in ((0, 0, HALF, T), (0, 1, HALF, T), (0, 0, 0, HALF), (0, 1, 0, HALF), (1, 1, 0, HALF), (1, 0, 0, HALF), (1, 0, HALF, T)):
+            nc.scalar.activation(got[:, r, h, t0:t1], fetched(r, h, t0, t1), COPY)
         for h in range(HALVES):
-            nc.vector.tensor_tensor(sums[:, 1, h, :], ds[h][:], sums[:, 0, h, :], ADD)
-        for h, t0, t1 in closing:
-            nc.vector.tensor_tensor(sums[:, 2, h, t0:t1], sums[:, 1, h, t0:t1], got[:, 1, h, t0:t1], ADD)
+            nc.vector.tensor_tensor(sums[:, 0, h, :HALF], fetched(2, h, 0, HALF), opening[:, h, :], ADD)
+        for h in range(HALVES):
+            nc.vector.tensor_tensor(sums[:, 0, h, HALF:], fetched(2, h, HALF, T), got[:, 0, h, HALF:], ADD)
+        nc.vector.tensor_tensor(sums[:, 1, :, :HALF], sums[:, 0, :, :HALF], got[:, 0, :, :HALF], ADD)
+        nc.vector.tensor_tensor(sums[:, 1, :, HALF:], ds[1][:].rearrange("p (h t) -> p h t", h=HALVES), sums[:, 0, :, HALF:], ADD)
+        for h, t0, t1 in ((1, 0, HALF), (0, 0, HALF), (1, HALF, T), (0, HALF, T)):
+            other = fetched(1, h, t0, t1) if (h, t0) == (1, HALF) else got[:, 1, h, t0:t1]
+            nc.vector.tensor_tensor(sums[:, 2, h, t0:t1], other, sums[:, 1, h, t0:t1], ADD)
             nc.sync.dma_start(out=out_rows[:, h, t0:t1], in_=sums[:, 2, h, t0:t1])

@@ -29,6 +29,7 @@ HALF = T // 2
 RUN = 2
 BANK = 512
 OWN = 5 * C
+MOST = 3 * P
 SPARE = 16
 ROW_STEP = 704
 LAST_WIDTH = (PACK - 1) * ROW_STEP + 2 * T
@@ -127,12 +128,17 @@ def tile_moe_bds_lin_none_kernel(tc, dyT, w_words, w_scales, gate, offs, pos1, p
 
         token_bf = rounded_tile(PASSES * T, "token_bf", "token_bf")
 
-        def token_part(q, a0, a1):
-            return token_bf[:, (q * PASSES + a0) * HALF * PACK : (q * PASSES + a1) * HALF * PACK]
+        token_place = {(0, 0): 0, (0, 2): 1, (0, 1): 2, (1, 1): 3, (1, 0): 4, (1, 2): 5}
 
-        def gpsimd_round(a, rows):
-            target = token_bf[:].rearrange("p (q a t j) -> p a q t j", q=2, a=PASSES, j=PACK)[:, a]
-            nc.gpsimd.tensor_scalar(target, rows.rearrange("p j (q t) -> p q t j", q=2), 1.0, 0.0, MULT, ADD)
+        def token_part(first, count):
+            return token_bf[:, token_place[first] * HALF * PACK : (token_place[first] + count) * HALF * PACK]
+
+        def gpsimd_round(target, rows):
+            nc.gpsimd.tensor_scalar(target, rows, 1.0, 0.0, MULT, ADD)
+
+        def round_apart(a, rows):
+            target = token_bf[:].rearrange("p (s t j) -> p s t j", t=HALF, j=PACK)[:, token_place[0, a] :: 4]
+            gpsimd_round(target, rows.rearrange("p j (q t) -> p q t j", q=2))
 
         coded = {}
 
@@ -177,11 +183,13 @@ def tile_moe_bds_lin_none_kernel(tc, dyT, w_words, w_scales, gate, offs, pos1, p
         rows_b = scalar_gather(1, 0, BANK, "rows_b")
         own = [vector_gather(LAST, 0, BANK), vector_gather(LAST, BANK, OWN), vector_gather(1, OWN, OWN + P)]
 
-        gpsimd_round(LAST, last_rows[:, : PACK * ROW_STEP].rearrange("p (j w) -> p j w", j=PACK)[:, :, 0:T])
+        round_apart(LAST, last_rows[:, : PACK * ROW_STEP].rearrange("p (j w) -> p j w", j=PACK)[:, :, 0:T])
         own_0 = rounded_tile(BANK, "own_0", "own_0")
         gpsimd_product(own[0][:], gates[0][:], own_0[:])
-        gpsimd_round(0, tokens[0][:])
-        gpsimd_round(1, tokens[1][:])
+        round_apart(0, tokens[0][:])
+        middle_bf = token_part((0, 1), 2).rearrange("p (t j) -> p t j", j=PACK)
+        middle = tokens[1][:].rearrange("p j t -> p t j")
+        gpsimd_round(middle_bf[:, :MOST], middle[:, :MOST])
         rows_c = scalar_gather(1, BANK, 2 * BANK, "tokens0")
         own_2 = rounded_tile(C + P, "own_2", "own_2")
         gpsimd_product(own[1][:, :, 0:C], gates[1][:, 0:C], own_2[:, : C * PACK])
@@ -212,8 +220,8 @@ def tile_moe_bds_lin_none_kernel(tc, dyT, w_words, w_scales, gate, offs, pos1, p
         rows_z = scalar_gather(1, OWN + P, S, "tokens0")
         vector_product(rows_f[:], OWN, bf_f[:])
         quantize(own_3[:], "own_3", [(2, 6, 8)])
-        quantize(token_part(0, 2, 3), "t02", [(2, 12, 14)], "rows_f")
-        quantize(token_part(0, 0, 2), "t00", [(0, 12, 14), (1, 12, 14)], "bf_a")
+        quantize(token_part((0, 1), 1), "t01", [(1, 12, 14)], "rows_f")
+        quantize(token_part((0, 0), 2), "t00", [(0, 12, 14), (2, 12, 14)], "bf_a")
         quantize(bf_f[:], "f", [(2, 10, 12)])
         quantize(bf_c[:], "c", [(1, 4, 8)])
         for a in (2, 1):
@@ -231,7 +239,8 @@ def tile_moe_bds_lin_none_kernel(tc, dyT, w_words, w_scales, gate, offs, pos1, p
         vector_product(rows_d[:], 2 * BANK, bf_d[:])
         vector_product(rows_e[:], 4 * C, bf_e[:])
 
-        dx = [keep.tile([P, S], F32, name="dx%d" % h, tag=tag, align_bytes=64) for h, tag in enumerate(("own0", "tokens1"))]
+        dx = [keep.tile([P, S], F32, name="dx%d" % h, tag=tag, align_bytes=64) for h, tag in enumerate(("own0", "dx1"))]
+        nc.scalar.copy(out=middle_bf[:, MOST:], in_=middle[:, MOST:])
         for h in (1, 0):
             nc.scalar.copy(out=dx[h][:, :BANK], in_=first_acc[h][:])
         for h in range(HALVES):
@@ -254,15 +263,15 @@ def tile_moe_bds_lin_none_kernel(tc, dyT, w_words, w_scales, gate, offs, pos1, p
 
         bf_z = rounded_tile(P, "bf_z", "own_2")
         vector_product(rows_z[:], OWN + P, bf_z[:])
-        quantize(token_part(1, 2, 3), "t12", [(2, 14, 16)], "bf_b")
+        quantize(token_part((1, 1), 1), "t11", [(1, 14, 16)], "bf_b")
         quantize(bf_z[:], "z", [(1, 11, 12)])
-        quantize(token_part(1, 0, 2), "t10", [(0, 14, 16), (1, 14, 16)], "own_0")
+        quantize(token_part((1, 0), 2), "t10", [(0, 14, 16), (2, 14, 16)], "own_0")
         halves_together(last_acc, 1, 11, 12, False, True)
         for h in range(HALVES):
             nc.scalar.copy(out=dx[h][:, OWN + P :], in_=last_acc[:, h * P : (h + 1) * P])
         ds.append(psum.tile([P, BANK], F32, name="ds1", tag="first_acc0"))
-        for a in (2, 0, 1):
-            halves_together(ds[1], a, 14, 16, a == 2, a == 1)
+        for a in (1, 0, 2):
+            halves_together(ds[1], a, 14, 16, a == 1, a == 2)
 
         def fetched(r, h, t0, t1):
             return dx[h][:].indirect(token_slot[r][:, t0 // 16 : t1 // 16])

@@ -29,7 +29,6 @@ HALF = T // 2
 RUN = 2
 BANK = 512
 OWN = 5 * C
-MOST = 3 * P
 SPARE = 16
 ROW_STEP = 704
 LAST_WIDTH = (PACK - 1) * ROW_STEP + 2 * T
@@ -63,7 +62,7 @@ def tile_moe_bds_lin_none_kernel(tc, dyT, w_words, w_scales, gate, offs, pos1, p
                 window[a, j] = keep.tile([P, most + SPARE], F32, name="window%d_%d" % (a, j))
         tokens = [keep.tile([P, PACK, T], F32, name="tokens%d" % a, tag="tokens%d" % a, align_bytes=64) for a in range(LAST)]
         gates = [keep.tile([P, BANK], F32, name="gates0"), keep.tile([P, OWN + P - BANK], F32, name="gates1")]
-        gate_cols = keep.tile([P, S // P], F32, name="gate_cols")
+        gate_cols = keep.tile([P, S // BANK, PACK], F32, name="gate_cols")
 
         nc.sync.dma_start(slot_token[:], offs)
         for j in range(PACK):
@@ -73,12 +72,11 @@ def tile_moe_bds_lin_none_kernel(tc, dyT, w_words, w_scales, gate, offs, pos1, p
             if j == 0:
                 nc.sync.dma_start(out=gates[0][:], in_=gate[0:P, 0:BANK])
         nc.sync.dma_start(out=tokens[0][:], in_=dy_rows[0])
-        with nc.allow_non_contiguous_dma(reason="one gate value a partition"):
-            nc.sync.dma_start(out=gate_cols[:], in_=gate[0, :].rearrange("(b p) -> p b", p=P))
+        nc.sync.dma_start(out=gate_cols[:], in_=gate[0, :].rearrange("(b p i) -> p b i", p=P, i=PACK))
         for j in range(PACK):
             nc.sync.dma_start(out=window[1, j][:, 0:T], in_=dy_rows[1, :, j, :])
-        nc.sync.dma_start(out=tokens[1][:], in_=dy_rows[1])
         nc.sync.dma_start(out=gates[1][:], in_=gate[0:P, BANK : OWN + P])
+        nc.sync.dma_start(out=tokens[1][:], in_=dy_rows[1])
         s_src = w_scales.rearrange("e a f k -> f (e a) k")
         for q in range(4):
             nc.sync.dma_start(out=w_exp[32 * q : 32 * q + 4, :, :].bitcast(I32), in_=s_src[4 * q : 4 * q + 4].bitcast(I32))
@@ -89,9 +87,8 @@ def tile_moe_bds_lin_none_kernel(tc, dyT, w_words, w_scales, gate, offs, pos1, p
         gate_bank = {}
         for b in range(S // BANK):
             gate_bank[b] = psum.tile([P, BANK], F32, name="gate_bank%d" % b, tag="gate_bank%d" % b)
-            for m in range(BANK // P):
-                col = b * BANK // P + m
-                nc.tensor.transpose(gate_bank[b][:, m * P : (m + 1) * P], gate_cols[:, col : col + 1].to_broadcast([P, P]), ident[:])
+            for i in range(PACK):
+                nc.tensor.transpose(gate_bank[b][:, i::PACK], gate_cols[:, b, i : i + 1].to_broadcast([P, P]), ident[:])
 
         def picked(a, j, c0, c1, width):
             source = last_rows[:, j * ROW_STEP : j * ROW_STEP + width] if a == LAST else window[a, j][:]
@@ -126,9 +123,9 @@ def tile_moe_bds_lin_none_kernel(tc, dyT, w_words, w_scales, gate, offs, pos1, p
             spread = weights.unsqueeze(2).to_broadcast([P, rows.shape[2], PACK])
             nc.gpsimd.tensor_tensor(target.rearrange("p (c j) -> p c j", j=PACK), rows.rearrange("p j c -> p c j"), spread, MULT)
 
-        token_bf = rounded_tile(PASSES * T, "token_bf", "token_bf")
+        token_bf = rounded_tile(PASSES * T + HALF, "token_bf", "token_bf")
 
-        token_place = {(0, 0): 0, (0, 2): 1, (0, 1): 2, (1, 1): 3, (1, 0): 4, (1, 2): 5}
+        token_place = {(0, 0): 0, (0, 2): 1, (1, 0): 2, (1, 2): 3, (0, 1): 4, (1, 1): 6}
 
         def token_part(first, count):
             return token_bf[:, token_place[first] * HALF * PACK : (token_place[first] + count) * HALF * PACK]
@@ -137,7 +134,7 @@ def tile_moe_bds_lin_none_kernel(tc, dyT, w_words, w_scales, gate, offs, pos1, p
             nc.gpsimd.tensor_scalar(target, rows, 1.0, 0.0, MULT, ADD)
 
         def round_apart(a, rows):
-            target = token_bf[:].rearrange("p (s t j) -> p s t j", t=HALF, j=PACK)[:, token_place[0, a] :: 4]
+            target = token_bf[:].rearrange("p (s t j) -> p s t j", t=HALF, j=PACK)[:, token_place[0, a] : token_place[1, a] + 1 : 2]
             gpsimd_round(target, rows.rearrange("p j (q t) -> p q t j", q=2))
 
         coded = {}
@@ -187,13 +184,11 @@ def tile_moe_bds_lin_none_kernel(tc, dyT, w_words, w_scales, gate, offs, pos1, p
         own_0 = rounded_tile(BANK, "own_0", "own_0")
         gpsimd_product(own[0][:], gates[0][:], own_0[:])
         round_apart(0, tokens[0][:])
-        middle_bf = token_part((0, 1), 2).rearrange("p (t j) -> p t j", j=PACK)
-        middle = tokens[1][:].rearrange("p j t -> p t j")
-        gpsimd_round(middle_bf[:, :MOST], middle[:, :MOST])
         rows_c = scalar_gather(1, BANK, 2 * BANK, "tokens0")
         own_2 = rounded_tile(C + P, "own_2", "own_2")
         gpsimd_product(own[1][:, :, 0:C], gates[1][:, 0:C], own_2[:, : C * PACK])
         gpsimd_product(own[2][:], gates[1][:, OWN - BANK :], own_2[:, C * PACK :])
+        round_apart(1, tokens[1][:])
 
         bf_a = rounded_tile(2 * BANK, "bf_a", "bf_a")
         bf_b = rounded_tile(BANK, "bf_b", "bf_b")
@@ -202,6 +197,7 @@ def tile_moe_bds_lin_none_kernel(tc, dyT, w_words, w_scales, gate, offs, pos1, p
         vector_product(rows_b[:], 0, bf_b[:])
         rows_d = scalar_gather(0, 2 * BANK, S, "rows_a")
         rows_e = scalar_gather(1, 4 * C, 5 * C, "rows_b")
+        quantize(token_part((0, 1), 1), "t01", [(1, 12, 14)])
         quantize(own_2[:], "own_2", [(2, 4, 6), (1, 10, 11)])
         quantize(bf_a[:], "a", [(0, 0, 8)])
         quantize(own_0[:], "own_0", [(2, 0, 4)])
@@ -214,16 +210,15 @@ def tile_moe_bds_lin_none_kernel(tc, dyT, w_words, w_scales, gate, offs, pos1, p
 
         own_3 = rounded_tile(C, "own_3", "bf_b")
         gpsimd_product(own[1][:, :, C:BANK], gates[1][:, C:BANK], own_3[:])
-        bf_c = rounded_tile(BANK, "bf_c", "own_2")
+        bf_c = token_part((0, 1), 2)
         bf_f = rounded_tile(C, "bf_f", "own_0")
-        vector_product(rows_c[:], BANK, bf_c[:])
+        vector_product(rows_c[:], BANK, bf_c)
         rows_z = scalar_gather(1, OWN + P, S, "tokens0")
         vector_product(rows_f[:], OWN, bf_f[:])
         quantize(own_3[:], "own_3", [(2, 6, 8)])
-        quantize(token_part((0, 1), 1), "t01", [(1, 12, 14)], "rows_f")
         quantize(token_part((0, 0), 2), "t00", [(0, 12, 14), (2, 12, 14)], "bf_a")
         quantize(bf_f[:], "f", [(2, 10, 12)])
-        quantize(bf_c[:], "c", [(1, 4, 8)])
+        quantize(bf_c, "c", [(1, 4, 8)])
         for a in (2, 1):
             halves_apart(second_acc, 4, a, 4, 8, False, a == 1)
         ds = [psum.tile([P, BANK], F32, name="ds0", tag="gate_bank1")]
@@ -232,15 +227,14 @@ def tile_moe_bds_lin_none_kernel(tc, dyT, w_words, w_scales, gate, offs, pos1, p
         last_acc = psum.tile([P, HALVES * P], F32, name="last_acc", tag="gate_bank0")
         halves_together(last_acc, 2, 11, 12, True, False)
 
-        own_4 = rounded_tile(C, "own_4", "own_2")
-        gpsimd_product(own[1][:, :, BANK:], gates[1][:, BANK : OWN - BANK], own_4[:])
+        own_4 = token_part((0, 1), 1)
+        gpsimd_product(own[1][:, :, BANK:], gates[1][:, BANK : OWN - BANK], own_4)
         bf_d = rounded_tile(BANK, "bf_d", "bf_b")
         bf_e = rounded_tile(C, "bf_e", "own_0")
         vector_product(rows_d[:], 2 * BANK, bf_d[:])
         vector_product(rows_e[:], 4 * C, bf_e[:])
 
-        dx = [keep.tile([P, S], F32, name="dx%d" % h, tag=tag, align_bytes=64) for h, tag in enumerate(("own0", "dx1"))]
-        nc.scalar.copy(out=middle_bf[:, MOST:], in_=middle[:, MOST:])
+        dx = [keep.tile([P, S], F32, name="dx%d" % h, tag=tag, align_bytes=64) for h, tag in enumerate(("own0", "tokens1"))]
         for h in (1, 0):
             nc.scalar.copy(out=dx[h][:, :BANK], in_=first_acc[h][:])
         for h in range(HALVES):
@@ -251,7 +245,7 @@ def tile_moe_bds_lin_none_kernel(tc, dyT, w_words, w_scales, gate, offs, pos1, p
         halves_apart(third_acc, 8, 2, 10, 11, True, False)
         halves_apart(third_acc, 8, 1, 10, 11, False, False)
 
-        quantize(own_4[:], "own_4", [(2, 8, 10)])
+        quantize(own_4, "own_4", [(2, 8, 10)])
         quantize(bf_d[:], "d", [(0, 8, 12)])
         quantize(bf_e[:], "e", [(1, 8, 10)])
         halves_apart(third_acc, 8, 2, 8, 10, False, False)
@@ -261,10 +255,10 @@ def tile_moe_bds_lin_none_kernel(tc, dyT, w_words, w_scales, gate, offs, pos1, p
         for h in range(HALVES):
             nc.scalar.copy(out=dx[h][:, 2 * BANK : OWN + P], in_=third_acc[h][:])
 
-        bf_z = rounded_tile(P, "bf_z", "own_2")
-        vector_product(rows_z[:], OWN + P, bf_z[:])
+        bf_z = token_part((0, 1), 1)[:, : P * PACK]
+        vector_product(rows_z[:], OWN + P, bf_z)
         quantize(token_part((1, 1), 1), "t11", [(1, 14, 16)], "bf_b")
-        quantize(bf_z[:], "z", [(1, 11, 12)])
+        quantize(bf_z, "z", [(1, 11, 12)])
         quantize(token_part((1, 0), 2), "t10", [(0, 14, 16), (2, 14, 16)], "own_0")
         halves_together(last_acc, 1, 11, 12, False, True)
         for h in range(HALVES):

@@ -30,8 +30,9 @@ RUN = 2
 BANK = 512
 OWN = 5 * C
 SPARE = 16
-ROW_STEP = 704
-LAST_WIDTH = (PACK - 1) * ROW_STEP + 2 * T
+FIRST = 448
+ROW_STEP = 608
+LAST_WIDTH = (PACK - 1) * ROW_STEP + 1120
 
 
 def tile_moe_bds_lin_none_kernel(tc, dyT, w_words, w_scales, gate, offs, pos1, pos2, pos3, out):
@@ -61,7 +62,7 @@ def tile_moe_bds_lin_none_kernel(tc, dyT, w_words, w_scales, gate, offs, pos1, p
             for j in range(PACK):
                 window[a, j] = keep.tile([P, most + SPARE], F32, name="window%d_%d" % (a, j))
         tokens = [keep.tile([P, PACK, T], F32, name="tokens%d" % a, tag="tokens%d" % a, align_bytes=64) for a in range(LAST)]
-        gates = [keep.tile([P, BANK], F32, name="gates0"), keep.tile([P, OWN + P - BANK], F32, name="gates1")]
+        gates = [keep.tile([P, FIRST], F32, name="gates0"), keep.tile([P, OWN + P - FIRST], F32, name="gates1")]
         gate_cols = keep.tile([P, S // BANK, PACK], F32, name="gate_cols")
 
         nc.sync.dma_start(slot_token[:], offs)
@@ -70,12 +71,12 @@ def tile_moe_bds_lin_none_kernel(tc, dyT, w_words, w_scales, gate, offs, pos1, p
         for j in range(PACK):
             nc.sync.dma_start(out=window[0, j][:, 0:T], in_=dy_rows[0, :, j, :])
             if j == 0:
-                nc.sync.dma_start(out=gates[0][:], in_=gate[0:P, 0:BANK])
+                nc.sync.dma_start(out=gates[0][:], in_=gate[0:P, 0:FIRST])
         nc.sync.dma_start(out=tokens[0][:], in_=dy_rows[0])
         nc.sync.dma_start(out=gate_cols[:], in_=gate[0, :].rearrange("(b p i) -> p b i", p=P, i=PACK))
         for j in range(PACK):
             nc.sync.dma_start(out=window[1, j][:, 0:T], in_=dy_rows[1, :, j, :])
-        nc.sync.dma_start(out=gates[1][:], in_=gate[0:P, BANK : OWN + P])
+        nc.sync.dma_start(out=gates[1][:], in_=gate[0:P, FIRST : OWN + P])
         nc.sync.dma_start(out=tokens[1][:], in_=dy_rows[1])
         s_src = w_scales.rearrange("e a f k -> f (e a) k")
         for q in range(4):
@@ -123,19 +124,14 @@ def tile_moe_bds_lin_none_kernel(tc, dyT, w_words, w_scales, gate, offs, pos1, p
             spread = weights.unsqueeze(2).to_broadcast([P, rows.shape[2], PACK])
             nc.gpsimd.tensor_tensor(target.rearrange("p (c j) -> p c j", j=PACK), rows.rearrange("p j c -> p c j"), spread, MULT)
 
-        token_bf = rounded_tile(PASSES * T + HALF, "token_bf", "token_bf")
+        rounded = rounded_tile(12 * C, "rounded", "rounded")
 
-        token_place = {(0, 0): 0, (0, 2): 1, (1, 0): 2, (1, 2): 3, (0, 1): 4, (1, 1): 6}
+        def spot(first, count):
+            return rounded[:, first * C * PACK : (first + count) * C * PACK]
 
-        def token_part(first, count):
-            return token_bf[:, token_place[first] * HALF * PACK : (token_place[first] + count) * HALF * PACK]
-
-        def gpsimd_round(target, rows):
-            nc.gpsimd.tensor_scalar(target, rows, 1.0, 0.0, MULT, ADD)
-
-        def round_apart(a, rows):
-            target = token_bf[:].rearrange("p (s t j) -> p s t j", t=HALF, j=PACK)[:, token_place[0, a] : token_place[1, a] + 1 : 2]
-            gpsimd_round(target, rows.rearrange("p j (q t) -> p q t j", q=2))
+        def round_tokens(rows, first, second):
+            target = rounded[:].rearrange("p (s t j) -> p s t j", t=HALF, j=PACK)[:, first : second + 1 : second - first]
+            nc.gpsimd.tensor_scalar(target, rows.rearrange("p j (q t) -> p q t j", q=2), 1.0, 0.0, MULT, ADD)
 
         coded = {}
 
@@ -178,61 +174,53 @@ def tile_moe_bds_lin_none_kernel(tc, dyT, w_words, w_scales, gate, offs, pos1, p
         rows_f = scalar_gather(LAST, OWN, S, "rows_f")
         rows_a = scalar_gather(0, 0, 2 * BANK, "rows_a")
         rows_b = scalar_gather(1, 0, BANK, "rows_b")
-        own = [vector_gather(LAST, 0, BANK), vector_gather(LAST, BANK, OWN), vector_gather(1, OWN, OWN + P)]
+        own = [vector_gather(LAST, 0, FIRST), vector_gather(LAST, FIRST, OWN), vector_gather(1, OWN, OWN + P)]
 
-        round_apart(LAST, last_rows[:, : PACK * ROW_STEP].rearrange("p (j w) -> p j w", j=PACK)[:, :, 0:T])
-        own_0 = rounded_tile(BANK, "own_0", "own_0")
-        gpsimd_product(own[0][:], gates[0][:], own_0[:])
-        round_apart(0, tokens[0][:])
+        def own_product(c0, c1, target):
+            gpsimd_product(own[1][:, :, c0 - FIRST : c1 - FIRST], gates[1][:, c0 - FIRST : c1 - FIRST], target)
+
+        late = rounded_tile(P + BANK, "late", "late")
+        round_tokens(last_rows[:, : PACK * ROW_STEP].rearrange("p (j w) -> p j w", j=PACK)[:, :, 0:T], 1, 11)
+        gpsimd_product(own[0][:], gates[0][:], spot(5, 3)[:, : FIRST * PACK])
+        round_tokens(tokens[0][:], 0, 10)
         rows_c = scalar_gather(1, BANK, 2 * BANK, "tokens0")
-        own_2 = rounded_tile(C + P, "own_2", "own_2")
-        gpsimd_product(own[1][:, :, 0:C], gates[1][:, 0:C], own_2[:, : C * PACK])
-        gpsimd_product(own[2][:], gates[1][:, OWN - BANK :], own_2[:, C * PACK :])
-        round_apart(1, tokens[1][:])
+        own_product(FIRST, 3 * C, spot(5, 3)[:, FIRST * PACK :])
+        gpsimd_product(own[2][:], gates[1][:, OWN - FIRST :], late[:, : P * PACK])
+        round_tokens(tokens[1][:], 8, 9)
 
         bf_a = rounded_tile(2 * BANK, "bf_a", "bf_a")
-        bf_b = rounded_tile(BANK, "bf_b", "bf_b")
         for i in range(2):
             vector_product(rows_a[:, :, i * BANK : (i + 1) * BANK], i * BANK, bf_a[:, i * BANK * PACK : (i + 1) * BANK * PACK])
-        vector_product(rows_b[:], 0, bf_b[:])
+        vector_product(rows_b[:], 0, spot(3, 2))
         rows_d = scalar_gather(0, 2 * BANK, S, "rows_a")
         rows_e = scalar_gather(1, 4 * C, 5 * C, "rows_b")
-        quantize(token_part((0, 1), 1), "t01", [(1, 12, 14)])
-        quantize(own_2[:], "own_2", [(2, 4, 6), (1, 10, 11)])
+        quantize(spot(7, 2), "g", [(2, 4, 6), (1, 12, 14)])
         quantize(bf_a[:], "a", [(0, 0, 8)])
-        quantize(own_0[:], "own_0", [(2, 0, 4)])
-        quantize(bf_b[:], "b", [(1, 0, 4)])
+        quantize(spot(3, 4), "b", [(1, 0, 4), (2, 0, 4)])
         first_acc = [psum.tile([P, BANK], F32, name="first_acc%d" % h, tag="first_acc%d" % h) for h in range(HALVES)]
         second_acc = [psum.tile([P, BANK], F32, name="second_acc%d" % h) for h in range(HALVES)]
-        for a in (0, 2, 1):
-            halves_apart(first_acc, 0, a, 0, 4, a == 0, a == 1)
+        for a in range(PASSES):
+            halves_apart(first_acc, 0, a, 0, 4, a == 0, a == LAST)
         halves_apart(second_acc, 4, 0, 4, 8, True, False)
+        halves_apart(second_acc, 4, 2, 4, 6, False, False)
 
-        own_3 = rounded_tile(C, "own_3", "bf_b")
-        gpsimd_product(own[1][:, :, C:BANK], gates[1][:, C:BANK], own_3[:])
-        bf_c = token_part((0, 1), 2)
-        bf_f = rounded_tile(C, "bf_f", "own_0")
-        vector_product(rows_c[:], BANK, bf_c)
+        own_product(3 * C, 4 * C, spot(3, 1))
+        vector_product(rows_f[:], OWN, spot(2, 1))
+        vector_product(rows_c[:], BANK, late[:, P * PACK :])
         rows_z = scalar_gather(1, OWN + P, S, "tokens0")
-        vector_product(rows_f[:], OWN, bf_f[:])
-        quantize(own_3[:], "own_3", [(2, 6, 8)])
-        quantize(token_part((0, 0), 2), "t00", [(0, 12, 14), (2, 12, 14)], "bf_a")
-        quantize(bf_f[:], "f", [(2, 10, 12)])
-        quantize(bf_c, "c", [(1, 4, 8)])
-        for a in (2, 1):
-            halves_apart(second_acc, 4, a, 4, 8, False, a == 1)
+        quantize(spot(0, 4), "h", [(0, 12, 14), (2, 12, 14), (2, 10, 12), (2, 6, 8)])
+        quantize(late[:, P * PACK :], "c", [(1, 4, 8)])
+        halves_apart(second_acc, 4, 2, 6, 8, False, False)
+        halves_apart(second_acc, 4, 1, 4, 8, False, True)
         ds = [psum.tile([P, BANK], F32, name="ds0", tag="gate_bank1")]
         for a in range(PASSES):
             halves_together(ds[0], a, 12, 14, a == 0, a == LAST)
         last_acc = psum.tile([P, HALVES * P], F32, name="last_acc", tag="gate_bank0")
         halves_together(last_acc, 2, 11, 12, True, False)
 
-        own_4 = token_part((0, 1), 1)
-        gpsimd_product(own[1][:, :, BANK:], gates[1][:, BANK : OWN - BANK], own_4)
-        bf_d = rounded_tile(BANK, "bf_d", "bf_b")
-        bf_e = rounded_tile(C, "bf_e", "own_0")
-        vector_product(rows_d[:], 2 * BANK, bf_d[:])
-        vector_product(rows_e[:], 4 * C, bf_e[:])
+        own_product(4 * C, OWN, late[:, P * PACK : (P + C) * PACK])
+        vector_product(rows_d[:], 2 * BANK, spot(0, 2))
+        vector_product(rows_e[:], 4 * C, spot(2, 1))
 
         dx = [keep.tile([P, S], F32, name="dx%d" % h, tag=tag, align_bytes=64) for h, tag in enumerate(("own0", "tokens1"))]
         for h in (1, 0):
@@ -243,23 +231,22 @@ def tile_moe_bds_lin_none_kernel(tc, dyT, w_words, w_scales, gate, offs, pos1, p
         nc.scalar.copy(out=opening[:].rearrange("p h t -> p (h t)"), in_=ds[0][:])
         third_acc = [psum.tile([P, C + P], F32, name="third_acc0"), psum.tile([P, C + P], F32, name="third_acc1", tag="first_acc1")]
         halves_apart(third_acc, 8, 2, 10, 11, True, False)
-        halves_apart(third_acc, 8, 1, 10, 11, False, False)
 
-        quantize(own_4, "own_4", [(2, 8, 10)])
-        quantize(bf_d[:], "d", [(0, 8, 12)])
-        quantize(bf_e[:], "e", [(1, 8, 10)])
+        quantize(late[:, : (P + C) * PACK], "late", [(1, 10, 11), (2, 8, 10)])
+        quantize(spot(0, 2), "d", [(0, 8, 12)])
+        quantize(spot(2, 1), "e", [(1, 8, 10)])
         halves_apart(third_acc, 8, 2, 8, 10, False, False)
+        halves_apart(third_acc, 8, 1, 10, 11, False, False)
         halves_apart(third_acc, 8, 0, 8, 11, False, False)
         halves_apart(third_acc, 8, 1, 8, 10, False, True)
         halves_together(last_acc, 0, 11, 12, False, False)
         for h in range(HALVES):
             nc.scalar.copy(out=dx[h][:, 2 * BANK : OWN + P], in_=third_acc[h][:])
 
-        bf_z = token_part((0, 1), 1)[:, : P * PACK]
-        vector_product(rows_z[:], OWN + P, bf_z)
-        quantize(token_part((1, 1), 1), "t11", [(1, 14, 16)], "bf_b")
-        quantize(bf_z, "z", [(1, 11, 12)])
-        quantize(token_part((1, 0), 2), "t10", [(0, 14, 16), (2, 14, 16)], "own_0")
+        vector_product(rows_z[:], OWN + P, late[:, : P * PACK])
+        quantize(spot(9, 1), "t11", [(1, 14, 16)], "rows_b")
+        quantize(late[:, : P * PACK], "z", [(1, 11, 12)])
+        quantize(spot(10, 2), "t10", [(0, 14, 16), (2, 14, 16)], "tokens0")
         halves_together(last_acc, 1, 11, 12, False, True)
         for h in range(HALVES):
             nc.scalar.copy(out=dx[h][:, OWN + P :], in_=last_acc[:, h * P : (h + 1) * P])
@@ -270,7 +257,7 @@ def tile_moe_bds_lin_none_kernel(tc, dyT, w_words, w_scales, gate, offs, pos1, p
         def fetched(r, h, t0, t1):
             return dx[h][:].indirect(token_slot[r][:, t0 // 16 : t1 // 16])
 
-        got = keep.tile([P, 2, HALVES, T], F32, name="got", tag="own%d" % BANK, align_bytes=64)
+        got = keep.tile([P, 2, HALVES, T], F32, name="got", tag="own%d" % FIRST, align_bytes=64)
         sums = keep.tile([P, 3, HALVES, T], F32, name="sums", tag="rows_a", align_bytes=64)
         out_rows = out.rearrange("(h p) t -> p h t", p=P)
         for r, h, t0, t1 in ((0, 0, HALF, T), (0, 1, HALF, T), (0, 0, 0, HALF), (0, 1, 0, HALF), (1, 1, 0, HALF), (1, 0, 0, HALF), (1, 0, HALF, T)):

from contextlib import ExitStack

import concourse.mybir as mybir
from concourse.masks import make_identity

K, T, E, C, N = 256, 512, 6, 256, 1536
S = E * C
P = 128
PACK = 4
PASSES = N // (P * PACK)
FLOPS = 2 * K * N * (S + T)
BYTES = N * T * 4 + (E + 1) * PASSES * (P * 512 + 16 * K) + P * S * 4 + P * (S + 3 * T) // 16 * 2 + K * T * 4

F32 = mybir.dt.float32
BF16 = mybir.dt.bfloat16
I32 = mybir.dt.int32
U32 = mybir.dt.uint32
U16 = mybir.dt.uint16
U8 = mybir.dt.uint8
FP8X4 = mybir.dt.float8_e4m3fn_x4
FP4X4 = mybir.dt.float4_e2m1fn_x4
MULT = mybir.AluOpType.mult
ADD = mybir.AluOpType.add
COPY = mybir.ActivationFunctionType.Copy

LAST = PASSES - 1
HALVES = K // P
HALF = T // 2
RUN = 2
BANK = 512
OWN = 5 * C
SPARE = 16
FIRST = 448
ROW_STEP = 608
LAST_WIDTH = (PACK - 1) * ROW_STEP + 1120


def tile_moe_bds_lin_none_kernel(tc, dyT, w_words, w_scales, gate, offs, pos1, pos2, pos3, out):
    nc = tc.nc
    with ExitStack() as ctx:
        lists = ctx.enter_context(tc.tile_pool(name="lists", bufs=1))
        keep = ctx.enter_context(tc.tile_pool(name="keep", bufs=1))
        psum = ctx.enter_context(tc.psum_pool(name="psum", bufs=1))

        slot_token = lists.tile([P, S // 16], U16, name="slot_token")
        token_slot = [lists.tile([P, T // 16], U16, name="token_slot%d" % r) for r in range(3)]

        dy_rows = dyT.rearrange("(a p j) t -> a p j t", p=P, j=PACK)
        w_codes = keep.tile([P, (E + 1) * PASSES, 2 * K], U8, name="w_codes", align_bytes=64)
        w_exp = keep.tile([P, (E + 1) * PASSES, K], U8, name="w_exp", align_bytes=64)
        nc.vector.memset(w_exp[:].rearrange("p g k -> p (g k)").bitcast(I32), 0)

        warm = keep.tile([P, 2], F32, name="warm")
        nc.vector.memset(warm[:, 0:1], 0.0)
        nc.scalar.activation(warm[:, 1:2], warm[:, 0:1], COPY)
        ident = keep.tile([P, P], F32, name="ident")
        make_identity(nc, ident[:])

        last_rows = keep.tile([P, LAST_WIDTH], F32, name="last_rows")
        window = {}
        for a, most in ((0, 2 * BANK), (1, BANK)):
            for j in range(PACK):
                window[a, j] = keep.tile([P, most + SPARE], F32, name="window%d_%d" % (a, j))
        tokens = [keep.tile([P, PACK, T], F32, name="tokens%d" % a, tag="tokens%d" % a, align_bytes=64) for a in range(LAST)]
        gates = [keep.tile([P, FIRST], F32, name="gates0"), keep.tile([P, OWN + P - FIRST], F32, name="gates1")]
        gate_cols = keep.tile([P, S // BANK, PACK], F32, name="gate_cols")

        nc.sync.dma_start(slot_token[:], offs)
        for j in range(PACK):
            nc.sync.dma_start(out=last_rows[:, j * ROW_STEP : j * ROW_STEP + T], in_=dy_rows[LAST, :, j, :])
        for j in range(PACK):
            nc.sync.dma_start(out=window[0, j][:, 0:T], in_=dy_rows[0, :, j, :])
            if j == 0:
                nc.sync.dma_start(out=gates[0][:], in_=gate[0:P, 0:FIRST])
        nc.sync.dma_start(out=tokens[0][:], in_=dy_rows[0])
        nc.sync.dma_start(out=gate_cols[:], in_=gate[0, :].rearrange("(b p i) -> p b i", p=P, i=PACK))
        for j in range(PACK):
            nc.sync.dma_start(out=window[1, j][:, 0:T], in_=dy_rows[1, :, j, :])
        nc.sync.dma_start(out=gates[1][:], in_=gate[0:P, FIRST : OWN + P])
        nc.sync.dma_start(out=tokens[1][:], in_=dy_rows[1])
        s_src = w_scales.rearrange("e a f k -> f (e a) k")
        for q in range(4):
            nc.sync.dma_start(out=w_exp[32 * q : 32 * q + 4, :, :].bitcast(I32), in_=s_src[4 * q : 4 * q + 4].bitcast(I32))
        nc.sync.dma_start(out=w_codes[:].bitcast(I32), in_=w_words.rearrange("e a p b -> p (e a) b").bitcast(I32))
        for r, src in enumerate((pos1, pos2, pos3)):
            nc.sync.dma_start(token_slot[r][:], src)

        gate_bank = {}
        for b in range(S // BANK):
            gate_bank[b] = psum.tile([P, BANK], F32, name="gate_bank%d" % b, tag="gate_bank%d" % b)
            for i in range(PACK):
                nc.tensor.transpose(gate_bank[b][:, i::PACK], gate_cols[:, b, i : i + 1].to_broadcast([P, P]), ident[:])

        def picked(a, j, c0, c1, width):
            source = last_rows[:, j * ROW_STEP : j * ROW_STEP + width] if a == LAST else window[a, j][:]
            return source.indirect(slot_token[:, c0 // 16 : c1 // 16])

        def rows_tile(a, c0, c1, tag):
            return keep.tile([P, PACK, c1 - c0], F32, name="rows%d_%d" % (a, c0), tag=tag, align_bytes=64)

        def scalar_gather(a, c0, c1, tag):
            rows = rows_tile(a, c0, c1, tag)
            for j in range(PACK):
                nc.scalar.activation(rows[:, j, :], picked(a, j, c0, c1, T), COPY)
            return rows

        def vector_gather(a, c0, c1):
            rows = rows_tile(a, c0, c1, "own%d" % c0)
            for j in range(PACK):
                nc.vector.tensor_copy(rows[:, j, :], picked(a, j, c0, c1, ROW_STEP if c0 == 0 else LAST_WIDTH - j * ROW_STEP))
            return rows

        def rounded_tile(n, name, tag):
            return keep.tile([P, n * PACK], BF16, name=name, tag=tag, align_bytes=64)

        def vector_product(rows, c0, target):
            n = rows.shape[2]
            weights = gate_bank[c0 // BANK][:, c0 % BANK : c0 % BANK + n]
            spread = weights.rearrange("p (c i) -> p c i", i=RUN).unsqueeze(2).to_broadcast([P, n // RUN, PACK, RUN])
            woven = target.rearrange("p (c i j) -> p c j i", i=RUN, j=PACK)
            nc.vector.tensor_tensor(woven, rows.rearrange("p j (c i) -> p c j i", i=RUN), spread, MULT)

        def gpsimd_product(rows, weights, target):
            spread = weights.unsqueeze(2).to_broadcast([P, rows.shape[2], PACK])
            nc.gpsimd.tensor_tensor(target.rearrange("p (c j) -> p c j", j=PACK), rows.rearrange("p j c -> p c j"), spread, MULT)

        rounded = rounded_tile(12 * C, "rounded", "rounded")

        def spot(first, count):
            return rounded[:, first * C * PACK : (first + count) * C * PACK]

        def round_tokens(rows, first, second):
            target = rounded[:].rearrange("p (s t j) -> p s t j", t=HALF, j=PACK)[:, first : second + 1 : second - first]
            nc.gpsimd.tensor_scalar(target, rows.rearrange("p j (q t) -> p q t j", q=2), 1.0, 0.0, MULT, ADD)

        coded = {}

        def quantize(source, name, parts, tag=None):
            n = source.shape[1] // PACK
            codes = keep.tile([P, n], U32, name="codes_" + name, tag=tag or "codes_" + name, align_bytes=64)
            exps = keep.tile([P, n], U8, name="exps_" + name, align_bytes=64)
            nc.vector.quantize_mx(out=codes[:].bitcast(FP8X4), scales=exps[:], in_=source)
            place = 0
            for a, b0, b1 in parts:
                for b in range(b0, b1):
                    coded[a, b] = (codes, exps, place)
                    place = place + P

        def product(acc, h, a, b0, b1, start, stop):
            g = min(b0 // 2, E) * PASSES + a
            codes, exps, place = coded[a, b0]
            cols = slice(place, place + (b1 - b0) * P)
            nc.tensor.matmul_mx(
                out=acc,
                lhsT=w_codes[:, g, 2 * P * h : 2 * P * (h + 1)].bitcast(FP4X4),
                lhsT_scale=w_exp[:, g, P * h : P * (h + 1)],
                rhs=codes[:, cols].bitcast(FP8X4),
                rhs_scale=exps[:, cols],
                start=start,
                stop=stop,
            )

        def halves_apart(acc, base, a, b0, b1, start, stop):
            cuts = [(b, min(b + 2, b1)) for b in range(b0, b1, 2)]
            for h in range(HALVES):
                for c0, c1 in cuts:
                    product(acc[h][:, (c0 - base) * P : (c1 - base) * P], h, a, c0, c1, start and c0 == b0, stop and c1 == b1)

        def halves_together(acc, a, b0, b1, start, stop):
            n = (b1 - b0) * P
            for h in range(HALVES):
                product(acc[:, h * n : (h + 1) * n], h, a, b0, b1, start and h == 0, stop and h == HALVES - 1)

        rows_f = scalar_gather(LAST, OWN, S, "rows_f")
        rows_a = scalar_gather(0, 0, 2 * BANK, "rows_a")
        rows_b = scalar_gather(1, 0, BANK, "rows_b")
        own = [vector_gather(LAST, 0, FIRST), vector_gather(LAST, FIRST, OWN), vector_gather(1, OWN, OWN + P)]

        def own_product(c0, c1, target):
            gpsimd_product(own[1][:, :, c0 - FIRST : c1 - FIRST], gates[1][:, c0 - FIRST : c1 - FIRST], target)

        late = rounded_tile(P + BANK, "late", "late")
        round_tokens(last_rows[:, : PACK * ROW_STEP].rearrange("p (j w) -> p j w", j=PACK)[:, :, 0:T], 1, 11)
        gpsimd_product(own[0][:], gates[0][:], spot(5, 3)[:, : FIRST * PACK])
        round_tokens(tokens[0][:], 0, 10)
        rows_c = scalar_gather(1, BANK, 2 * BANK, "tokens0")
        own_product(FIRST, 3 * C, spot(5, 3)[:, FIRST * PACK :])
        gpsimd_product(own[2][:], gates[1][:, OWN - FIRST :], late[:, : P * PACK])
        round_tokens(tokens[1][:], 8, 9)

        bf_a = rounded_tile(2 * BANK, "bf_a", "bf_a")
        for i in range(2):
            vector_product(rows_a[:, :, i * BANK : (i + 1) * BANK], i * BANK, bf_a[:, i * BANK * PACK : (i + 1) * BANK * PACK])
        vector_product(rows_b[:], 0, spot(3, 2))
        rows_d = scalar_gather(0, 2 * BANK, S, "rows_a")
        rows_e = scalar_gather(1, 4 * C, 5 * C, "rows_b")
        quantize(spot(7, 2), "g", [(2, 4, 6), (1, 12, 14)])
        quantize(bf_a[:], "a", [(0, 0, 8)])
        quantize(spot(3, 4), "b", [(1, 0, 4), (2, 0, 4)])
        first_acc = [psum.tile([P, BANK], F32, name="first_acc%d" % h, tag="first_acc%d" % h) for h in range(HALVES)]
        second_acc = [psum.tile([P, BANK], F32, name="second_acc%d" % h) for h in range(HALVES)]
        for a in range(PASSES):
            halves_apart(first_acc, 0, a, 0, 4, a == 0, a == LAST)
        halves_apart(second_acc, 4, 0, 4, 8, True, False)
        halves_apart(second_acc, 4, 2, 4, 6, False, False)

        own_product(3 * C, 4 * C, spot(3, 1))
        vector_product(rows_f[:], OWN, spot(2, 1))
        vector_product(rows_c[:], BANK, late[:, P * PACK :])
        rows_z = scalar_gather(1, OWN + P, S, "tokens0")
        quantize(spot(0, 4), "h", [(0, 12, 14), (2, 12, 14), (2, 10, 12), (2, 6, 8)])
        quantize(late[:, P * PACK :], "c", [(1, 4, 8)])
        halves_apart(second_acc, 4, 2, 6, 8, False, False)
        halves_apart(second_acc, 4, 1, 4, 8, False, True)
        ds = [psum.tile([P, BANK], F32, name="ds0", tag="gate_bank1")]
        for a in range(PASSES):
            halves_together(ds[0], a, 12, 14, a == 0, a == LAST)
        last_acc = psum.tile([P, HALVES * P], F32, name="last_acc", tag="gate_bank0")
        halves_together(last_acc, 2, 11, 12, True, False)

        own_product(4 * C, OWN, late[:, P * PACK : (P + C) * PACK])
        vector_product(rows_d[:], 2 * BANK, spot(0, 2))
        vector_product(rows_e[:], 4 * C, spot(2, 1))

        dx = [keep.tile([P, S], F32, name="dx%d" % h, tag=tag, align_bytes=64) for h, tag in enumerate(("own0", "tokens1"))]
        for h in (1, 0):
            nc.scalar.copy(out=dx[h][:, :BANK], in_=first_acc[h][:])
        for h in range(HALVES):
            nc.scalar.copy(out=dx[h][:, BANK : 2 * BANK], in_=second_acc[h][:])
        opening = keep.tile([P, HALVES, HALF], F32, name="opening", align_bytes=64)
        nc.scalar.copy(out=opening[:].rearrange("p h t -> p (h t)"), in_=ds[0][:])
        third_acc = [psum.tile([P, C + P], F32, name="third_acc0"), psum.tile([P, C + P], F32, name="third_acc1", tag="first_acc1")]
        halves_apart(third_acc, 8, 2, 10, 11, True, False)

        quantize(late[:, : (P + C) * PACK], "late", [(1, 10, 11), (2, 8, 10)])
        quantize(spot(0, 2), "d", [(0, 8, 12)])
        quantize(spot(2, 1), "e", [(1, 8, 10)])
        halves_apart(third_acc, 8, 2, 8, 10, False, False)
        halves_apart(third_acc, 8, 1, 10, 11, False, False)
        halves_apart(third_acc, 8, 0, 8, 11, False, False)
        halves_apart(third_acc, 8, 1, 8, 10, False, True)
        halves_together(last_acc, 0, 11, 12, False, False)
        for h in range(HALVES):
            nc.scalar.copy(out=dx[h][:, 2 * BANK : OWN + P], in_=third_acc[h][:])

        vector_product(rows_z[:], OWN + P, late[:, : P * PACK])
        quantize(spot(9, 1), "t11", [(1, 14, 16)], "rows_b")
        quantize(late[:, : P * PACK], "z", [(1, 11, 12)])
        quantize(spot(10, 2), "t10", [(0, 14, 16), (2, 14, 16)], "tokens0")
        halves_together(last_acc, 1, 11, 12, False, True)
        for h in range(HALVES):
            nc.scalar.copy(out=dx[h][:, OWN + P :], in_=last_acc[:, h * P : (h + 1) * P])
        ds.append(psum.tile([P, BANK], F32, name="ds1", tag="first_acc0"))
        for a in (1, 0, 2):
            halves_together(ds[1], a, 14, 16, a == 1, a == 2)

        def fetched(r, h, t0, t1):
            return dx[h][:].indirect(token_slot[r][:, t0 // 16 : t1 // 16])

        got = keep.tile([P, 2, HALVES, T], F32, name="got", tag="own%d" % FIRST, align_bytes=64)
        sums = keep.tile([P, 3, HALVES, T], F32, name="sums", tag="rows_a", align_bytes=64)
        out_rows = out.rearrange("(h p) t -> p h t", p=P)
        for r, h, t0, t1 in ((0, 0, HALF, T), (0, 1, HALF, T), (0, 0, 0, HALF), (0, 1, 0, HALF), (1, 1, 0, HALF), (1, 0, 0, HALF), (1, 0, HALF, T)):
            nc.scalar.activation(got[:, r, h, t0:t1], fetched(r, h, t0, t1), COPY)
        for h in range(HALVES):
            nc.vector.tensor_tensor(sums[:, 0, h, :HALF], fetched(2, h, 0, HALF), opening[:, h, :], ADD)
        for h in range(HALVES):
            nc.vector.tensor_tensor(sums[:, 0, h, HALF:], fetched(2, h, HALF, T), got[:, 0, h, HALF:], ADD)
        nc.vector.tensor_tensor(sums[:, 1, :, :HALF], sums[:, 0, :, :HALF], got[:, 0, :, :HALF], ADD)
        nc.vector.tensor_tensor(sums[:, 1, :, HALF:], ds[1][:].rearrange("p (h t) -> p h t", h=HALVES), sums[:, 0, :, HALF:], ADD)
        for h, t0, t1 in ((1, 0, HALF), (0, 0, HALF), (1, HALF, T), (0, HALF, T)):
            other = fetched(1, h, t0, t1) if (h, t0) == (1, HALF) else got[:, 1, h, t0:t1]
            nc.vector.tensor_tensor(sums[:, 2, h, t0:t1], other, sums[:, 1, h, t0:t1], ADD)
            nc.sync.dma_start(out=out_rows[:, h, t0:t1], in_=sums[:, 2, h, t0:t1])
